import numpy as np
import ml_dtypes


def mxq(x, axis, fmt="e4m3"):
    dtype, down = {"e4m3": (ml_dtypes.float8_e4m3fn, 7), "e5m2": (ml_dtypes.float8_e5m2, 14)}[fmt]
    v = np.moveaxis(np.asarray(x, np.float32).astype(ml_dtypes.bfloat16).astype(np.float64), axis, -1)
    blocks = v.reshape(v.shape[:-1] + (-1, 32))
    amax = np.abs(blocks).max(-1, keepdims=True)
    byte = np.maximum(np.where(amax > 0, np.frexp(amax)[1] - 1 + 127, 0) - down, 1)
    scale = np.exp2(byte - 127.0)
    codes = (blocks / scale).astype(np.float32).astype(dtype).astype(np.float64)
    return np.moveaxis((codes * scale).reshape(v.shape), -1, axis)


WIDE = False


def mx_kscale(k):
    if not WIDE:
        return np.ones(k)
    levels = np.array([10, -10, 5, -5, 0])
    if k % 512:
        return np.exp2(np.random.permutation(np.resize(levels, k // 32))).repeat(32)
    a = np.empty((k // 512, 16))
    for p in range(k // 512):
        a[p, :8] = np.random.permutation(np.resize(levels, 8))
        for g in range(8):
            far = levels[np.abs(levels - a[p, g]) >= 10]
            a[p, g + 8] = far[np.random.randint(len(far))]
    return np.exp2(a.ravel()).repeat(32)


def f64(x):
    return np.asarray(x).astype(np.float64)


def striped(idx):
    return np.tile(idx.reshape(-1, 16).T, (8, 1)).astype(np.uint16)


def unstriped(offs):
    return offs[:16].T.reshape(-1).astype(np.int64)


E2M1 = np.array([0.0, 0.5, 1.0, 1.5, 2.0, 3.0, 4.0, 6.0, -0.0, -0.5, -1.0, -1.5, -2.0, -3.0, -4.0, -6.0])


def pack_weight(w, fmt):
    k, n = w.shape
    w = f64(np.asarray(w, np.float32).astype(ml_dtypes.bfloat16)).reshape(k // 32, 32, n)
    amax = np.abs(w).max(1)
    if fmt == "e4m3":
        byte = np.frexp(amax)[1] - 1 + 127 - 7
    else:
        mant, ex = np.frexp(amax / 6.0)
        byte = np.where(mant > 0.5, ex, ex - 1) + 127
    byte = np.clip(np.where(amax > 0, byte, 1), 1, 254)
    scaled = (w * np.exp2(127.0 - byte)[:, None, :]).reshape(k, n).astype(np.float32)
    by_word = np.ascontiguousarray(scaled.reshape(k // 512, 128, 4, n).transpose(0, 1, 3, 2))
    if fmt == "e4m3":
        words = by_word.astype(ml_dtypes.float8_e4m3fn).view(np.uint8)
    else:
        c = by_word.astype(ml_dtypes.float4_e2m1fn).view(np.uint8) & 0xF
        words = (c[..., 0::2] | (c[..., 1::2] << 4)).reshape(k // 512, 128, 2 * n)
    return np.ascontiguousarray(words), np.ascontiguousarray(byte.astype(np.uint8).reshape(k // 512, 16, n))


def unpack_weight(words, scales, fmt):
    g, _, n = scales.shape
    words = np.ascontiguousarray(words).reshape(g, 128, n, -1)
    if fmt == "e4m3":
        vals = words.view(ml_dtypes.float8_e4m3fn).astype(np.float64)
    else:
        nib = np.empty((g, 128, n, 4), np.uint8)
        nib[..., 0::2] = words & 0xF
        nib[..., 1::2] = words >> 4
        vals = E2M1[nib]
    vals = vals * np.repeat(np.exp2(scales.astype(np.float64) - 127.0), 8, axis=1)[..., None]
    return vals.transpose(0, 1, 3, 2).reshape(g * 512, n)


def gelu(v):
    return 0.5 * v * (1.0 + np.tanh(np.sqrt(2.0 / np.pi) * (v + 0.044715 * v**3)))


def bf(x):
    return np.asarray(x, np.float32).astype(ml_dtypes.bfloat16)

def planes(Y):
    n, m = Y.shape
    b = f64(bf(Y)).reshape(n // 32, 32, m)
    amax = np.abs(b).max(1)
    byte = np.clip(np.where(amax > 0, np.frexp(amax)[1] - 1 + 127 - 7, 1), 1, 254)
    codes = (b * np.exp2(127.0 - byte)[:, None, :]).reshape(n, m).astype(np.float32).astype(ml_dtypes.float8_e4m3fn).view(np.uint8)
    words = codes.reshape(n // 512, 128, 4, m).transpose(0, 1, 3, 2)
    return np.ascontiguousarray(words), np.ascontiguousarray(byte.astype(np.uint8).reshape(n // 512, 16, m))


K, T, S, M, N = 1024, 2048, 1024, 1024, 512

def setup_inputs():
    n = np.random.standard_normal
    s = mx_kscale(K)[:, None]
    u = mx_kscale(S)
    idx = np.random.permutation(T)[:S]
    r = np.exp(0.8 * n(N))
    tab_words, tab_scales = pack_weight(0.75 * n((K, T)) * s / np.sqrt(K), "e4m3")
    x = n((K, M)) / s
    wdT = 0.6 * n((N, T)) * r[:, None] / np.sqrt(S)
    wdT[:, idx] /= u
    w4_words, w4_scales = pack_weight(0.8 * n((K, N)) * s * r / np.sqrt(K), "e2m1")
    return {
        "x": x.astype(np.float32),
        "tab_words": tab_words, "tab_scales": tab_scales,
        "offs": striped(idx),
        "b": (0.3 * n(S)).astype(np.float32),
        "g": (np.exp(0.3 * n(S)) * u).astype(np.float32),
        "wdT": wdT.astype(np.float32),
        "w4_words": w4_words, "w4_scales": w4_scales,
        "c": (0.4 * n(N) * r).astype(np.float32),
    }

def reference(x, tab_words, tab_scales, offs, b, g, wdT, w4_words, w4_scales, c):
    v = unpack_weight(tab_words, tab_scales, "e4m3")[:, unstriped(offs)]
    wd = f64(wdT)[:, unstriped(offs)]
    w4 = unpack_weight(w4_words, w4_scales, "e2m1")
    xq = mxq(f64(x), 0, "e4m3")
    a = (v.T @ xq) + f64(b)[:, None]
    h = a * a * a * f64(g)[:, None]
    y = (mxq(wd, 1, "e4m3") @ mxq(h, 0, "e4m3") + w4.T @ xq) + f64(c)[:, None]
    words, scales = planes(y)
    return y, words, scales

@@ -1,0 +1,280 @@
+from contextlib import ExitStack
+
+import concourse.mybir as mybir
+from concourse.masks import make_identity
+
+K, T, S, M, N = 1024, 2048, 1024, 1024, 512
+FLOPS = 2 * M * (K * S + S * N + K * N)
+
+F32 = mybir.dt.float32
+BF16 = mybir.dt.bfloat16
+I32 = mybir.dt.int32
+U32 = mybir.dt.uint32
+U16 = mybir.dt.uint16
+U8 = mybir.dt.uint8
+FP8X4 = mybir.dt.float8_e4m3fn_x4
+FP4X4 = mybir.dt.float4_e2m1fn_x4
+ACT = mybir.ActivationFunctionType
+ALU = mybir.AluOpType
+
+P = 128
+PACK = 4
+PASS = P * PACK
+CHUNKS = ((0, 256), (256, 512), (768, 256))
+GAP = 32
+
+
+def woven(tile_ap):
+    return tile_ap.rearrange("p (c i) t -> p c t i", i=4)
+
+
+def planes(tile_ap):
+    return tile_ap.rearrange("p t (c i) -> p c t i", i=4)
+
+
+def tile_list_cube_parser_layer_kernel(tc, x, tab_words, tab_scales, offs, b, g, wdT, w4_words, w4_scales, c, out_0, out_1, out_2):
+    nc = tc.nc
+    with ExitStack() as ctx:
+        keep = ctx.enter_context(tc.tile_pool(name="keep", bufs=1))
+        ring = ctx.enter_context(tc.tile_pool(name="ring", bufs=2))
+        pre_pool = ctx.enter_context(tc.psum_pool(name="pre", bufs=3))
+        acc_pool = ctx.enter_context(tc.psum_pool(name="acc", bufs=4))
+        turn_pool = ctx.enter_context(tc.psum_pool(name="turn", bufs=1))
+
+        def held(name, shape, dtype):
+            return keep.tile(shape, dtype, name=name, align_bytes=64)
+
+        offsets = keep.tile([P, S // 16], U16, name="offsets")
+        nc.sync.dma_start(offsets[:], offs)
+
+        tab_s = held("tab_s", [P, T], U8)
+        nc.vector.memset(tab_s[:].bitcast(I32), 0)
+        for q in range(4):
+            nc.scalar.dma_start(
+                out=tab_s[32 * q : 32 * q + 8, :].bitcast(I32),
+                in_=tab_scales[:, 4 * q : 4 * q + 4, :].bitcast(I32),
+            )
+        w4_s = held("w4_s", [P, 2, N], U8)
+        nc.gpsimd.memset(w4_s[:].rearrange("p a n -> p (a n)").bitcast(I32), 0)
+        ident = held("ident", [P, P], F32)
+        make_identity(nc, ident[:])
+
+        b_sb = held("b_sb", [P, 2, PACK], F32)
+        g_sb = held("g_sb", [P, 2, PACK], F32)
+        c_sb = held("c_sb", [P, PACK], F32)
+
+        x_raw = {}
+
+        def load_x(ci):
+            m0, w = CHUNKS[ci]
+            for a in range(2):
+                raw = held("x_raw%d%d" % (ci, a), [P, PACK, w], F32)
+                nc.sync.dma_start(out=raw[:], in_=x[PASS * a : PASS * (a + 1), m0 : m0 + w].rearrange("(p i) m -> p i m", i=PACK))
+                x_raw[ci, a] = raw
+
+        wd_raw = {}
+
+        def load_wd(t):
+            raw = held("wd_raw%d" % t, [P, T], F32)
+            nc.sync.dma_start(out=raw[:], in_=wdT.rearrange("(p t) e -> p t e", t=PACK)[:, t, :])
+            wd_raw[t] = raw
+
+        load_x(0)
+        tab_w = []
+        for a in range(2):
+            words = held("tab_w%d" % a, [P, T], U32)
+            nc.sync.dma_start(out=words[:].bitcast(I32), in_=tab_words[a].rearrange("p e i -> p (e i)").bitcast(I32))
+            tab_w.append(words)
+            if a == 0:
+                nc.sync.dma_start(out=b_sb[:], in_=b.rearrange("(g p t) -> p g t", g=2, t=PACK))
+                nc.sync.dma_start(out=g_sb[:], in_=g.rearrange("(g p t) -> p g t", g=2, t=PACK))
+        load_x(1)
+        load_wd(0)
+        w4_w = held("w4_w", [P, 2, 2 * N], U8)
+        nc.sync.dma_start(out=w4_w[:].bitcast(I32), in_=w4_words.rearrange("a p e -> p a e").bitcast(I32))
+        for q in range(4):
+            nc.sync.dma_start(
+                out=w4_s[32 * q : 32 * q + 4, :, :].bitcast(I32),
+                in_=w4_scales[:, 4 * q : 4 * q + 4, :].rearrange("a r n -> r a n").bitcast(I32),
+            )
+        nc.sync.dma_start(out=c_sb[:], in_=c.rearrange("(p t) -> p t", t=PACK))
+        load_wd(1)
+        load_x(2)
+        load_wd(2)
+        load_wd(3)
+
+        gb_sb = held("gb_sb", [P, 2, PACK], F32)
+        nc.gpsimd.tensor_mul(out=gb_sb[:], in0=g_sb[:], in1=b_sb[:])
+
+        v_s_listed = held("v_s_listed", [P, S], U8)
+        nc.vector.tensor_copy(out=v_s_listed[:], in_=tab_s[:].indirect(offsets[:]))
+        v_s = held("v_s", [P, S], U8)
+        nc.vector.tensor_copy(
+            out=v_s[:].rearrange("p (g t q) -> p g t q", g=2, t=PACK),
+            in_=v_s_listed[:].rearrange("p (g q t) -> p g t q", g=2, t=PACK),
+        )
+
+        x_w, x_s, x_bf = {}, {}, {}
+
+        def cast_x(ci, a, on_vector):
+            w = CHUNKS[ci][1]
+            bf = held("x_bf%d%d" % (ci, a), [P, w, PACK], BF16)
+            if on_vector:
+                nc.vector.tensor_copy(out=woven(bf[:]), in_=planes(x_raw[ci, a][:]))
+            else:
+                nc.scalar.activation(out=woven(bf[:]), in_=planes(x_raw[ci, a][:]), func=ACT.Copy)
+            x_bf[ci, a] = bf
+
+        def quantize(name, bf, width):
+            words = held(name + "_w", [P, width], U32)
+            scales = held(name + "_s", [P, width], U8)
+            nc.vector.quantize_mx(out=words[:].bitcast(FP8X4), scales=scales[:], in_=bf)
+            return words, scales
+
+        def quantize_x(ci, a):
+            w = CHUNKS[ci][1]
+            x_w[ci, a], x_s[ci, a] = quantize("x%d%d" % (ci, a), x_bf[ci, a][:].rearrange("p m t -> p (m t)"), w)
+
+        v_w = {}
+
+        def gather_table(a, jg):
+            words = held("v_w%d%d" % (a, jg), [P, PASS], U32)
+            nc.vector.tensor_copy(
+                out=words[:].rearrange("p (t q) -> p q t", t=PACK),
+                in_=tab_w[a][:].indirect(offsets[:, 32 * jg : 32 * (jg + 1)]),
+            )
+            v_w[a, jg] = words
+
+        h_w, h_s = {}, {}
+
+        def hidden(ci, jg):
+            w = CHUNKS[ci][1]
+            sq = ring.tile([P, PACK, 512], F32, name="sq", align_bytes=64)
+            lin = ring.tile([P, PACK, 512], F32, name="lin", align_bytes=64)
+            for t in range(PACK):
+                pre = pre_pool.tile([P, 512], F32, name="pre")
+                cols = slice(P * t, P * (t + 1))
+                scale_cols = slice(PASS * jg + P * t, PASS * jg + P * (t + 1))
+                for a in range(2):
+                    nc.tensor.matmul_mx(
+                        out=pre[:, :w],
+                        lhsT=v_w[a, jg][:, cols].bitcast(FP8X4),
+                        lhsT_scale=v_s[4 * a : P, scale_cols],
+                        rhs=x_w[ci, a][:].bitcast(FP8X4),
+                        rhs_scale=x_s[ci, a][:],
+                        start=(a == 0),
+                        stop=(a == 1),
+                    )
+                nc.scalar.activation(out=sq[:, t, :w], in_=pre[:, :w], func=ACT.Square, bias=b_sb[:, jg, t : t + 1])
+                nc.scalar.activation(
+                    out=lin[:, t, :w], in_=pre[:, :w], func=ACT.Identity,
+                    bias=gb_sb[:, jg, t : t + 1], scale=g_sb[:, jg, t : t + 1],
+                )
+            bf = ring.tile([P, 512, PACK], BF16, name="h_bf", align_bytes=64)
+            nc.vector.tensor_tensor(out=woven(bf[:, :w, :]), in0=planes(sq[:, :, :w]), in1=planes(lin[:, :, :w]), op=ALU.mult)
+            h_w[ci, jg], h_s[ci, jg] = quantize("h%d%d" % (ci, jg), bf[:, :w, :].rearrange("p m t -> p (m t)"), w)
+
+        wd_w, wd_s = {}, {}
+
+        def down_weights(t):
+            picked = ring.tile([P, 2, PASS + GAP], BF16, name="wd_picked", align_bytes=64)
+            nc.vector.tensor_copy(out=picked[:, :, :PASS], in_=wd_raw[t][:].indirect(offsets[:]))
+            pairs = picked[:].bitcast(F32)
+            turned = turn_pool.tile([P, 2, 2, P], F32, name="turned")
+            for jg in range(2):
+                for u in range(2):
+                    nc.tensor.transpose(turned[:, jg, u, :], pairs[:, jg, u : 2 * P : 2], ident[:])
+            bf = ring.tile([P, 2, P, PACK], BF16, name="wd_bf", align_bytes=64)
+            nc.scalar.copy(out=bf[:].bitcast(F32), in_=turned[:].rearrange("p g u n -> p g n u"))
+            wd_w[t], wd_s[t] = quantize("wd%d" % t, bf[:].rearrange("p g n t -> p (g n t)"), 2 * P)
+
+        w4_w_dealt = held("w4_w_dealt", [P, 2, 2 * N], U8)
+        w4_s_dealt = held("w4_s_dealt", [P, 2, N], U8)
+
+        def deal_w4():
+            nc.vector.tensor_copy(
+                out=w4_w_dealt[:].bitcast(U16).rearrange("p a (t q) -> p a t q", t=PACK),
+                in_=w4_w[:].bitcast(U16).rearrange("p a (q t) -> p a t q", t=PACK),
+            )
+            nc.vector.tensor_copy(
+                out=w4_s_dealt[:].rearrange("p a (t q) -> p a t q", t=PACK),
+                in_=w4_s[:].rearrange("p a (q t) -> p a t q", t=PACK),
+            )
+
+        y_s = held("y_s", [P, M], U8)
+        y_rows = out_0.rearrange("(p t) m -> p t m", t=PACK)
+        y_words = out_1[0].rearrange("p m t -> p (m t)")
+
+        def output(ci):
+            m0, w = CHUNKS[ci]
+            last = ci == len(CHUNKS) - 1
+            y = held("y%d" % ci, [P, PACK, w], F32)
+            step = 512 if w == 512 else 128
+            for t in range(PACK):
+                acc = acc_pool.tile([P, 512], F32, name="acc")
+                for a in range(2):
+                    for n0 in range(0, w, step):
+                        nc.tensor.matmul_mx(
+                            out=acc[:, n0 : n0 + step],
+                            lhsT=w4_w_dealt[:, a, 2 * P * t : 2 * P * (t + 1)].bitcast(FP4X4),
+                            lhsT_scale=w4_s_dealt[:, a, P * t : P * (t + 1)],
+                            rhs=x_w[ci, a][:, n0 : n0 + step].bitcast(FP8X4),
+                            rhs_scale=x_s[ci, a][:, n0 : n0 + step],
+                            start=(a == 0 and n0 == 0),
+                            stop=False,
+                        )
+                for jg in range(2):
+                    nc.tensor.matmul_mx(
+                        out=acc[:, :w],
+                        lhsT=wd_w[t][:, P * jg : P * (jg + 1)].bitcast(FP8X4),
+                        lhsT_scale=wd_s[t][:, P * jg : P * (jg + 1)],
+                        rhs=h_w[ci, jg][:].bitcast(FP8X4),
+                        rhs_scale=h_s[ci, jg][:],
+                        start=False,
+                        stop=(jg == 1),
+                    )
+                if last and t % 2 == 1:
+                    nc.vector.tensor_scalar_add(out=y[:, t, :], in0=acc[:, :w], scalar1=c_sb[:, t : t + 1])
+                else:
+                    nc.scalar.activation(out=y[:, t, :], in_=acc[:, :w], func=ACT.Identity, bias=c_sb[:, t : t + 1])
+            nc.sync.dma_start(out=y_rows[:, :, m0 : m0 + w], in_=y[:])
+            bf = held("y_bf%d" % ci, [P, w, PACK], BF16)
+            nc.vector.tensor_copy(out=woven(bf[:]), in_=planes(y[:]))
+            words = held("y_w%d" % ci, [P, w], U32)
+            nc.vector.quantize_mx(out=words[:].bitcast(FP8X4), scales=y_s[:, m0 : m0 + w], in_=bf[:].rearrange("p m t -> p (m t)"))
+            nc.sync.dma_start(out=y_words[:, 4 * m0 : 4 * (m0 + w)].bitcast(I32), in_=words[:].bitcast(I32))
+
+        for a in range(2):
+            cast_x(0, a, False)
+        for a in range(2):
+            quantize_x(0, a)
+        gather_table(0, 0)
+        gather_table(1, 0)
+        gather_table(0, 1)
+        gather_table(1, 1)
+        hidden(0, 0)
+        for a in range(2):
+            cast_x(1, a, False)
+            quantize_x(1, a)
+        hidden(0, 1)
+        down_weights(0)
+        hidden(1, 0)
+        deal_w4()
+        down_weights(1)
+        for a in range(2):
+            cast_x(2, a, True)
+        for a in range(2):
+            quantize_x(2, a)
+        down_weights(2)
+        hidden(1, 1)
+        down_weights(3)
+        hidden(2, 0)
+        output(0)
+        hidden(2, 1)
+        output(1)
+        output(2)
+        for q in range(4):
+            nc.scalar.dma_start(
+                out=out_2[0, 4 * q : 4 * q + 4, :].bitcast(I32),
+                in_=y_s[32 * q : 32 * q + 4, :].bitcast(I32),
+            )

@@ -3,6 +3,7 @@ from contextlib import ExitStack
 import concourse.mybir as mybir
 from concourse.masks import make_identity
 
+
 K, T, S, M, N = 1024, 2048, 1024, 1024, 512
 FLOPS = 2 * M * (K * S + S * N + K * N)
 
@@ -21,25 +22,32 @@ P = 128
 PACK = 4
 PASS = P * PACK
 CHUNKS = ((0, 256), (256, 512), (768, 256))
+XSPLIT = (1, 1, 1)
+OSPLIT = (1, 1, 1)
 GAP = 32
+BANKS = 8
+RING = 2
 
 
 def woven(tile_ap):
-    return tile_ap.rearrange("p (c i) t -> p c t i", i=4)
+    return tile_ap.rearrange("p (c i) t -> p c t i", i=2)
 
 
 def planes(tile_ap):
-    return tile_ap.rearrange("p t (c i) -> p c t i", i=4)
+    return tile_ap.rearrange("p t (c i) -> p c t i", i=2)
 
 
 def tile_list_cube_parser_layer_kernel(tc, x, tab_words, tab_scales, offs, b, g, wdT, w4_words, w4_scales, c, out_0, out_1, out_2):
     nc = tc.nc
     with ExitStack() as ctx:
         keep = ctx.enter_context(tc.tile_pool(name="keep", bufs=1))
-        ring = ctx.enter_context(tc.tile_pool(name="ring", bufs=2))
-        pre_pool = ctx.enter_context(tc.psum_pool(name="pre", bufs=3))
-        acc_pool = ctx.enter_context(tc.psum_pool(name="acc", bufs=4))
-        turn_pool = ctx.enter_context(tc.psum_pool(name="turn", bufs=1))
+        ring = ctx.enter_context(tc.tile_pool(name="ring", bufs=RING))
+        psum = ctx.enter_context(tc.psum_pool(name="psum", bufs=1))
+        taken = []
+
+        def next_bank():
+            taken.append(len(taken) % BANKS)
+            return psum.tile([P, 512], F32, name="bank%d" % taken[-1])
 
         def held(name, shape, dtype):
             return keep.tile(shape, dtype, name=name, align_bytes=64)
@@ -48,9 +56,9 @@ def tile_list_cube_parser_layer_kernel(tc, x, tab_words, tab_scales, offs, b, g,
         nc.sync.dma_start(offsets[:], offs)
 
         tab_s = held("tab_s", [P, T], U8)
-        nc.vector.memset(tab_s[:].bitcast(I32), 0)
+        nc.gpsimd.memset(tab_s[:].bitcast(I32), 0)
         for q in range(4):
-            nc.scalar.dma_start(
+            nc.sync.dma_start(
                 out=tab_s[32 * q : 32 * q + 8, :].bitcast(I32),
                 in_=tab_scales[:, 4 * q : 4 * q + 4, :].bitcast(I32),
             )
@@ -65,12 +73,13 @@ def tile_list_cube_parser_layer_kernel(tc, x, tab_words, tab_scales, offs, b, g,
 
         x_raw = {}
 
-        def load_x(ci):
+        def load_x(ci, a, k):
             m0, w = CHUNKS[ci]
-            for a in range(2):
-                raw = held("x_raw%d%d" % (ci, a), [P, PACK, w], F32)
-                nc.sync.dma_start(out=raw[:], in_=x[PASS * a : PASS * (a + 1), m0 : m0 + w].rearrange("(p i) m -> p i m", i=PACK))
-                x_raw[ci, a] = raw
+            w = w // XSPLIT[ci]
+            m0 = m0 + k * w
+            raw = held("x_raw%d%d%d" % (ci, a, k), [P, PACK, w], F32)
+            nc.sync.dma_start(out=raw[:], in_=x[PASS * a : PASS * (a + 1), m0 : m0 + w].rearrange("(p i) m -> p i m", i=PACK))
+            x_raw[ci, a, k] = raw
 
         wd_raw = {}
 
@@ -79,29 +88,42 @@ def tile_list_cube_parser_layer_kernel(tc, x, tab_words, tab_scales, offs, b, g,
             nc.sync.dma_start(out=raw[:], in_=wdT.rearrange("(p t) e -> p t e", t=PACK)[:, t, :])
             wd_raw[t] = raw
 
-        load_x(0)
-        tab_w = []
-        for a in range(2):
+        tab_w = {}
+
+        def load_table(a):
             words = held("tab_w%d" % a, [P, T], U32)
             nc.sync.dma_start(out=words[:].bitcast(I32), in_=tab_words[a].rearrange("p e i -> p (e i)").bitcast(I32))
-            tab_w.append(words)
-            if a == 0:
-                nc.sync.dma_start(out=b_sb[:], in_=b.rearrange("(g p t) -> p g t", g=2, t=PACK))
-                nc.sync.dma_start(out=g_sb[:], in_=g.rearrange("(g p t) -> p g t", g=2, t=PACK))
-        load_x(1)
-        load_wd(0)
+            tab_w[a] = words
+
+        def load_gains():
+            nc.sync.dma_start(out=b_sb[:], in_=b.rearrange("(g p t) -> p g t", g=2, t=PACK))
+            nc.sync.dma_start(out=g_sb[:], in_=g.rearrange("(g p t) -> p g t", g=2, t=PACK))
+
         w4_w = held("w4_w", [P, 2, 2 * N], U8)
-        nc.sync.dma_start(out=w4_w[:].bitcast(I32), in_=w4_words.rearrange("a p e -> p a e").bitcast(I32))
-        for q in range(4):
-            nc.sync.dma_start(
-                out=w4_s[32 * q : 32 * q + 4, :, :].bitcast(I32),
-                in_=w4_scales[:, 4 * q : 4 * q + 4, :].rearrange("a r n -> r a n").bitcast(I32),
-            )
-        nc.sync.dma_start(out=c_sb[:], in_=c.rearrange("(p t) -> p t", t=PACK))
-        load_wd(1)
-        load_x(2)
+
+        def load_w4():
+            nc.sync.dma_start(out=w4_w[:].bitcast(I32), in_=w4_words.rearrange("a p e -> p a e").bitcast(I32))
+            for q in range(4):
+                nc.sync.dma_start(
+                    out=w4_s[32 * q : 32 * q + 4, :, :].bitcast(I32),
+                    in_=w4_scales[:, 4 * q : 4 * q + 4, :].rearrange("a r n -> r a n").bitcast(I32),
+                )
+            nc.sync.dma_start(out=c_sb[:], in_=c.rearrange("(p t) -> p t", t=PACK))
+
+        load_gains()
+        load_x(0, 0, 0)
+        load_table(0)
+        load_x(0, 1, 0)
+        load_table(1)
         load_wd(2)
+        load_x(1, 0, 0)
+        load_x(2, 1, 0)
+        load_x(1, 1, 0)
+        load_x(2, 0, 0)
+        load_wd(0)
         load_wd(3)
+        load_wd(1)
+        load_w4()
 
         gb_sb = held("gb_sb", [P, 2, PACK], F32)
         nc.gpsimd.tensor_mul(out=gb_sb[:], in0=g_sb[:], in1=b_sb[:])
@@ -114,16 +136,19 @@ def tile_list_cube_parser_layer_kernel(tc, x, tab_words, tab_scales, offs, b, g,
             in_=v_s_listed[:].rearrange("p (g q t) -> p g t q", g=2, t=PACK),
         )
 
-        x_w, x_s, x_bf = {}, {}, {}
+        x_w, x_s, x_bf, x_cast = {}, {}, {}, set()
 
-        def cast_x(ci, a, on_vector):
+        def cast_x(ci, a, k, on_vector):
             w = CHUNKS[ci][1]
-            bf = held("x_bf%d%d" % (ci, a), [P, w, PACK], BF16)
+            if (ci, a) not in x_bf:
+                x_bf[ci, a] = held("x_bf%d%d" % (ci, a), [P, w * PACK], BF16)
+            n = w * PACK // XSPLIT[ci]
+            bf = x_bf[ci, a][:, k * n : (k + 1) * n].rearrange("p (m t) -> p m t", t=PACK)
             if on_vector:
-                nc.vector.tensor_copy(out=woven(bf[:]), in_=planes(x_raw[ci, a][:]))
+                nc.vector.tensor_copy(out=woven(bf), in_=planes(x_raw[ci, a, k][:]))
             else:
-                nc.scalar.activation(out=woven(bf[:]), in_=planes(x_raw[ci, a][:]), func=ACT.Copy)
-            x_bf[ci, a] = bf
+                nc.scalar.activation(out=woven(bf), in_=planes(x_raw[ci, a, k][:]), func=ACT.Copy)
+            x_cast.add((ci, a, k))
 
         def quantize(name, bf, width):
             words = held(name + "_w", [P, width], U32)
@@ -133,7 +158,8 @@ def tile_list_cube_parser_layer_kernel(tc, x, tab_words, tab_scales, offs, b, g,
 
         def quantize_x(ci, a):
             w = CHUNKS[ci][1]
-            x_w[ci, a], x_s[ci, a] = quantize("x%d%d" % (ci, a), x_bf[ci, a][:].rearrange("p m t -> p (m t)"), w)
+
+            x_w[ci, a], x_s[ci, a] = quantize("x%d%d" % (ci, a), x_bf[ci, a][:], w)
 
         v_w = {}
 
@@ -145,14 +171,14 @@ def tile_list_cube_parser_layer_kernel(tc, x, tab_words, tab_scales, offs, b, g,
             )
             v_w[a, jg] = words
 
-        h_w, h_s = {}, {}
+        h_w, h_s, h_bf, factors = {}, {}, {}, {}
 
-        def hidden(ci, jg):
+        def hidden(ci, jg, shared):
             w = CHUNKS[ci][1]
             sq = ring.tile([P, PACK, 512], F32, name="sq", align_bytes=64)
             lin = ring.tile([P, PACK, 512], F32, name="lin", align_bytes=64)
             for t in range(PACK):
-                pre = pre_pool.tile([P, 512], F32, name="pre")
+                pre = next_bank()
                 cols = slice(P * t, P * (t + 1))
                 scale_cols = slice(PASS * jg + P * t, PASS * jg + P * (t + 1))
                 for a in range(2):
@@ -166,26 +192,50 @@ def tile_list_cube_parser_layer_kernel(tc, x, tab_words, tab_scales, offs, b, g,
                         stop=(a == 1),
                     )
                 nc.scalar.activation(out=sq[:, t, :w], in_=pre[:, :w], func=ACT.Square, bias=b_sb[:, jg, t : t + 1])
-                nc.scalar.activation(
-                    out=lin[:, t, :w], in_=pre[:, :w], func=ACT.Identity,
-                    bias=gb_sb[:, jg, t : t + 1], scale=g_sb[:, jg, t : t + 1],
-                )
+                if shared:
+                    nc.vector.tensor_scalar(
+                        out=lin[:, t, :w], in0=pre[:, :w], scalar1=b_sb[:, jg, t : t + 1],
+                        scalar2=g_sb[:, jg, t : t + 1], op0=ALU.add, op1=ALU.mult,
+                    )
+                else:
+                    nc.scalar.activation(
+                        out=lin[:, t, :w], in_=pre[:, :w], func=ACT.Identity,
+                        bias=gb_sb[:, jg, t : t + 1], scale=g_sb[:, jg, t : t + 1],
+                    )
+            factors[ci, jg] = sq, lin
+
+        def cube(ci, jg, k):
+            w = CHUNKS[ci][1] // OSPLIT[ci]
+            cols = slice(k * w, (k + 1) * w)
+            sq, lin = factors[ci, jg]
             bf = ring.tile([P, 512, PACK], BF16, name="h_bf", align_bytes=64)
-            nc.vector.tensor_tensor(out=woven(bf[:, :w, :]), in0=planes(sq[:, :, :w]), in1=planes(lin[:, :, :w]), op=ALU.mult)
-            h_w[ci, jg], h_s[ci, jg] = quantize("h%d%d" % (ci, jg), bf[:, :w, :].rearrange("p m t -> p (m t)"), w)
+            h_bf[ci, jg, k] = bf
+            nc.vector.tensor_tensor(out=woven(bf[:, :w, :]), in0=planes(sq[:, :, cols]), in1=planes(lin[:, :, cols]), op=ALU.mult)
 
-        wd_w, wd_s = {}, {}
+        def quantize_h(ci, jg, k):
+            w = CHUNKS[ci][1] // OSPLIT[ci]
+            bf = h_bf[ci, jg, k]
+            h_w[ci, jg, k], h_s[ci, jg, k] = quantize("h%d%d%d" % (ci, jg, k), bf[:, :w, :].rearrange("p m t -> p (m t)"), w)
 
-        def down_weights(t):
-            picked = ring.tile([P, 2, PASS + GAP], BF16, name="wd_picked", align_bytes=64)
+        wd_w, wd_s, wd_picked, wd_bf = {}, {}, {}, {}
+
+        def gather_down(t):
+            picked = held("wd_picked%d" % t, [P, 2, PASS + GAP], BF16)
+            wd_picked[t] = picked
             nc.vector.tensor_copy(out=picked[:, :, :PASS], in_=wd_raw[t][:].indirect(offsets[:]))
-            pairs = picked[:].bitcast(F32)
-            turned = turn_pool.tile([P, 2, 2, P], F32, name="turned")
+
+        def turn_down(t):
+            pairs = wd_picked[t][:].bitcast(F32)
+            turned = next_bank()[:].rearrange("p (g u n) -> p g u n", g=2, u=2)
             for jg in range(2):
                 for u in range(2):
                     nc.tensor.transpose(turned[:, jg, u, :], pairs[:, jg, u : 2 * P : 2], ident[:])
-            bf = ring.tile([P, 2, P, PACK], BF16, name="wd_bf", align_bytes=64)
-            nc.scalar.copy(out=bf[:].bitcast(F32), in_=turned[:].rearrange("p g u n -> p g n u"))
+            bf = held("wd_bf%d" % t, [P, 2, P, PACK], BF16)
+            nc.scalar.copy(out=bf[:].bitcast(F32), in_=turned.rearrange("p g u n -> p g n u"))
+            wd_bf[t] = bf
+
+        def quantize_down(t):
+            bf = wd_bf[t]
             wd_w[t], wd_s[t] = quantize("wd%d" % t, bf[:].rearrange("p g n t -> p (g n t)"), 2 * P)
 
         w4_w_dealt = held("w4_w_dealt", [P, 2, 2 * N], U8)
@@ -205,21 +255,28 @@ def tile_list_cube_parser_layer_kernel(tc, x, tab_words, tab_scales, offs, b, g,
         y_rows = out_0.rearrange("(p t) m -> p t m", t=PACK)
         y_words = out_1[0].rearrange("p m t -> p (m t)")
 
-        def output(ci):
+        y_f32, y_bf = {}, {}
+
+        def piece(ci, k):
             m0, w = CHUNKS[ci]
-            last = ci == len(CHUNKS) - 1
-            y = held("y%d" % ci, [P, PACK, w], F32)
+            w = w // OSPLIT[ci]
+            return m0 + k * w, w
+
+        def output(ci, k, shared):
+            m0, w = piece(ci, k)
+            y = held("y%d%d" % (ci, k), [P, PACK, w], F32)
+            y_f32[ci, k] = y
             step = 512 if w == 512 else 128
             for t in range(PACK):
-                acc = acc_pool.tile([P, 512], F32, name="acc")
+                acc = next_bank()
                 for a in range(2):
                     for n0 in range(0, w, step):
                         nc.tensor.matmul_mx(
                             out=acc[:, n0 : n0 + step],
                             lhsT=w4_w_dealt[:, a, 2 * P * t : 2 * P * (t + 1)].bitcast(FP4X4),
                             lhsT_scale=w4_s_dealt[:, a, P * t : P * (t + 1)],
-                            rhs=x_w[ci, a][:, n0 : n0 + step].bitcast(FP8X4),
-                            rhs_scale=x_s[ci, a][:, n0 : n0 + step],
+                            rhs=x_w[ci, a][:, k * w + n0 : k * w + n0 + step].bitcast(FP8X4),
+                            rhs_scale=x_s[ci, a][:, k * w + n0 : k * w + n0 + step],
                             start=(a == 0 and n0 == 0),
                             stop=False,
                         )
@@ -228,51 +285,91 @@ def tile_list_cube_parser_layer_kernel(tc, x, tab_words, tab_scales, offs, b, g,
                         out=acc[:, :w],
                         lhsT=wd_w[t][:, P * jg : P * (jg + 1)].bitcast(FP8X4),
                         lhsT_scale=wd_s[t][:, P * jg : P * (jg + 1)],
-                        rhs=h_w[ci, jg][:].bitcast(FP8X4),
-                        rhs_scale=h_s[ci, jg][:],
+                        rhs=h_w[ci, jg, k][:].bitcast(FP8X4),
+                        rhs_scale=h_s[ci, jg, k][:],
                         start=False,
                         stop=(jg == 1),
                     )
-                if last and t % 2 == 1:
+                if shared and t % 2 == 1:
                     nc.vector.tensor_scalar_add(out=y[:, t, :], in0=acc[:, :w], scalar1=c_sb[:, t : t + 1])
                 else:
                     nc.scalar.activation(out=y[:, t, :], in_=acc[:, :w], func=ACT.Identity, bias=c_sb[:, t : t + 1])
-            nc.sync.dma_start(out=y_rows[:, :, m0 : m0 + w], in_=y[:])
-            bf = held("y_bf%d" % ci, [P, w, PACK], BF16)
-            nc.vector.tensor_copy(out=woven(bf[:]), in_=planes(y[:]))
-            words = held("y_w%d" % ci, [P, w], U32)
+                if t % 2 == 1:
+                    nc.sync.dma_start(out=y_rows[:, t - 1 : t + 1, m0 : m0 + w], in_=y[:, t - 1 : t + 1, :])
+
+        def cast_y(ci, k, cast_on_vector):
+            m0, w = piece(ci, k)
+            y = y_f32[ci, k]
+            bf = held("y_bf%d%d" % (ci, k), [P, w, PACK], BF16)
+            y_bf[ci, k] = bf
+            if cast_on_vector:
+                nc.vector.tensor_copy(out=woven(bf[:]), in_=planes(y[:]))
+            else:
+                nc.scalar.activation(out=woven(bf[:]), in_=planes(y[:]), func=ACT.Copy)
+
+        def quantize_y(ci, k):
+            m0, w = piece(ci, k)
+            bf = y_bf[ci, k]
+            words = held("y_w%d%d" % (ci, k), [P, w], U32)
             nc.vector.quantize_mx(out=words[:].bitcast(FP8X4), scales=y_s[:, m0 : m0 + w], in_=bf[:].rearrange("p m t -> p (m t)"))
             nc.sync.dma_start(out=y_words[:, 4 * m0 : 4 * (m0 + w)].bitcast(I32), in_=words[:].bitcast(I32))
 
-        for a in range(2):
-            cast_x(0, a, False)
-        for a in range(2):
-            quantize_x(0, a)
+        cast_x(0, 1, 0, False)
+        quantize_x(0, 1)
         gather_table(0, 0)
-        gather_table(1, 0)
-        gather_table(0, 1)
         gather_table(1, 1)
-        hidden(0, 0)
-        for a in range(2):
-            cast_x(1, a, False)
-            quantize_x(1, a)
-        hidden(0, 1)
-        down_weights(0)
-        hidden(1, 0)
+        cast_x(0, 0, 0, False)
+        gather_table(1, 0)
+        cast_x(1, 0, 0, True)
+        gather_down(1)
+        cast_x(2, 1, 0, True)
+        quantize_x(2, 1)
+        quantize_x(0, 0)
+        gather_table(0, 1)
+        gather_down(0)
+        hidden(0, 0, False)
+        cast_x(2, 0, 0, False)
+        cube(0, 0, 0)
+        quantize_x(1, 0)
+        cast_x(1, 1, 0, False)
+        hidden(0, 1, False)
+        cube(0, 1, 0)
+        quantize_x(1, 1)
+        hidden(1, 0, False)
+        quantize_h(0, 0, 0)
+        turn_down(0)
+        cube(1, 0, 0)
+        quantize_h(0, 1, 0)
+        gather_down(2)
+        hidden(1, 1, False)
+        quantize_x(2, 0)
+        turn_down(1)
+        gather_down(3)
+        cube(1, 1, 0)
+        hidden(2, 1, False)
+        turn_down(2)
+        turn_down(3)
+        quantize_h(1, 0, 0)
+        quantize_h(1, 1, 0)
         deal_w4()
-        down_weights(1)
-        for a in range(2):
-            cast_x(2, a, True)
-        for a in range(2):
-            quantize_x(2, a)
-        down_weights(2)
-        hidden(1, 1)
-        down_weights(3)
-        hidden(2, 0)
-        output(0)
-        hidden(2, 1)
-        output(1)
-        output(2)
+        quantize_down(1)
+        quantize_down(2)
+        quantize_down(3)
+        quantize_down(0)
+        output(1, 0, True)
+        hidden(2, 0, True)
+        cube(2, 0, 0)
+        output(0, 0, True)
+        cast_y(0, 0, True)
+        cube(2, 1, 0)
+        quantize_h(2, 0, 0)
+        quantize_h(2, 1, 0)
+        output(2, 0, False)
+        cast_y(1, 0, False)
+        cast_y(2, 0, True)
+        quantize_y(1, 0)
+        quantize_y(0, 0)
+        quantize_y(2, 0)
         for q in range(4):
             nc.scalar.dma_start(
                 out=out_2[0, 4 * q : 4 * q + 4, :].bitcast(I32),

@@ -26,7 +26,8 @@ XSPLIT = (1, 1, 1)
 OSPLIT = (1, 1, 1)
 GAP = 32
 BANKS = 8
-RING = 2
+RING = 9
+STAGES = 5
 
 
 def woven(tile_ap):
@@ -41,13 +42,18 @@ def tile_list_cube_parser_layer_kernel(tc, x, tab_words, tab_scales, offs, b, g,
     nc = tc.nc
     with ExitStack() as ctx:
         keep = ctx.enter_context(tc.tile_pool(name="keep", bufs=1))
-        ring = ctx.enter_context(tc.tile_pool(name="ring", bufs=RING))
         psum = ctx.enter_context(tc.psum_pool(name="psum", bufs=1))
         taken = []
 
         def next_bank():
             taken.append(len(taken) % BANKS)
             return psum.tile([P, 512], F32, name="bank%d" % taken[-1])
+
+        staged = []
+
+        def next_stage(shape):
+            staged.append(len(staged) % STAGES)
+            return keep.tile(shape, BF16, name="stage%d" % staged[-1], align_bytes=64)
 
         def held(name, shape, dtype):
             return keep.tile(shape, dtype, name=name, align_bytes=64)
@@ -96,8 +102,8 @@ def tile_list_cube_parser_layer_kernel(tc, x, tab_words, tab_scales, offs, b, g,
             tab_w[a] = words
 
         def load_gains():
-            nc.sync.dma_start(out=b_sb[:], in_=b.rearrange("(g p t) -> p g t", g=2, t=PACK))
-            nc.sync.dma_start(out=g_sb[:], in_=g.rearrange("(g p t) -> p g t", g=2, t=PACK))
+            nc.scalar.dma_start(out=b_sb[:], in_=b.rearrange("(g p t) -> p g t", g=2, t=PACK))
+            nc.scalar.dma_start(out=g_sb[:], in_=g.rearrange("(g p t) -> p g t", g=2, t=PACK))
 
         w4_w = held("w4_w", [P, 2, 2 * N], U8)
 
@@ -110,19 +116,19 @@ def tile_list_cube_parser_layer_kernel(tc, x, tab_words, tab_scales, offs, b, g,
                 )
             nc.sync.dma_start(out=c_sb[:], in_=c.rearrange("(p t) -> p t", t=PACK))
 
-        load_gains()
         load_x(0, 0, 0)
+        load_gains()
         load_table(0)
         load_x(0, 1, 0)
         load_table(1)
-        load_wd(2)
         load_x(1, 0, 0)
-        load_x(2, 1, 0)
         load_x(1, 1, 0)
-        load_x(2, 0, 0)
         load_wd(0)
-        load_wd(3)
+        load_wd(2)
         load_wd(1)
+        load_wd(3)
+        load_x(2, 0, 0)
+        load_x(2, 1, 0)
         load_w4()
 
         gb_sb = held("gb_sb", [P, 2, PACK], F32)
@@ -141,7 +147,7 @@ def tile_list_cube_parser_layer_kernel(tc, x, tab_words, tab_scales, offs, b, g,
         def cast_x(ci, a, k, on_vector):
             w = CHUNKS[ci][1]
             if (ci, a) not in x_bf:
-                x_bf[ci, a] = held("x_bf%d%d" % (ci, a), [P, w * PACK], BF16)
+                x_bf[ci, a] = next_stage([P, w * PACK])
             n = w * PACK // XSPLIT[ci]
             bf = x_bf[ci, a][:, k * n : (k + 1) * n].rearrange("p (m t) -> p m t", t=PACK)
             if on_vector:
@@ -175,8 +181,8 @@ def tile_list_cube_parser_layer_kernel(tc, x, tab_words, tab_scales, offs, b, g,
 
         def hidden(ci, jg, shared):
             w = CHUNKS[ci][1]
-            sq = ring.tile([P, PACK, 512], F32, name="sq", align_bytes=64)
-            lin = ring.tile([P, PACK, 512], F32, name="lin", align_bytes=64)
+            sq = held("sq%d%d" % (ci, jg), [P, PACK, w], F32)
+            lin = held("lin%d%d" % (ci, jg), [P, PACK, w], F32)
             for t in range(PACK):
                 pre = next_bank()
                 cols = slice(P * t, P * (t + 1))
@@ -208,7 +214,7 @@ def tile_list_cube_parser_layer_kernel(tc, x, tab_words, tab_scales, offs, b, g,
             w = CHUNKS[ci][1] // OSPLIT[ci]
             cols = slice(k * w, (k + 1) * w)
             sq, lin = factors[ci, jg]
-            bf = ring.tile([P, 512, PACK], BF16, name="h_bf", align_bytes=64)
+            bf = next_stage([P, w, PACK])
             h_bf[ci, jg, k] = bf
             nc.vector.tensor_tensor(out=woven(bf[:, :w, :]), in0=planes(sq[:, :, cols]), in1=planes(lin[:, :, cols]), op=ALU.mult)
 
@@ -220,7 +226,7 @@ def tile_list_cube_parser_layer_kernel(tc, x, tab_words, tab_scales, offs, b, g,
         wd_w, wd_s, wd_picked, wd_bf = {}, {}, {}, {}
 
         def gather_down(t):
-            picked = held("wd_picked%d" % t, [P, 2, PASS + GAP], BF16)
+            picked = next_stage([P, 2, PASS + GAP])
             wd_picked[t] = picked
             nc.vector.tensor_copy(out=picked[:, :, :PASS], in_=wd_raw[t][:].indirect(offsets[:]))
 
@@ -230,7 +236,7 @@ def tile_list_cube_parser_layer_kernel(tc, x, tab_words, tab_scales, offs, b, g,
             for jg in range(2):
                 for u in range(2):
                     nc.tensor.transpose(turned[:, jg, u, :], pairs[:, jg, u : 2 * P : 2], ident[:])
-            bf = held("wd_bf%d" % t, [P, 2, P, PACK], BF16)
+            bf = next_stage([P, 2, P, PACK])
             nc.scalar.copy(out=bf[:].bitcast(F32), in_=turned.rearrange("p g u n -> p g n u"))
             wd_bf[t] = bf
 
@@ -264,7 +270,7 @@ def tile_list_cube_parser_layer_kernel(tc, x, tab_words, tab_scales, offs, b, g,
 
         def output(ci, k, shared):
             m0, w = piece(ci, k)
-            y = held("y%d%d" % (ci, k), [P, PACK, w], F32)
+            y = held("x_raw%d0%d" % (ci, k), [P, PACK, w], F32)
             y_f32[ci, k] = y
             step = 512 if w == 512 else 128
             for t in range(PACK):
@@ -300,7 +306,7 @@ def tile_list_cube_parser_layer_kernel(tc, x, tab_words, tab_scales, offs, b, g,
         def cast_y(ci, k, cast_on_vector):
             m0, w = piece(ci, k)
             y = y_f32[ci, k]
-            bf = held("y_bf%d%d" % (ci, k), [P, w, PACK], BF16)
+            bf = next_stage([P, w, PACK])
             y_bf[ci, k] = bf
             if cast_on_vector:
                 nc.vector.tensor_copy(out=woven(bf[:]), in_=planes(y[:]))
@@ -314,61 +320,61 @@ def tile_list_cube_parser_layer_kernel(tc, x, tab_words, tab_scales, offs, b, g,
             nc.vector.quantize_mx(out=words[:].bitcast(FP8X4), scales=y_s[:, m0 : m0 + w], in_=bf[:].rearrange("p m t -> p (m t)"))
             nc.sync.dma_start(out=y_words[:, 4 * m0 : 4 * (m0 + w)].bitcast(I32), in_=words[:].bitcast(I32))
 
-        cast_x(0, 1, 0, False)
-        quantize_x(0, 1)
         gather_table(0, 0)
-        gather_table(1, 1)
+        cast_x(1, 1, 0, True)
         cast_x(0, 0, 0, False)
-        gather_table(1, 0)
-        cast_x(1, 0, 0, True)
-        gather_down(1)
-        cast_x(2, 1, 0, True)
-        quantize_x(2, 1)
+        cast_x(0, 1, 0, False)
         quantize_x(0, 0)
-        gather_table(0, 1)
-        gather_down(0)
-        hidden(0, 0, False)
-        cast_x(2, 0, 0, False)
-        cube(0, 0, 0)
-        quantize_x(1, 0)
-        cast_x(1, 1, 0, False)
-        hidden(0, 1, False)
-        cube(0, 1, 0)
         quantize_x(1, 1)
-        hidden(1, 0, False)
+        quantize_x(0, 1)
+        gather_table(1, 0)
+        hidden(0, 0, False)
+        gather_table(1, 1)
+        cast_x(1, 0, 0, True)
+        cube(0, 0, 0)
+        gather_table(0, 1)
+        hidden(0, 1, False)
+        gather_down(1)
+        quantize_x(1, 0)
         quantize_h(0, 0, 0)
-        turn_down(0)
-        cube(1, 0, 0)
-        quantize_h(0, 1, 0)
+        cube(0, 1, 0)
+        gather_down(0)
         gather_down(2)
-        hidden(1, 1, False)
-        quantize_x(2, 0)
-        turn_down(1)
-        gather_down(3)
-        cube(1, 1, 0)
-        hidden(2, 1, False)
-        turn_down(2)
-        turn_down(3)
-        quantize_h(1, 0, 0)
-        quantize_h(1, 1, 0)
+        turn_down(0)
         deal_w4()
+        turn_down(1)
+        quantize_h(0, 1, 0)
+        gather_down(3)
+        cast_x(2, 1, 0, False)
+        hidden(1, 0, False)
         quantize_down(1)
-        quantize_down(2)
-        quantize_down(3)
+        hidden(1, 1, False)
+        turn_down(2)
+        quantize_x(2, 1)
         quantize_down(0)
-        output(1, 0, True)
-        hidden(2, 0, True)
-        cube(2, 0, 0)
-        output(0, 0, True)
-        cast_y(0, 0, True)
+        cast_x(2, 0, 0, True)
+        turn_down(3)
+        quantize_down(3)
+        quantize_x(2, 0)
+        cube(1, 1, 0)
+        cube(1, 0, 0)
+        quantize_down(2)
+        hidden(2, 1, False)
+        output(0, 0, False)
+        quantize_h(1, 1, 0)
+        hidden(2, 0, False)
+        quantize_h(1, 0, 0)
         cube(2, 1, 0)
+        cast_y(0, 0, True)
+        output(1, 0, False)
+        cube(2, 0, 0)
+        cast_y(1, 0, True)
         quantize_h(2, 0, 0)
         quantize_h(2, 1, 0)
-        output(2, 0, False)
-        cast_y(1, 0, False)
-        cast_y(2, 0, True)
         quantize_y(1, 0)
+        output(2, 0, False)
         quantize_y(0, 0)
+        cast_y(2, 0, True)
         quantize_y(2, 0)
         for q in range(4):
             nc.scalar.dma_start(

@@ -107,8 +107,9 @@ def tile_list_cube_parser_layer_kernel(tc, x, tab_words, tab_scales, offs, b, g,
 
         w4_w = held("w4_w", [P, 2, 2 * N], U8)
 
+        nc.sync.dma_start(out=w4_w[:].bitcast(I32), in_=w4_words.rearrange("a p e -> p a e").bitcast(I32))
+
         def load_w4():
-            nc.sync.dma_start(out=w4_w[:].bitcast(I32), in_=w4_words.rearrange("a p e -> p a e").bitcast(I32))
             for q in range(4):
                 nc.sync.dma_start(
                     out=w4_s[32 * q : 32 * q + 4, :, :].bitcast(I32),
@@ -247,11 +248,12 @@ def tile_list_cube_parser_layer_kernel(tc, x, tab_words, tab_scales, offs, b, g,
         w4_w_dealt = held("w4_w_dealt", [P, 2, 2 * N], U8)
         w4_s_dealt = held("w4_s_dealt", [P, 2, N], U8)
 
+        nc.vector.tensor_copy(
+            out=w4_w_dealt[:].bitcast(U16).rearrange("p a (t q) -> p a t q", t=PACK),
+            in_=w4_w[:].bitcast(U16).rearrange("p a (q t) -> p a t q", t=PACK),
+        )
+
         def deal_w4():
-            nc.vector.tensor_copy(
-                out=w4_w_dealt[:].bitcast(U16).rearrange("p a (t q) -> p a t q", t=PACK),
-                in_=w4_w[:].bitcast(U16).rearrange("p a (q t) -> p a t q", t=PACK),
-            )
             nc.vector.tensor_copy(
                 out=w4_s_dealt[:].rearrange("p a (t q) -> p a t q", t=PACK),
                 in_=w4_s[:].rearrange("p a (q t) -> p a t q", t=PACK),

@@ -31,11 +31,11 @@ STAGES = 5
 
 
 def woven(tile_ap):
-    return tile_ap.rearrange("p (c i) t -> p c t i", i=2)
+    return tile_ap.rearrange("p (c i) t -> p c t i", i=4)
 
 
 def planes(tile_ap):
-    return tile_ap.rearrange("p t (c i) -> p c t i", i=2)
+    return tile_ap.rearrange("p t (c i) -> p c t i", i=4)
 
 
 def tile_list_cube_parser_layer_kernel(tc, x, tab_words, tab_scales, offs, b, g, wdT, w4_words, w4_scales, c, out_0, out_1, out_2):

@@ -3,7 +3,6 @@ from contextlib import ExitStack
 import concourse.mybir as mybir
 from concourse.masks import make_identity
 
-
 K, T, S, M, N = 1024, 2048, 1024, 1024, 512
 FLOPS = 2 * M * (K * S + S * N + K * N)
 
@@ -21,21 +20,17 @@ ALU = mybir.AluOpType
 P = 128
 PACK = 4
 PASS = P * PACK
-CHUNKS = ((0, 256), (256, 512), (768, 256))
-XSPLIT = (1, 1, 1)
-OSPLIT = (1, 1, 1)
 GAP = 32
-BANKS = 8
-RING = 9
-STAGES = 5
+BANKS = 5
+CHUNKS = ((0, 256), (256, 512), (768, 256))
 
 
 def woven(tile_ap):
-    return tile_ap.rearrange("p (c i) t -> p c t i", i=4)
+    return tile_ap.rearrange("p (c i) t -> p c t i", i=PACK)
 
 
 def planes(tile_ap):
-    return tile_ap.rearrange("p t (c i) -> p c t i", i=4)
+    return tile_ap.rearrange("p t (c i) -> p c t i", i=PACK)
 
 
 def tile_list_cube_parser_layer_kernel(tc, x, tab_words, tab_scales, offs, b, g, wdT, w4_words, w4_scales, c, out_0, out_1, out_2):
@@ -49,17 +44,16 @@ def tile_list_cube_parser_layer_kernel(tc, x, tab_words, tab_scales, offs, b, g,
             taken.append(len(taken) % BANKS)
             return psum.tile([P, 512], F32, name="bank%d" % taken[-1])
 
-        staged = []
-
-        def next_stage(shape):
-            staged.append(len(staged) % STAGES)
-            return keep.tile(shape, BF16, name="stage%d" % staged[-1], align_bytes=64)
-
         def held(name, shape, dtype):
             return keep.tile(shape, dtype, name=name, align_bytes=64)
 
         offsets = keep.tile([P, S // 16], U16, name="offsets")
         nc.sync.dma_start(offsets[:], offs)
+
+        b_sb = held("b_sb", [P, 2, PACK], F32)
+        g_sb = held("g_sb", [P, 2, PACK], F32)
+        nc.sync.dma_start(out=b_sb[:], in_=b.rearrange("(g p t) -> p g t", g=2, t=PACK))
+        nc.sync.dma_start(out=g_sb[:], in_=g.rearrange("(g p t) -> p g t", g=2, t=PACK))
 
         tab_s = held("tab_s", [P, T], U8)
         nc.gpsimd.memset(tab_s[:].bitcast(I32), 0)
@@ -73,43 +67,32 @@ def tile_list_cube_parser_layer_kernel(tc, x, tab_words, tab_scales, offs, b, g,
         ident = held("ident", [P, P], F32)
         make_identity(nc, ident[:])
 
-        b_sb = held("b_sb", [P, 2, PACK], F32)
-        g_sb = held("g_sb", [P, 2, PACK], F32)
+        gb_sb = held("gb_sb", [P, 2, PACK], F32)
+        nc.gpsimd.tensor_mul(out=gb_sb[:], in0=g_sb[:], in1=b_sb[:])
         c_sb = held("c_sb", [P, PACK], F32)
+        w4_w = held("w4_w", [P, 2, 2 * N], U8)
+        x_raw, wd_raw, tab_w = {}, {}, {}
 
-        x_raw = {}
-
-        def load_x(ci, a, k):
+        def load_x(ci, a):
             m0, w = CHUNKS[ci]
-            w = w // XSPLIT[ci]
-            m0 = m0 + k * w
-            raw = held("x_raw%d%d%d" % (ci, a, k), [P, PACK, w], F32)
+            raw = held("x_raw%d%d" % (ci, a), [P, PACK, w], F32)
             nc.sync.dma_start(out=raw[:], in_=x[PASS * a : PASS * (a + 1), m0 : m0 + w].rearrange("(p i) m -> p i m", i=PACK))
-            x_raw[ci, a, k] = raw
+            x_raw[ci, a] = raw
 
-        wd_raw = {}
-
-        def load_wd(t):
+        def load_down(t):
             raw = held("wd_raw%d" % t, [P, T], F32)
             nc.sync.dma_start(out=raw[:], in_=wdT.rearrange("(p t) e -> p t e", t=PACK)[:, t, :])
             wd_raw[t] = raw
-
-        tab_w = {}
 
         def load_table(a):
             words = held("tab_w%d" % a, [P, T], U32)
             nc.sync.dma_start(out=words[:].bitcast(I32), in_=tab_words[a].rearrange("p e i -> p (e i)").bitcast(I32))
             tab_w[a] = words
 
-        def load_gains():
-            nc.scalar.dma_start(out=b_sb[:], in_=b.rearrange("(g p t) -> p g t", g=2, t=PACK))
-            nc.scalar.dma_start(out=g_sb[:], in_=g.rearrange("(g p t) -> p g t", g=2, t=PACK))
+        def load_bypass_words():
+            nc.sync.dma_start(out=w4_w[:].bitcast(I32), in_=w4_words.rearrange("a p e -> p a e").bitcast(I32))
 
-        w4_w = held("w4_w", [P, 2, 2 * N], U8)
-
-        nc.sync.dma_start(out=w4_w[:].bitcast(I32), in_=w4_words.rearrange("a p e -> p a e").bitcast(I32))
-
-        def load_w4():
+        def load_bypass_scales():
             for q in range(4):
                 nc.sync.dma_start(
                     out=w4_s[32 * q : 32 * q + 4, :, :].bitcast(I32),
@@ -117,143 +100,125 @@ def tile_list_cube_parser_layer_kernel(tc, x, tab_words, tab_scales, offs, b, g,
                 )
             nc.sync.dma_start(out=c_sb[:], in_=c.rearrange("(p t) -> p t", t=PACK))
 
-        load_x(0, 0, 0)
-        load_gains()
-        load_table(0)
-        load_x(0, 1, 0)
-        load_table(1)
-        load_x(1, 0, 0)
-        load_x(1, 1, 0)
-        load_wd(0)
-        load_wd(2)
-        load_wd(1)
-        load_wd(3)
-        load_x(2, 0, 0)
-        load_x(2, 1, 0)
-        load_w4()
-
-        gb_sb = held("gb_sb", [P, 2, PACK], F32)
-        nc.gpsimd.tensor_mul(out=gb_sb[:], in0=g_sb[:], in1=b_sb[:])
-
-        v_s_listed = held("v_s_listed", [P, S], U8)
-        nc.vector.tensor_copy(out=v_s_listed[:], in_=tab_s[:].indirect(offsets[:]))
         v_s = held("v_s", [P, S], U8)
-        nc.vector.tensor_copy(
-            out=v_s[:].rearrange("p (g t q) -> p g t q", g=2, t=PACK),
-            in_=v_s_listed[:].rearrange("p (g q t) -> p g t q", g=2, t=PACK),
-        )
 
-        x_w, x_s, x_bf, x_cast = {}, {}, {}, set()
-
-        def cast_x(ci, a, k, on_vector):
-            w = CHUNKS[ci][1]
-            if (ci, a) not in x_bf:
-                x_bf[ci, a] = next_stage([P, w * PACK])
-            n = w * PACK // XSPLIT[ci]
-            bf = x_bf[ci, a][:, k * n : (k + 1) * n].rearrange("p (m t) -> p m t", t=PACK)
-            if on_vector:
-                nc.vector.tensor_copy(out=woven(bf), in_=planes(x_raw[ci, a, k][:]))
-            else:
-                nc.scalar.activation(out=woven(bf), in_=planes(x_raw[ci, a, k][:]), func=ACT.Copy)
-            x_cast.add((ci, a, k))
-
-        def quantize(name, bf, width):
-            words = held(name + "_w", [P, width], U32)
-            scales = held(name + "_s", [P, width], U8)
-            nc.vector.quantize_mx(out=words[:].bitcast(FP8X4), scales=scales[:], in_=bf)
-            return words, scales
-
-        def quantize_x(ci, a):
-            w = CHUNKS[ci][1]
-
-            x_w[ci, a], x_s[ci, a] = quantize("x%d%d" % (ci, a), x_bf[ci, a][:], w)
+        def gather_scales():
+            listed = held("v_s_listed", [P, S], U8)
+            nc.vector.tensor_copy(out=listed[:], in_=tab_s[:].indirect(offsets[:]))
+            nc.vector.tensor_copy(
+                out=v_s[:].rearrange("p (g t q) -> p g t q", g=2, t=PACK),
+                in_=listed[:].rearrange("p (g q t) -> p g t q", g=2, t=PACK),
+            )
 
         v_w = {}
 
-        def gather_table(a, jg):
-            words = held("v_w%d%d" % (a, jg), [P, PASS], U32)
+        def gather_table(a, groups, tag=None):
+            first, count = groups[0], len(groups)
+            words = held(tag or "v_w%d%d" % (a, first), [P, count, PASS], U32)
             nc.vector.tensor_copy(
-                out=words[:].rearrange("p (t q) -> p q t", t=PACK),
-                in_=tab_w[a][:].indirect(offsets[:, 32 * jg : 32 * (jg + 1)]),
+                out=words[:].rearrange("p g (t q) -> p g q t", t=PACK),
+                in_=tab_w[a][:].indirect(offsets[:, 32 * first : 32 * (first + count)]),
             )
-            v_w[a, jg] = words
+            for jg in groups:
+                v_w[a, jg] = words[:, jg - first, :]
 
-        h_w, h_s, h_bf, factors = {}, {}, {}, {}
+        def weave(engine, out, in_):
+            if engine is nc.vector:
+                nc.vector.tensor_copy(out=woven(out), in_=planes(in_))
+            else:
+                nc.scalar.activation(out=woven(out), in_=planes(in_), func=ACT.Copy)
 
-        def hidden(ci, jg, shared):
+        def quantize(name, bf, tags=None):
+            count, width = bf.shape[1], bf.shape[2]
+            words = held(tags[0] if tags else name + "_w", [P, count, width], U32)
+            scales = held(tags[1] if tags and len(tags) > 1 else name + "_s", [P, count, width], U8)
+            nc.vector.quantize_mx(
+                out=words[:].rearrange("p o m -> p (o m)").bitcast(FP8X4),
+                scales=scales[:].rearrange("p o m -> p (o m)"),
+                in_=bf[:].rearrange("p o m t -> p (o m t)"),
+            )
+            return [(words[:, o, :], scales[:, o, :]) for o in range(count)]
+
+        x_bf, x_q = {}, {}
+
+        def cast_x(ci, passes, engine, tag=None):
             w = CHUNKS[ci][1]
-            sq = held("sq%d%d" % (ci, jg), [P, PACK, w], F32)
-            lin = held("lin%d%d" % (ci, jg), [P, PACK, w], F32)
+            bf = held(tag or "x_bf%d%d" % (ci, passes[0]), [P, len(passes), w, PACK], BF16)
+            for o, a in enumerate(passes):
+                weave(engine, bf[:, o], x_raw[ci, a][:])
+            x_bf[ci, passes] = bf
+
+        def quantize_x(ci, passes, tags=None):
+            for a, made in zip(passes, quantize("x%d%d" % (ci, passes[0]), x_bf[ci, passes], tags)):
+                x_q[ci, a] = made
+
+        factors, h_bf, h_q = {}, {}, {}
+
+        def hidden(ci, jg, tag):
+            w = CHUNKS[ci][1]
+            sq = held("sq" + tag, [P, PACK, w], F32)
+            lin = held("lin" + tag, [P, PACK, w], F32)
             for t in range(PACK):
                 pre = next_bank()
-                cols = slice(P * t, P * (t + 1))
-                scale_cols = slice(PASS * jg + P * t, PASS * jg + P * (t + 1))
                 for a in range(2):
                     nc.tensor.matmul_mx(
                         out=pre[:, :w],
-                        lhsT=v_w[a, jg][:, cols].bitcast(FP8X4),
-                        lhsT_scale=v_s[4 * a : P, scale_cols],
-                        rhs=x_w[ci, a][:].bitcast(FP8X4),
-                        rhs_scale=x_s[ci, a][:],
+                        lhsT=v_w[a, jg][:, P * t : P * (t + 1)].bitcast(FP8X4),
+                        lhsT_scale=v_s[4 * a : P, PASS * jg + P * t : PASS * jg + P * (t + 1)],
+                        rhs=x_q[ci, a][0].bitcast(FP8X4),
+                        rhs_scale=x_q[ci, a][1],
                         start=(a == 0),
                         stop=(a == 1),
                     )
-                nc.scalar.activation(out=sq[:, t, :w], in_=pre[:, :w], func=ACT.Square, bias=b_sb[:, jg, t : t + 1])
-                if shared:
-                    nc.vector.tensor_scalar(
-                        out=lin[:, t, :w], in0=pre[:, :w], scalar1=b_sb[:, jg, t : t + 1],
-                        scalar2=g_sb[:, jg, t : t + 1], op0=ALU.add, op1=ALU.mult,
-                    )
-                else:
-                    nc.scalar.activation(
-                        out=lin[:, t, :w], in_=pre[:, :w], func=ACT.Identity,
-                        bias=gb_sb[:, jg, t : t + 1], scale=g_sb[:, jg, t : t + 1],
-                    )
+                nc.scalar.activation(out=sq[:, t, :], in_=pre[:, :w], func=ACT.Square, bias=b_sb[:, jg, t : t + 1])
+                nc.scalar.activation(
+                    out=lin[:, t, :], in_=pre[:, :w], func=ACT.Identity,
+                    bias=gb_sb[:, jg, t : t + 1], scale=g_sb[:, jg, t : t + 1],
+                )
             factors[ci, jg] = sq, lin
 
-        def cube(ci, jg, k):
-            w = CHUNKS[ci][1] // OSPLIT[ci]
-            cols = slice(k * w, (k + 1) * w)
+        def cube(ci, jg, tag=None):
             sq, lin = factors[ci, jg]
-            bf = next_stage([P, w, PACK])
-            h_bf[ci, jg, k] = bf
-            nc.vector.tensor_tensor(out=woven(bf[:, :w, :]), in0=planes(sq[:, :, cols]), in1=planes(lin[:, :, cols]), op=ALU.mult)
+            bf = held(tag or "h_bf%d%d" % (ci, jg), [P, 1, CHUNKS[ci][1], PACK], BF16)
+            nc.vector.tensor_tensor(out=woven(bf[:, 0]), in0=planes(sq[:]), in1=planes(lin[:]), op=ALU.mult)
+            h_bf[ci, jg] = bf
 
-        def quantize_h(ci, jg, k):
-            w = CHUNKS[ci][1] // OSPLIT[ci]
-            bf = h_bf[ci, jg, k]
-            h_w[ci, jg, k], h_s[ci, jg, k] = quantize("h%d%d%d" % (ci, jg, k), bf[:, :w, :].rearrange("p m t -> p (m t)"), w)
+        def quantize_h(ci, jg, tags=None):
+            h_q[ci, jg] = quantize("h%d%d" % (ci, jg), h_bf[ci, jg], tags)[0]
 
-        wd_w, wd_s, wd_picked, wd_bf = {}, {}, {}, {}
+        wd_picked, wd_bf, wd_q = {}, {}, {}
 
-        def gather_down(t):
-            picked = next_stage([P, 2, PASS + GAP])
-            wd_picked[t] = picked
+        def gather_down(t, tag=None):
+            picked = held(tag or "picked%d" % t, [P, 2, PASS + GAP], BF16)
             nc.vector.tensor_copy(out=picked[:, :, :PASS], in_=wd_raw[t][:].indirect(offsets[:]))
+            wd_picked[t] = picked
 
-        def turn_down(t):
+        def turn_down(t, slices):
+            if slices not in wd_bf:
+                wd_bf[slices] = held("wd_bf%d" % slices[0], [P, 2 * len(slices), P, PACK], BF16)
             pairs = wd_picked[t][:].bitcast(F32)
             turned = next_bank()[:].rearrange("p (g u n) -> p g u n", g=2, u=2)
             for jg in range(2):
                 for u in range(2):
                     nc.tensor.transpose(turned[:, jg, u, :], pairs[:, jg, u : 2 * P : 2], ident[:])
-            bf = next_stage([P, 2, P, PACK])
-            nc.scalar.copy(out=bf[:].bitcast(F32), in_=turned.rearrange("p g u n -> p g n u"))
-            wd_bf[t] = bf
+            o = 2 * slices.index(t)
+            nc.scalar.copy(out=wd_bf[slices][:, o : o + 2].bitcast(F32), in_=turned.rearrange("p g u n -> p g n u"))
 
-        def quantize_down(t):
-            bf = wd_bf[t]
-            wd_w[t], wd_s[t] = quantize("wd%d" % t, bf[:].rearrange("p g n t -> p (g n t)"), 2 * P)
+        def quantize_down(slices, tags=None):
+            made = quantize("wd%d" % slices[0], wd_bf[slices], tags)
+            for o, t in enumerate(slices):
+                wd_q[t] = made[2 * o : 2 * o + 2]
 
         w4_w_dealt = held("w4_w_dealt", [P, 2, 2 * N], U8)
         w4_s_dealt = held("w4_s_dealt", [P, 2, N], U8)
 
-        nc.vector.tensor_copy(
-            out=w4_w_dealt[:].bitcast(U16).rearrange("p a (t q) -> p a t q", t=PACK),
-            in_=w4_w[:].bitcast(U16).rearrange("p a (q t) -> p a t q", t=PACK),
-        )
+        def deal_bypass_words():
+            nc.vector.tensor_copy(
+                out=w4_w_dealt[:].bitcast(U16).rearrange("p a (t q) -> p a t q", t=PACK),
+                in_=w4_w[:].bitcast(U16).rearrange("p a (q t) -> p a t q", t=PACK),
+            )
 
-        def deal_w4():
+        def deal_bypass_scales():
             nc.vector.tensor_copy(
                 out=w4_s_dealt[:].rearrange("p a (t q) -> p a t q", t=PACK),
                 in_=w4_s[:].rearrange("p a (q t) -> p a t q", t=PACK),
@@ -262,124 +227,133 @@ def tile_list_cube_parser_layer_kernel(tc, x, tab_words, tab_scales, offs, b, g,
         y_s = held("y_s", [P, M], U8)
         y_rows = out_0.rearrange("(p t) m -> p t m", t=PACK)
         y_words = out_1[0].rearrange("p m t -> p (m t)")
-
         y_f32, y_bf = {}, {}
 
-        def piece(ci, k):
+        def output(ci, t):
             m0, w = CHUNKS[ci]
-            w = w // OSPLIT[ci]
-            return m0 + k * w, w
-
-        def output(ci, k, shared):
-            m0, w = piece(ci, k)
-            y = held("x_raw%d0%d" % (ci, k), [P, PACK, w], F32)
-            y_f32[ci, k] = y
+            if ci not in y_f32:
+                y_f32[ci] = held("x_raw%d0" % ci, [P, PACK, w], F32)
+            y = y_f32[ci]
             step = 512 if w == 512 else 128
-            for t in range(PACK):
-                acc = next_bank()
-                for a in range(2):
-                    for n0 in range(0, w, step):
-                        nc.tensor.matmul_mx(
-                            out=acc[:, n0 : n0 + step],
-                            lhsT=w4_w_dealt[:, a, 2 * P * t : 2 * P * (t + 1)].bitcast(FP4X4),
-                            lhsT_scale=w4_s_dealt[:, a, P * t : P * (t + 1)],
-                            rhs=x_w[ci, a][:, k * w + n0 : k * w + n0 + step].bitcast(FP8X4),
-                            rhs_scale=x_s[ci, a][:, k * w + n0 : k * w + n0 + step],
-                            start=(a == 0 and n0 == 0),
-                            stop=False,
-                        )
-                for jg in range(2):
+            acc = next_bank()
+            for a in range(2):
+                for n0 in range(0, w, step):
                     nc.tensor.matmul_mx(
-                        out=acc[:, :w],
-                        lhsT=wd_w[t][:, P * jg : P * (jg + 1)].bitcast(FP8X4),
-                        lhsT_scale=wd_s[t][:, P * jg : P * (jg + 1)],
-                        rhs=h_w[ci, jg, k][:].bitcast(FP8X4),
-                        rhs_scale=h_s[ci, jg, k][:],
-                        start=False,
-                        stop=(jg == 1),
+                        out=acc[:, n0 : n0 + step],
+                        lhsT=w4_w_dealt[:, a, 2 * P * t : 2 * P * (t + 1)].bitcast(FP4X4),
+                        lhsT_scale=w4_s_dealt[:, a, P * t : P * (t + 1)],
+                        rhs=x_q[ci, a][0][:, n0 : n0 + step].bitcast(FP8X4),
+                        rhs_scale=x_q[ci, a][1][:, n0 : n0 + step],
+                        start=(a == 0 and n0 == 0),
+                        stop=False,
                     )
-                if shared and t % 2 == 1:
-                    nc.vector.tensor_scalar_add(out=y[:, t, :], in0=acc[:, :w], scalar1=c_sb[:, t : t + 1])
-                else:
-                    nc.scalar.activation(out=y[:, t, :], in_=acc[:, :w], func=ACT.Identity, bias=c_sb[:, t : t + 1])
-                if t % 2 == 1:
-                    nc.sync.dma_start(out=y_rows[:, t - 1 : t + 1, m0 : m0 + w], in_=y[:, t - 1 : t + 1, :])
+            for jg in range(2):
+                nc.tensor.matmul_mx(
+                    out=acc[:, :w],
+                    lhsT=wd_q[t][jg][0].bitcast(FP8X4),
+                    lhsT_scale=wd_q[t][jg][1],
+                    rhs=h_q[ci, jg][0].bitcast(FP8X4),
+                    rhs_scale=h_q[ci, jg][1],
+                    start=False,
+                    stop=(jg == 1),
+                )
+            nc.scalar.activation(out=y[:, t, :], in_=acc[:, :w], func=ACT.Identity, bias=c_sb[:, t : t + 1])
+            if t % 2 == 1:
+                nc.sync.dma_start(out=y_rows[:, t - 1 : t + 1, m0 : m0 + w], in_=y[:, t - 1 : t + 1, :])
 
-        def cast_y(ci, k, cast_on_vector):
-            m0, w = piece(ci, k)
-            y = y_f32[ci, k]
-            bf = next_stage([P, w, PACK])
-            y_bf[ci, k] = bf
-            if cast_on_vector:
-                nc.vector.tensor_copy(out=woven(bf[:]), in_=planes(y[:]))
-            else:
-                nc.scalar.activation(out=woven(bf[:]), in_=planes(y[:]), func=ACT.Copy)
+        def cast_y(ci, engine, tag=None):
+            bf = held(tag or "y_bf%d" % ci, [P, CHUNKS[ci][1], PACK], BF16)
+            weave(engine, bf[:], y_f32[ci][:])
+            y_bf[ci] = bf
 
-        def quantize_y(ci, k):
-            m0, w = piece(ci, k)
-            bf = y_bf[ci, k]
-            words = held("y_w%d%d" % (ci, k), [P, w], U32)
-            nc.vector.quantize_mx(out=words[:].bitcast(FP8X4), scales=y_s[:, m0 : m0 + w], in_=bf[:].rearrange("p m t -> p (m t)"))
+        def quantize_y(ci):
+            m0, w = CHUNKS[ci]
+            words = held("y_w%d" % ci, [P, w], U32)
+            nc.vector.quantize_mx(
+                out=words[:].bitcast(FP8X4), scales=y_s[:, m0 : m0 + w], in_=y_bf[ci][:].rearrange("p m t -> p (m t)")
+            )
             nc.sync.dma_start(out=y_words[:, 4 * m0 : 4 * (m0 + w)].bitcast(I32), in_=words[:].bitcast(I32))
 
-        gather_table(0, 0)
-        cast_x(1, 1, 0, True)
-        cast_x(0, 0, 0, False)
-        cast_x(0, 1, 0, False)
-        quantize_x(0, 0)
-        quantize_x(1, 1)
-        quantize_x(0, 1)
-        gather_table(1, 0)
-        hidden(0, 0, False)
-        gather_table(1, 1)
-        cast_x(1, 0, 0, True)
-        cube(0, 0, 0)
-        gather_table(0, 1)
-        hidden(0, 1, False)
-        gather_down(1)
-        quantize_x(1, 0)
-        quantize_h(0, 0, 0)
-        cube(0, 1, 0)
+        def store_scales():
+            for q in range(4):
+                queue = nc.scalar if q < 2 else nc.sync
+                queue.dma_start(
+                    out=out_2[0, 4 * q : 4 * q + 4, :].bitcast(I32),
+                    in_=y_s[32 * q : 32 * q + 4, :].bitcast(I32),
+                )
+
+        load_table(0)
+        load_x(0, 0)
+        load_x(0, 1)
+        load_table(1)
+        load_x(1, 0)
+        load_x(1, 1)
+        load_down(0)
+        load_down(1)
+        load_x(2, 0)
+        load_x(2, 1)
+        load_bypass_words()
+        load_bypass_scales()
+        load_down(2)
+        load_down(3)
+
+        gather_scales()
+        gather_table(0, (0, 1))
+        cast_x(0, (0, 1), nc.scalar)
+        quantize_x(0, (0, 1))
+        gather_table(1, (0,))
+        hidden(0, 0, "a")
+        gather_table(1, (1,))
+        hidden(0, 1, "b")
+        cast_x(1, (0,), nc.vector)
+        cast_x(1, (1,), nc.vector)
+        quantize_x(1, (0,))
+        quantize_x(1, (1,))
+        hidden(1, 0, "c")
+        cube(0, 0)
         gather_down(0)
+        quantize_h(0, 0)
+        cube(0, 1)
+        gather_down(1)
+        quantize_h(0, 1)
+        cast_x(2, (0, 1), nc.scalar)
+        turn_down(0, (0, 1))
+        turn_down(1, (0, 1))
+        hidden(1, 1, "d")
+        cube(1, 0)
+        quantize_x(2, (0, 1))
+        quantize_h(1, 0)
+        hidden(2, 0, "a")
         gather_down(2)
-        turn_down(0)
-        deal_w4()
-        turn_down(1)
-        quantize_h(0, 1, 0)
+        quantize_down((0, 1))
+        deal_bypass_words()
+        deal_bypass_scales()
+        turn_down(2, (2,))
+        cube(1, 1)
+        output(0, 0)
+        output(0, 1)
         gather_down(3)
-        cast_x(2, 1, 0, False)
-        hidden(1, 0, False)
-        quantize_down(1)
-        hidden(1, 1, False)
-        turn_down(2)
-        quantize_x(2, 1)
-        quantize_down(0)
-        cast_x(2, 0, 0, True)
-        turn_down(3)
-        quantize_down(3)
-        quantize_x(2, 0)
-        cube(1, 1, 0)
-        cube(1, 0, 0)
-        quantize_down(2)
-        hidden(2, 1, False)
-        output(0, 0, False)
-        quantize_h(1, 1, 0)
-        hidden(2, 0, False)
-        quantize_h(1, 0, 0)
-        cube(2, 1, 0)
-        cast_y(0, 0, True)
-        output(1, 0, False)
-        cube(2, 0, 0)
-        cast_y(1, 0, True)
-        quantize_h(2, 0, 0)
-        quantize_h(2, 1, 0)
-        quantize_y(1, 0)
-        output(2, 0, False)
-        quantize_y(0, 0)
-        cast_y(2, 0, True)
-        quantize_y(2, 0)
-        for q in range(4):
-            nc.scalar.dma_start(
-                out=out_2[0, 4 * q : 4 * q + 4, :].bitcast(I32),
-                in_=y_s[32 * q : 32 * q + 4, :].bitcast(I32),
-            )
+        quantize_h(1, 1)
+        quantize_down((2,))
+        hidden(2, 1, "b")
+        turn_down(3, (3,))
+        output(1, 0)
+        output(1, 1)
+        cube(2, 0)
+        quantize_down((3,))
+        output(0, 2)
+        output(1, 2)
+        quantize_h(2, 0)
+        output(0, 3)
+        output(1, 3)
+        cube(2, 1)
+        cast_y(0, nc.scalar, "x_bf00")
+        quantize_h(2, 1)
+        for t in range(PACK):
+            output(2, t)
+        quantize_y(0)
+        cast_y(1, nc.vector, "x_bf10")
+        quantize_y(1)
+        cast_y(2, nc.vector, "x_bf20")
+        quantize_y(2)
+        store_scales()

@@ -21,7 +21,7 @@ P = 128
 PACK = 4
 PASS = P * PACK
 GAP = 32
-BANKS = 5
+RING = 4
 CHUNKS = ((0, 256), (256, 512), (768, 256))
 
 
@@ -40,9 +40,12 @@ def tile_list_cube_parser_layer_kernel(tc, x, tab_words, tab_scales, offs, b, g,
         psum = ctx.enter_context(tc.psum_pool(name="psum", bufs=1))
         taken = []
 
+        def bank(number):
+            return psum.tile([P, 512], F32, name="bank%d" % number)
+
         def next_bank():
-            taken.append(len(taken) % BANKS)
-            return psum.tile([P, 512], F32, name="bank%d" % taken[-1])
+            taken.append(len(taken) % RING)
+            return bank(taken[-1])
 
         def held(name, shape, dtype):
             return keep.tile(shape, dtype, name=name, align_bytes=64)
@@ -154,9 +157,9 @@ def tile_list_cube_parser_layer_kernel(tc, x, tab_words, tab_scales, offs, b, g,
 
         factors, h_bf, h_q = {}, {}, {}
 
-        def hidden(ci, jg, tag):
+        def hidden(ci, jg, tag, sq_tag=None):
             w = CHUNKS[ci][1]
-            sq = held("sq" + tag, [P, PACK, w], F32)
+            sq = held(sq_tag or "sq" + tag, [P, PACK, w], F32)
             lin = held("lin" + tag, [P, PACK, w], F32)
             for t in range(PACK):
                 pre = next_bank()
@@ -235,7 +238,7 @@ def tile_list_cube_parser_layer_kernel(tc, x, tab_words, tab_scales, offs, b, g,
                 y_f32[ci] = held("x_raw%d0" % ci, [P, PACK, w], F32)
             y = y_f32[ci]
             step = 512 if w == 512 else 128
-            acc = next_bank()
+            acc = next_bank() if ci == len(CHUNKS) - 1 else bank(RING + t)
             for a in range(2):
                 for n0 in range(0, w, step):
                     nc.tensor.matmul_mx(
@@ -323,31 +326,29 @@ def tile_list_cube_parser_layer_kernel(tc, x, tab_words, tab_scales, offs, b, g,
         cube(1, 0)
         quantize_x(2, (0, 1))
         quantize_h(1, 0)
-        hidden(2, 0, "a")
-        gather_down(2)
         quantize_down((0, 1))
         deal_bypass_words()
         deal_bypass_scales()
-        turn_down(2, (2,))
-        cube(1, 1)
         output(0, 0)
         output(0, 1)
+        gather_down(2)
+        hidden(2, 0, "a")
+        turn_down(2, (2,))
         gather_down(3)
-        quantize_h(1, 1)
         quantize_down((2,))
-        hidden(2, 1, "b")
-        turn_down(3, (3,))
-        output(1, 0)
-        output(1, 1)
-        cube(2, 0)
-        quantize_down((3,))
+        cube(1, 1)
         output(0, 2)
-        output(1, 2)
-        quantize_h(2, 0)
+        turn_down(3, (3,))
+        quantize_h(1, 1)
+        hidden(2, 1, "b")
+        quantize_down((3,))
         output(0, 3)
-        output(1, 3)
+        cube(2, 0)
+        for t in range(PACK):
+            output(1, t)
+        quantize_h(2, 0)
         cube(2, 1)
-        cast_y(0, nc.scalar, "x_bf00")
+        cast_y(0, nc.vector, "x_bf00")
         quantize_h(2, 1)
         for t in range(PACK):
             output(2, t)

@@ -232,13 +232,13 @@ def tile_list_cube_parser_layer_kernel(tc, x, tab_words, tab_scales, offs, b, g,
         y_words = out_1[0].rearrange("p m t -> p (m t)")
         y_f32, y_bf = {}, {}
 
-        def output(ci, t):
-            m0, w = CHUNKS[ci]
-            if ci not in y_f32:
-                y_f32[ci] = held("x_raw%d0" % ci, [P, PACK, w], F32)
-            y = y_f32[ci]
+        sums = {}
+
+        def bypass(ci, t):
+            w = CHUNKS[ci][1]
             step = 512 if w == 512 else 128
             acc = next_bank() if ci == len(CHUNKS) - 1 else bank(RING + t)
+            sums[ci, t] = acc
             for a in range(2):
                 for n0 in range(0, w, step):
                     nc.tensor.matmul_mx(
@@ -250,19 +250,35 @@ def tile_list_cube_parser_layer_kernel(tc, x, tab_words, tab_scales, offs, b, g,
                         start=(a == 0 and n0 == 0),
                         stop=False,
                     )
-            for jg in range(2):
-                nc.tensor.matmul_mx(
-                    out=acc[:, :w],
-                    lhsT=wd_q[t][jg][0].bitcast(FP8X4),
-                    lhsT_scale=wd_q[t][jg][1],
-                    rhs=h_q[ci, jg][0].bitcast(FP8X4),
-                    rhs_scale=h_q[ci, jg][1],
-                    start=False,
-                    stop=(jg == 1),
-                )
-            nc.scalar.activation(out=y[:, t, :], in_=acc[:, :w], func=ACT.Identity, bias=c_sb[:, t : t + 1])
+
+        def down(ci, t, jg):
+            nc.tensor.matmul_mx(
+                out=sums[ci, t][:, : CHUNKS[ci][1]],
+                lhsT=wd_q[t][jg][0].bitcast(FP8X4),
+                lhsT_scale=wd_q[t][jg][1],
+                rhs=h_q[ci, jg][0].bitcast(FP8X4),
+                rhs_scale=h_q[ci, jg][1],
+                start=False,
+                stop=(jg == 1),
+            )
+
+        def finish(ci, t, on_vector=False):
+            m0, w = CHUNKS[ci]
+            if ci not in y_f32:
+                y_f32[ci] = held("x_raw%d0" % ci, [P, PACK, w], F32)
+            y = y_f32[ci]
+            down(ci, t, 1)
+            if on_vector:
+                nc.vector.tensor_scalar_add(out=y[:, t, :], in0=sums[ci, t][:, :w], scalar1=c_sb[:, t : t + 1])
+            else:
+                nc.scalar.activation(out=y[:, t, :], in_=sums[ci, t][:, :w], func=ACT.Identity, bias=c_sb[:, t : t + 1])
             if t % 2 == 1:
                 nc.sync.dma_start(out=y_rows[:, t - 1 : t + 1, m0 : m0 + w], in_=y[:, t - 1 : t + 1, :])
+
+        def output(ci, t):
+            bypass(ci, t)
+            down(ci, t, 0)
+            finish(ci, t)
 
         def cast_y(ci, engine, tag=None):
             bf = held(tag or "y_bf%d" % ci, [P, CHUNKS[ci][1], PACK], BF16)
@@ -331,27 +347,37 @@ def tile_list_cube_parser_layer_kernel(tc, x, tab_words, tab_scales, offs, b, g,
         deal_bypass_scales()
         output(0, 0)
         output(0, 1)
+        for t in range(2):
+            bypass(1, t)
+            down(1, t, 0)
         gather_down(2)
         hidden(2, 0, "a")
         turn_down(2, (2,))
         gather_down(3)
         quantize_down((2,))
-        cube(1, 1)
+        cube(1, 1, "wd_raw3")
         output(0, 2)
+        bypass(1, 2)
+        down(1, 2, 0)
         turn_down(3, (3,))
         quantize_h(1, 1)
         hidden(2, 1, "b")
         quantize_down((3,))
         output(0, 3)
-        cube(2, 0)
+        bypass(1, 3)
+        down(1, 3, 0)
+        cube(2, 0, "wd_bf3")
         for t in range(PACK):
-            output(1, t)
+            finish(1, t)
         quantize_h(2, 0)
         cube(2, 1)
         cast_y(0, nc.vector, "x_bf00")
+        for t in range(PACK):
+            bypass(2, t)
+            down(2, t, 0)
         quantize_h(2, 1)
         for t in range(PACK):
-            output(2, t)
+            finish(2, t)
         quantize_y(0)
         cast_y(1, nc.vector, "x_bf10")
         quantize_y(1)

@@ -55,8 +55,8 @@ def tile_list_cube_parser_layer_kernel(tc, x, tab_words, tab_scales, offs, b, g,
 
         b_sb = held("b_sb", [P, 2, PACK], F32)
         g_sb = held("g_sb", [P, 2, PACK], F32)
-        nc.sync.dma_start(out=b_sb[:], in_=b.rearrange("(g p t) -> p g t", g=2, t=PACK))
-        nc.sync.dma_start(out=g_sb[:], in_=g.rearrange("(g p t) -> p g t", g=2, t=PACK))
+        w4_w = held("w4_w", [P, 2, 2 * N], U8)
+        nc.sync.dma_start(out=w4_w[:].bitcast(I32), in_=w4_words.rearrange("a p e -> p a e").bitcast(I32))
 
         tab_s = held("tab_s", [P, T], U8)
         nc.gpsimd.memset(tab_s[:].bitcast(I32), 0)
@@ -71,9 +71,7 @@ def tile_list_cube_parser_layer_kernel(tc, x, tab_words, tab_scales, offs, b, g,
         make_identity(nc, ident[:])
 
         gb_sb = held("gb_sb", [P, 2, PACK], F32)
-        nc.gpsimd.tensor_mul(out=gb_sb[:], in0=g_sb[:], in1=b_sb[:])
         c_sb = held("c_sb", [P, PACK], F32)
-        w4_w = held("w4_w", [P, 2, 2 * N], U8)
         x_raw, wd_raw, tab_w = {}, {}, {}
 
         def load_x(ci, a):
@@ -92,8 +90,10 @@ def tile_list_cube_parser_layer_kernel(tc, x, tab_words, tab_scales, offs, b, g,
             nc.sync.dma_start(out=words[:].bitcast(I32), in_=tab_words[a].rearrange("p e i -> p (e i)").bitcast(I32))
             tab_w[a] = words
 
-        def load_bypass_words():
-            nc.sync.dma_start(out=w4_w[:].bitcast(I32), in_=w4_words.rearrange("a p e -> p a e").bitcast(I32))
+        def load_gains():
+            nc.sync.dma_start(out=b_sb[:], in_=b.rearrange("(g p t) -> p g t", g=2, t=PACK))
+            nc.sync.dma_start(out=g_sb[:], in_=g.rearrange("(g p t) -> p g t", g=2, t=PACK))
+            nc.gpsimd.tensor_mul(out=gb_sb[:], in0=g_sb[:], in1=b_sb[:])
 
         def load_bypass_scales():
             for q in range(4):
@@ -101,6 +101,8 @@ def tile_list_cube_parser_layer_kernel(tc, x, tab_words, tab_scales, offs, b, g,
                     out=w4_s[32 * q : 32 * q + 4, :, :].bitcast(I32),
                     in_=w4_scales[:, 4 * q : 4 * q + 4, :].rearrange("a r n -> r a n").bitcast(I32),
                 )
+
+        def load_bias():
             nc.sync.dma_start(out=c_sb[:], in_=c.rearrange("(p t) -> p t", t=PACK))
 
         v_s = held("v_s", [P, S], U8)
@@ -234,51 +236,45 @@ def tile_list_cube_parser_layer_kernel(tc, x, tab_words, tab_scales, offs, b, g,
 
         sums = {}
 
-        def bypass(ci, t):
+        def bypass(ci, slices, acc):
             w = CHUNKS[ci][1]
             step = 512 if w == 512 else 128
-            acc = next_bank() if ci == len(CHUNKS) - 1 else bank(RING + t)
-            sums[ci, t] = acc
-            for a in range(2):
-                for n0 in range(0, w, step):
-                    nc.tensor.matmul_mx(
-                        out=acc[:, n0 : n0 + step],
-                        lhsT=w4_w_dealt[:, a, 2 * P * t : 2 * P * (t + 1)].bitcast(FP4X4),
-                        lhsT_scale=w4_s_dealt[:, a, P * t : P * (t + 1)],
-                        rhs=x_q[ci, a][0][:, n0 : n0 + step].bitcast(FP8X4),
-                        rhs_scale=x_q[ci, a][1][:, n0 : n0 + step],
-                        start=(a == 0 and n0 == 0),
-                        stop=False,
-                    )
+            for o, t in enumerate(slices):
+                sums[ci, t] = acc[:, o * w : (o + 1) * w]
+                for a in range(2):
+                    for n0 in range(0, w, step):
+                        nc.tensor.matmul_mx(
+                            out=sums[ci, t][:, n0 : n0 + step],
+                            lhsT=w4_w_dealt[:, a, 2 * P * t : 2 * P * (t + 1)].bitcast(FP4X4),
+                            lhsT_scale=w4_s_dealt[:, a, P * t : P * (t + 1)],
+                            rhs=x_q[ci, a][0][:, n0 : n0 + step].bitcast(FP8X4),
+                            rhs_scale=x_q[ci, a][1][:, n0 : n0 + step],
+                            start=(o == 0 and a == 0 and n0 == 0),
+                            stop=False,
+                        )
 
-        def down(ci, t, jg):
-            nc.tensor.matmul_mx(
-                out=sums[ci, t][:, : CHUNKS[ci][1]],
-                lhsT=wd_q[t][jg][0].bitcast(FP8X4),
-                lhsT_scale=wd_q[t][jg][1],
-                rhs=h_q[ci, jg][0].bitcast(FP8X4),
-                rhs_scale=h_q[ci, jg][1],
-                start=False,
-                stop=(jg == 1),
-            )
+        def down(ci, slices, jg):
+            for t in slices:
+                nc.tensor.matmul_mx(
+                    out=sums[ci, t],
+                    lhsT=wd_q[t][jg][0].bitcast(FP8X4),
+                    lhsT_scale=wd_q[t][jg][1],
+                    rhs=h_q[ci, jg][0].bitcast(FP8X4),
+                    rhs_scale=h_q[ci, jg][1],
+                    start=False,
+                    stop=(jg == 1 and t == slices[-1]),
+                )
 
-        def finish(ci, t, on_vector=False):
+        def finish(ci, slices):
             m0, w = CHUNKS[ci]
             if ci not in y_f32:
                 y_f32[ci] = held("x_raw%d0" % ci, [P, PACK, w], F32)
             y = y_f32[ci]
-            down(ci, t, 1)
-            if on_vector:
-                nc.vector.tensor_scalar_add(out=y[:, t, :], in0=sums[ci, t][:, :w], scalar1=c_sb[:, t : t + 1])
-            else:
-                nc.scalar.activation(out=y[:, t, :], in_=sums[ci, t][:, :w], func=ACT.Identity, bias=c_sb[:, t : t + 1])
-            if t % 2 == 1:
-                nc.sync.dma_start(out=y_rows[:, t - 1 : t + 1, m0 : m0 + w], in_=y[:, t - 1 : t + 1, :])
-
-        def output(ci, t):
-            bypass(ci, t)
-            down(ci, t, 0)
-            finish(ci, t)
+            down(ci, slices, 1)
+            for t in slices:
+                nc.scalar.activation(out=y[:, t, :], in_=sums[ci, t], func=ACT.Identity, bias=c_sb[:, t : t + 1])
+                if t % 2 == 1:
+                    nc.sync.dma_start(out=y_rows[:, t - 1 : t + 1, m0 : m0 + w], in_=y[:, t - 1 : t + 1, :])
 
         def cast_y(ci, engine, tag=None):
             bf = held(tag or "y_bf%d" % ci, [P, CHUNKS[ci][1], PACK], BF16)
@@ -303,6 +299,7 @@ def tile_list_cube_parser_layer_kernel(tc, x, tab_words, tab_scales, offs, b, g,
 
         load_table(0)
         load_x(0, 0)
+        load_gains()
         load_x(0, 1)
         load_table(1)
         load_x(1, 0)
@@ -311,11 +308,12 @@ def tile_list_cube_parser_layer_kernel(tc, x, tab_words, tab_scales, offs, b, g,
         load_down(1)
         load_x(2, 0)
         load_x(2, 1)
-        load_bypass_words()
         load_bypass_scales()
+        load_bias()
         load_down(2)
         load_down(3)
 
+        deal_bypass_words()
         gather_scales()
         gather_table(0, (0, 1))
         cast_x(0, (0, 1), nc.scalar)
@@ -343,41 +341,48 @@ def tile_list_cube_parser_layer_kernel(tc, x, tab_words, tab_scales, offs, b, g,
         quantize_x(2, (0, 1))
         quantize_h(1, 0)
         quantize_down((0, 1))
-        deal_bypass_words()
         deal_bypass_scales()
-        output(0, 0)
-        output(0, 1)
+        bypass(0, (0,), bank(RING + 0))
+        down(0, (0,), 0)
+        finish(0, (0,))
+        bypass(0, (1,), bank(RING + 1))
+        down(0, (1,), 0)
+        finish(0, (1,))
         for t in range(2):
-            bypass(1, t)
-            down(1, t, 0)
+            bypass(1, (t,), bank(RING + t))
+            down(1, (t,), 0)
         gather_down(2)
         hidden(2, 0, "a")
         turn_down(2, (2,))
         gather_down(3)
         quantize_down((2,))
         cube(1, 1, "wd_raw3")
-        output(0, 2)
-        bypass(1, 2)
-        down(1, 2, 0)
+        bypass(0, (2,), bank(RING + 2))
+        down(0, (2,), 0)
+        finish(0, (2,))
+        bypass(1, (2,), bank(RING + 2))
+        down(1, (2,), 0)
         turn_down(3, (3,))
         quantize_h(1, 1)
         hidden(2, 1, "b")
         quantize_down((3,))
-        output(0, 3)
-        bypass(1, 3)
-        down(1, 3, 0)
+        bypass(0, (3,), bank(RING + 3))
+        down(0, (3,), 0)
+        finish(0, (3,))
+        bypass(1, (3,), bank(RING + 3))
+        down(1, (3,), 0)
         cube(2, 0, "wd_bf3")
         for t in range(PACK):
-            finish(1, t)
+            finish(1, (t,))
         quantize_h(2, 0)
         cube(2, 1)
         cast_y(0, nc.vector, "x_bf00")
         for t in range(PACK):
-            bypass(2, t)
-            down(2, t, 0)
+            bypass(2, (t,), next_bank())
+            down(2, (t,), 0)
         quantize_h(2, 1)
         for t in range(PACK):
-            finish(2, t)
+            finish(2, (t,))
         quantize_y(0)
         cast_y(1, nc.vector, "x_bf10")
         quantize_y(1)

@@ -22,7 +22,9 @@ PACK = 4
 PASS = P * PACK
 GAP = 32
 RING = 4
-CHUNKS = ((0, 256), (256, 512), (768, 256))
+QUARTER = 256
+UNITS = ((0, (0,)), (1, (0, 1)), (0, (1, 2)), (1, (2, 3)), (0, (3,)))
+Y_CHUNKS = ((0, 1), (2,), (3,))
 
 
 def woven(tile_ap):
@@ -74,11 +76,11 @@ def tile_list_cube_parser_layer_kernel(tc, x, tab_words, tab_scales, offs, b, g,
         c_sb = held("c_sb", [P, PACK], F32)
         x_raw, wd_raw, tab_w = {}, {}, {}
 
-        def load_x(ci, a):
-            m0, w = CHUNKS[ci]
-            raw = held("x_raw%d%d" % (ci, a), [P, PACK, w], F32)
-            nc.sync.dma_start(out=raw[:], in_=x[PASS * a : PASS * (a + 1), m0 : m0 + w].rearrange("(p i) m -> p i m", i=PACK))
-            x_raw[ci, a] = raw
+        def load_x(q, a):
+            m0 = QUARTER * q
+            raw = held("x_raw%d%d" % (q, a), [P, PACK, QUARTER], F32)
+            nc.sync.dma_start(out=raw[:], in_=x[PASS * a : PASS * (a + 1), m0 : m0 + QUARTER].rearrange("(p i) m -> p i m", i=PACK))
+            x_raw[q, a] = raw
 
         def load_down(t):
             raw = held("wd_raw%d" % t, [P, T], F32)
@@ -93,7 +95,9 @@ def tile_list_cube_parser_layer_kernel(tc, x, tab_words, tab_scales, offs, b, g,
         def load_gains():
             nc.sync.dma_start(out=b_sb[:], in_=b.rearrange("(g p t) -> p g t", g=2, t=PACK))
             nc.sync.dma_start(out=g_sb[:], in_=g.rearrange("(g p t) -> p g t", g=2, t=PACK))
-            nc.gpsimd.tensor_mul(out=gb_sb[:], in0=g_sb[:], in1=b_sb[:])
+            for jg in range(2):
+                for t in range(PACK):
+                    nc.scalar.activation(out=gb_sb[:, jg, t : t + 1], in_=b_sb[:, jg, t : t + 1], func=ACT.Copy, scale=g_sb[:, jg, t : t + 1])
 
         def load_bypass_scales():
             for q in range(4):
@@ -144,52 +148,82 @@ def tile_list_cube_parser_layer_kernel(tc, x, tab_words, tab_scales, offs, b, g,
             )
             return [(words[:, o, :], scales[:, o, :]) for o in range(count)]
 
+        def runs(store, quarters, key):
+            found = []
+            for o, q in enumerate(quarters):
+                words, scales, row, col = store[q, key]
+                if found and found[-1][0] is words and found[-1][2] == row and found[-1][3] + found[-1][4] == col:
+                    found[-1][4] = found[-1][4] + QUARTER
+                else:
+                    found.append([words, scales, row, col, QUARTER, QUARTER * o])
+            return [(w[:, r, c0 : c0 + n], s[:, r, c0 : c0 + n], n, at) for w, s, r, c0, n, at in found]
+
         x_bf, x_q = {}, {}
+        x_head_w = [held("x_head_w%d" % a, [P, 1, 2 * QUARTER], U32) for a in range(2)]
+        x_head_s = [held("x_head_s%d" % a, [P, 1, 2 * QUARTER], U8) for a in range(2)]
 
-        def cast_x(ci, passes, engine, tag=None):
-            w = CHUNKS[ci][1]
-            bf = held(tag or "x_bf%d%d" % (ci, passes[0]), [P, len(passes), w, PACK], BF16)
+        def cast_x(q, passes, engine):
+            bf = held("x_bf%d%d" % (q, passes[0]), [P, len(passes), QUARTER, PACK], BF16)
             for o, a in enumerate(passes):
-                weave(engine, bf[:, o], x_raw[ci, a][:])
-            x_bf[ci, passes] = bf
+                weave(engine, bf[:, o], x_raw[q, a][:])
+            x_bf[q, passes] = bf
 
-        def quantize_x(ci, passes, tags=None):
-            for a, made in zip(passes, quantize("x%d%d" % (ci, passes[0]), x_bf[ci, passes], tags)):
-                x_q[ci, a] = made
+        def quantize_into(words, scales, bf):
+            nc.vector.quantize_mx(out=words.bitcast(FP8X4), scales=scales, in_=bf[:].rearrange("p o m t -> p (o m t)"))
+
+        def quantize_x_head(q, a):
+            cols = slice(QUARTER * q, QUARTER * (q + 1))
+            quantize_into(x_head_w[a][:, 0, cols], x_head_s[a][:, 0, cols], x_bf[q, (a,)])
+            x_q[q, a] = x_head_w[a], x_head_s[a], 0, QUARTER * q
+
+        def quantize_x(q, tag=None):
+            words = held(tag or "x_w%d" % q, [P, 2, QUARTER], U32)
+            scales = held("x_s%d" % q, [P, 2, QUARTER], U8)
+            quantize_into(words[:].rearrange("p o m -> p (o m)"), scales[:].rearrange("p o m -> p (o m)"), x_bf[q, (0, 1)])
+            for a in range(2):
+                x_q[q, a] = words, scales, a, 0
 
         factors, h_bf, h_q = {}, {}, {}
 
-        def hidden(ci, jg, tag, sq_tag=None):
-            w = CHUNKS[ci][1]
-            sq = held(sq_tag or "sq" + tag, [P, PACK, w], F32)
-            lin = held("lin" + tag, [P, PACK, w], F32)
+        def hidden(u, tag):
+            jg, quarters = UNITS[u]
+            w = QUARTER * len(quarters)
+            both = held(tag, [P, 2, PACK, w], F32)
+            sq, lin = both[:, 0], both[:, 1]
+            passes = [(a, run) for a in range(2) for run in reversed(runs(x_q, quarters, a))]
             for t in range(PACK):
                 pre = next_bank()
-                for a in range(2):
+                for o, (a, (words, scales, n, at)) in enumerate(passes):
                     nc.tensor.matmul_mx(
-                        out=pre[:, :w],
+                        out=pre[:, at : at + n],
                         lhsT=v_w[a, jg][:, P * t : P * (t + 1)].bitcast(FP8X4),
                         lhsT_scale=v_s[4 * a : P, PASS * jg + P * t : PASS * jg + P * (t + 1)],
-                        rhs=x_q[ci, a][0].bitcast(FP8X4),
-                        rhs_scale=x_q[ci, a][1],
-                        start=(a == 0),
-                        stop=(a == 1),
+                        rhs=words.bitcast(FP8X4),
+                        rhs_scale=scales,
+                        start=(o == 0),
+                        stop=(o == len(passes) - 1),
                     )
                 nc.scalar.activation(out=sq[:, t, :], in_=pre[:, :w], func=ACT.Square, bias=b_sb[:, jg, t : t + 1])
                 nc.scalar.activation(
                     out=lin[:, t, :], in_=pre[:, :w], func=ACT.Identity,
                     bias=gb_sb[:, jg, t : t + 1], scale=g_sb[:, jg, t : t + 1],
                 )
-            factors[ci, jg] = sq, lin
+            factors[u] = sq, lin
 
-        def cube(ci, jg, tag=None):
-            sq, lin = factors[ci, jg]
-            bf = held(tag or "h_bf%d%d" % (ci, jg), [P, 1, CHUNKS[ci][1], PACK], BF16)
-            nc.vector.tensor_tensor(out=woven(bf[:, 0]), in0=planes(sq[:]), in1=planes(lin[:]), op=ALU.mult)
-            h_bf[ci, jg] = bf
+        def cube(u, tag=None):
+            sq, lin = factors[u]
+            bf = held(tag or "h_bf%d" % u, [P, 1, QUARTER * len(UNITS[u][1]), PACK], BF16)
+            nc.vector.tensor_tensor(out=woven(bf[:, 0]), in0=planes(sq), in1=planes(lin), op=ALU.mult)
+            h_bf[u] = bf
 
-        def quantize_h(ci, jg, tags=None):
-            h_q[ci, jg] = quantize("h%d%d" % (ci, jg), h_bf[ci, jg], tags)[0]
+        def quantize_h(u):
+            jg, quarters = UNITS[u]
+            w = QUARTER * len(quarters)
+            words = held("h_w%d" % u, [P, 1, w], U32)
+            scales = held("h_s%d" % u, [P, 1, w], U8)
+            quantize_into(words[:, 0, :], scales[:, 0, :], h_bf[u])
+            for o, q in enumerate(quarters):
+                h_q[q, jg] = words, scales, 0, QUARTER * o
 
         wd_picked, wd_bf, wd_q = {}, {}, {}
 
@@ -236,53 +270,56 @@ def tile_list_cube_parser_layer_kernel(tc, x, tab_words, tab_scales, offs, b, g,
 
         sums = {}
 
-        def bypass(ci, slices, acc):
-            w = CHUNKS[ci][1]
-            step = 512 if w == 512 else 128
-            for o, t in enumerate(slices):
-                sums[ci, t] = acc[:, o * w : (o + 1) * w]
-                for a in range(2):
-                    for n0 in range(0, w, step):
+        def bypass(ci, t, acc):
+            sums[ci, t] = acc
+            first = True
+            for a in range(2):
+                for words, scales, n, at in runs(x_q, Y_CHUNKS[ci], a):
+                    step = 512 if n == 512 else 128
+                    for n0 in range(0, n, step):
                         nc.tensor.matmul_mx(
-                            out=sums[ci, t][:, n0 : n0 + step],
+                            out=acc[:, at + n0 : at + n0 + step],
                             lhsT=w4_w_dealt[:, a, 2 * P * t : 2 * P * (t + 1)].bitcast(FP4X4),
                             lhsT_scale=w4_s_dealt[:, a, P * t : P * (t + 1)],
-                            rhs=x_q[ci, a][0][:, n0 : n0 + step].bitcast(FP8X4),
-                            rhs_scale=x_q[ci, a][1][:, n0 : n0 + step],
-                            start=(o == 0 and a == 0 and n0 == 0),
+                            rhs=words[:, n0 : n0 + step].bitcast(FP8X4),
+                            rhs_scale=scales[:, n0 : n0 + step],
+                            start=first,
                             stop=False,
                         )
+                        first = False
 
-        def down(ci, slices, jg):
-            for t in slices:
+        def down(ci, t, jg, last):
+            found = runs(h_q, Y_CHUNKS[ci], jg)
+            for o, (words, scales, n, at) in enumerate(found):
                 nc.tensor.matmul_mx(
-                    out=sums[ci, t],
+                    out=sums[ci, t][:, at : at + n],
                     lhsT=wd_q[t][jg][0].bitcast(FP8X4),
                     lhsT_scale=wd_q[t][jg][1],
-                    rhs=h_q[ci, jg][0].bitcast(FP8X4),
-                    rhs_scale=h_q[ci, jg][1],
+                    rhs=words.bitcast(FP8X4),
+                    rhs_scale=scales,
                     start=False,
-                    stop=(jg == 1 and t == slices[-1]),
+                    stop=(last and o == len(found) - 1),
                 )
 
-        def finish(ci, slices):
-            m0, w = CHUNKS[ci]
-            if ci not in y_f32:
-                y_f32[ci] = held("x_raw%d0" % ci, [P, PACK, w], F32)
-            y = y_f32[ci]
-            down(ci, slices, 1)
-            for t in slices:
-                nc.scalar.activation(out=y[:, t, :], in_=sums[ci, t], func=ACT.Identity, bias=c_sb[:, t : t + 1])
-                if t % 2 == 1:
-                    nc.sync.dma_start(out=y_rows[:, t - 1 : t + 1, m0 : m0 + w], in_=y[:, t - 1 : t + 1, :])
+        def y_columns(ci):
+            return QUARTER * Y_CHUNKS[ci][0], QUARTER * len(Y_CHUNKS[ci])
 
-        def cast_y(ci, engine, tag=None):
-            bf = held(tag or "y_bf%d" % ci, [P, CHUNKS[ci][1], PACK], BF16)
+        def empty(ci, t, tag):
+            m0, w = y_columns(ci)
+            if ci not in y_f32:
+                y_f32[ci] = held(tag, [P, PACK, w], F32)
+            y = y_f32[ci]
+            nc.scalar.activation(out=y[:, t, :], in_=sums[ci, t][:, :w], func=ACT.Identity, bias=c_sb[:, t : t + 1])
+            if t % 2 == 1:
+                nc.sync.dma_start(out=y_rows[:, t - 1 : t + 1, m0 : m0 + w], in_=y[:, t - 1 : t + 1, :])
+
+        def cast_y(ci, engine, tag):
+            bf = held(tag, [P, y_columns(ci)[1], PACK], BF16)
             weave(engine, bf[:], y_f32[ci][:])
             y_bf[ci] = bf
 
         def quantize_y(ci):
-            m0, w = CHUNKS[ci]
+            m0, w = y_columns(ci)
             words = held("y_w%d" % ci, [P, w], U32)
             nc.vector.quantize_mx(
                 out=words[:].bitcast(FP8X4), scales=y_s[:, m0 : m0 + w], in_=y_bf[ci][:].rearrange("p m t -> p (m t)")
@@ -304,88 +341,81 @@ def tile_list_cube_parser_layer_kernel(tc, x, tab_words, tab_scales, offs, b, g,
         load_table(1)
         load_x(1, 0)
         load_x(1, 1)
+        load_bypass_scales()
         load_down(0)
-        load_down(1)
         load_x(2, 0)
         load_x(2, 1)
-        load_bypass_scales()
-        load_bias()
+        load_down(1)
+        load_x(3, 0)
+        load_x(3, 1)
         load_down(2)
         load_down(3)
+        load_bias()
 
         deal_bypass_words()
         gather_scales()
         gather_table(0, (0, 1))
-        cast_x(0, (0, 1), nc.scalar)
-        quantize_x(0, (0, 1))
+        cast_x(0, (0,), nc.scalar)
+        cast_x(0, (1,), nc.scalar)
+        quantize_x_head(0, 0)
+        quantize_x_head(0, 1)
         gather_table(1, (0,))
-        hidden(0, 0, "a")
-        gather_table(1, (1,))
-        hidden(0, 1, "b")
-        cast_x(1, (0,), nc.vector)
+        cast_x(1, (0,), nc.scalar)
+        hidden(0, "x_raw10")
         cast_x(1, (1,), nc.vector)
-        quantize_x(1, (0,))
-        quantize_x(1, (1,))
-        hidden(1, 0, "c")
-        cube(0, 0)
-        gather_down(0)
-        quantize_h(0, 0)
-        cube(0, 1)
-        gather_down(1)
-        quantize_h(0, 1)
-        cast_x(2, (0, 1), nc.scalar)
-        turn_down(0, (0, 1))
-        turn_down(1, (0, 1))
-        hidden(1, 1, "d")
-        cube(1, 0)
-        quantize_x(2, (0, 1))
-        quantize_h(1, 0)
-        quantize_down((0, 1))
+        quantize_x_head(1, 0)
+        quantize_x_head(1, 1)
+        gather_table(1, (1,))
+        hidden(1, "factors_b")
         deal_bypass_scales()
-        bypass(0, (0,), bank(RING + 0))
-        down(0, (0,), 0)
-        finish(0, (0,))
-        bypass(0, (1,), bank(RING + 1))
-        down(0, (1,), 0)
-        finish(0, (1,))
-        for t in range(2):
-            bypass(1, (t,), bank(RING + t))
-            down(1, (t,), 0)
+        gather_down(0)
+        cast_x(2, (0, 1), nc.vector)
+        quantize_x(2)
+        hidden(2, "factors_c")
+        gather_down(1)
+        cube(0, "wd_raw1")
+        cast_x(3, (0, 1), nc.scalar)
         gather_down(2)
-        hidden(2, 0, "a")
-        turn_down(2, (2,))
+        quantize_h(0)
         gather_down(3)
-        quantize_down((2,))
-        cube(1, 1, "wd_raw3")
-        bypass(0, (2,), bank(RING + 2))
-        down(0, (2,), 0)
-        finish(0, (2,))
-        bypass(1, (2,), bank(RING + 2))
-        down(1, (2,), 0)
-        turn_down(3, (3,))
-        quantize_h(1, 1)
-        hidden(2, 1, "b")
-        quantize_down((3,))
-        bypass(0, (3,), bank(RING + 3))
-        down(0, (3,), 0)
-        finish(0, (3,))
-        bypass(1, (3,), bank(RING + 3))
-        down(1, (3,), 0)
-        cube(2, 0, "wd_bf3")
+        quantize_x(3, "wd_raw3")
         for t in range(PACK):
-            finish(1, (t,))
-        quantize_h(2, 0)
-        cube(2, 1)
-        cast_y(0, nc.vector, "x_bf00")
+            turn_down(t, (0, 1, 2, 3))
+        hidden(3, "factors_d")
+        cube(1, "x_bf30")
         for t in range(PACK):
-            bypass(2, (t,), next_bank())
-            down(2, (t,), 0)
-        quantize_h(2, 1)
+            bypass(0, t, bank(RING + t))
+        quantize_down((0, 1, 2, 3))
+        hidden(4, "x_raw10")
+        cube(2, "factors_b")
+        quantize_h(1)
         for t in range(PACK):
-            finish(2, (t,))
+            down(0, t, 1, False)
+        quantize_h(2)
+        cube(3, "x_bf30")
+        for t in range(PACK):
+            down(0, t, 0, True)
+        for t in range(PACK):
+            bypass(1, t, next_bank())
+            down(1, t, 0, False)
+        for t in range(PACK):
+            empty(0, t, "factors_c")
+        quantize_h(3)
+        cube(4, "x_bf30")
+        for t in range(PACK):
+            down(1, t, 1, True)
+            empty(1, t, "x_raw11")
+        for t in range(PACK):
+            bypass(2, t, bank(RING + t))
+            down(2, t, 1, False)
+        quantize_h(4)
+        cast_y(0, nc.vector, "x_bf30")
+        for t in range(PACK):
+            down(2, t, 0, True)
+            empty(2, t, "x_raw20")
         quantize_y(0)
-        cast_y(1, nc.vector, "x_bf10")
+        cast_y(1, nc.vector, "x_bf00")
         quantize_y(1)
-        cast_y(2, nc.vector, "x_bf20")
+        cast_y(2, nc.vector, "x_bf01")
         quantize_y(2)
         store_scales()

@@ -176,39 +176,44 @@ def tile_list_cube_parser_layer_kernel(tc, x, tab_words, tab_scales, offs, b, g,
             quantize_into(x_head_w[a][:, 0, cols], x_head_s[a][:, 0, cols], x_bf[q, (a,)])
             x_q[q, a] = x_head_w[a], x_head_s[a], 0, QUARTER * q
 
-        def quantize_x(q, tag=None):
-            words = held(tag or "x_w%d" % q, [P, 2, QUARTER], U32)
-            scales = held("x_s%d" % q, [P, 2, QUARTER], U8)
-            quantize_into(words[:].rearrange("p o m -> p (o m)"), scales[:].rearrange("p o m -> p (o m)"), x_bf[q, (0, 1)])
-            for a in range(2):
-                x_q[q, a] = words, scales, a, 0
+        def quantize_x(q, passes):
+            words = held("x_w%d%d" % (q, passes[0]), [P, len(passes), QUARTER], U32)
+            scales = held("x_s%d%d" % (q, passes[0]), [P, len(passes), QUARTER], U8)
+            quantize_into(words[:].rearrange("p o m -> p (o m)"), scales[:].rearrange("p o m -> p (o m)"), x_bf[q, passes])
+            for o, a in enumerate(passes):
+                x_q[q, a] = words, scales, o, 0
 
         factors, h_bf, h_q = {}, {}, {}
 
-        def hidden(u, tag):
+        def hidden(u, tag, places=None, part=range(PACK)):
             jg, quarters = UNITS[u]
             w = QUARTER * len(quarters)
-            both = held(tag, [P, 2, PACK, w], F32)
-            sq, lin = both[:, 0], both[:, 1]
+            if u not in factors:
+                both = held(tag, [P, 2, PACK, w], F32)
+                factors[u] = both[:, 0], both[:, 1]
+            sq, lin = factors[u]
             passes = [(a, run) for a in range(2) for run in reversed(runs(x_q, quarters, a))]
-            for t in range(PACK):
-                pre = next_bank()
-                for o, (a, (words, scales, n, at)) in enumerate(passes):
-                    nc.tensor.matmul_mx(
-                        out=pre[:, at : at + n],
-                        lhsT=v_w[a, jg][:, P * t : P * (t + 1)].bitcast(FP8X4),
-                        lhsT_scale=v_s[4 * a : P, PASS * jg + P * t : PASS * jg + P * (t + 1)],
-                        rhs=words.bitcast(FP8X4),
-                        rhs_scale=scales,
-                        start=(o == 0),
-                        stop=(o == len(passes) - 1),
+            together = 2 if places else 1
+            for first in part[::together]:
+                slices = range(first, first + together)
+                pre = {t: places[t] if places else next_bank() for t in slices}
+                for t in slices:
+                    for o, (a, (words, scales, n, at)) in enumerate(passes):
+                        nc.tensor.matmul_mx(
+                            out=pre[t][:, at : at + n],
+                            lhsT=v_w[a, jg][:, P * t : P * (t + 1)].bitcast(FP8X4),
+                            lhsT_scale=v_s[4 * a : P, PASS * jg + P * t : PASS * jg + P * (t + 1)],
+                            rhs=words.bitcast(FP8X4),
+                            rhs_scale=scales,
+                            start=(o == 0),
+                            stop=(o == len(passes) - 1),
+                        )
+                for t in slices:
+                    nc.scalar.activation(out=sq[:, t, :], in_=pre[t][:, :w], func=ACT.Square, bias=b_sb[:, jg, t : t + 1])
+                    nc.scalar.activation(
+                        out=lin[:, t, :], in_=pre[t][:, :w], func=ACT.Identity,
+                        bias=gb_sb[:, jg, t : t + 1], scale=g_sb[:, jg, t : t + 1],
                     )
-                nc.scalar.activation(out=sq[:, t, :], in_=pre[:, :w], func=ACT.Square, bias=b_sb[:, jg, t : t + 1])
-                nc.scalar.activation(
-                    out=lin[:, t, :], in_=pre[:, :w], func=ACT.Identity,
-                    bias=gb_sb[:, jg, t : t + 1], scale=g_sb[:, jg, t : t + 1],
-                )
-            factors[u] = sq, lin
 
         def cube(u, tag=None):
             sq, lin = factors[u]
@@ -270,9 +275,11 @@ def tile_list_cube_parser_layer_kernel(tc, x, tab_words, tab_scales, offs, b, g,
 
         sums = {}
 
-        def bypass(ci, t, acc):
+        def halves(numbers):
+            return [whole[:, QUARTER * o : QUARTER * (o + 1)] for whole in map(bank, numbers) for o in range(2)]
+
+        def bypass(ci, t, acc, first=True):
             sums[ci, t] = acc
-            first = True
             for a in range(2):
                 for words, scales, n, at in runs(x_q, Y_CHUNKS[ci], a):
                     step = 512 if n == 512 else 128
@@ -370,48 +377,59 @@ def tile_list_cube_parser_layer_kernel(tc, x, tab_words, tab_scales, offs, b, g,
         deal_bypass_scales()
         gather_down(0)
         cast_x(2, (0, 1), nc.vector)
-        quantize_x(2)
+        quantize_x(2, (0, 1))
+        cube(0, "x_bf20")
+        cast_x(3, (0,), nc.scalar)
         hidden(2, "factors_c")
         gather_down(1)
-        cube(0, "wd_raw1")
-        cast_x(3, (0, 1), nc.scalar)
-        gather_down(2)
         quantize_h(0)
+        cube(1, "wd_raw1")
+        cast_x(3, (1,), nc.vector)
+        quantize_h(1)
+        quantize_x(3, (0,))
+        quantize_x(3, (1,))
+        gather_down(2)
         gather_down(3)
-        quantize_x(3, "wd_raw3")
-        for t in range(PACK):
-            turn_down(t, (0, 1, 2, 3))
-        hidden(3, "factors_d")
-        cube(1, "x_bf30")
+        turn_down(0, (0, 1))
+        turn_down(1, (0, 1))
+        hidden(3, "factors_d", part=range(0, 3))
+        turn_down(2, (2,))
+        hidden(3, "factors_d", part=range(3, 4))
+        turn_down(3, (3,))
         for t in range(PACK):
             bypass(0, t, bank(RING + t))
-        quantize_down((0, 1, 2, 3))
-        hidden(4, "x_raw10")
-        cube(2, "factors_b")
-        quantize_h(1)
+        cube(2, "wd_raw3")
+        quantize_down((0, 1))
+        quantize_down((2,))
+        quantize_down((3,))
+        hidden(4, "x_raw10", halves((0, 1)))
         for t in range(PACK):
             down(0, t, 1, False)
         quantize_h(2)
-        cube(3, "x_bf30")
+        cube(3)
         for t in range(PACK):
             down(0, t, 0, True)
+        for t, place in enumerate(halves((2, 3))):
+            bypass(1, t, place, t % 2 == 0)
         for t in range(PACK):
-            bypass(1, t, next_bank())
             down(1, t, 0, False)
         for t in range(PACK):
             empty(0, t, "factors_c")
         quantize_h(3)
-        cube(4, "x_bf30")
+        cube(4)
         for t in range(PACK):
-            down(1, t, 1, True)
+            down(1, t, 1, t % 2 == 1)
+        for t in range(PACK):
             empty(1, t, "x_raw11")
+        for t, place in enumerate(halves((0, 1))):
+            bypass(2, t, place, t % 2 == 0)
         for t in range(PACK):
-            bypass(2, t, bank(RING + t))
             down(2, t, 1, False)
         quantize_h(4)
-        cast_y(0, nc.vector, "x_bf30")
+        cast_y(0, nc.vector, "wd_raw1")
         for t in range(PACK):
-            down(2, t, 0, True)
+            down(2, t, 0, t % 2 == 1)
+        for t in range(PACK):
             empty(2, t, "x_raw20")
         quantize_y(0)
         cast_y(1, nc.vector, "x_bf00")

@@ -343,15 +343,15 @@ def tile_list_cube_parser_layer_kernel(tc, x, tab_words, tab_scales, offs, b, g,
 
         load_table(0)
         load_x(0, 0)
-        load_gains()
         load_x(0, 1)
+        load_bypass_scales()
         load_table(1)
+        load_gains()
         load_x(1, 0)
         load_x(1, 1)
-        load_bypass_scales()
-        load_down(0)
         load_x(2, 0)
         load_x(2, 1)
+        load_down(0)
         load_down(1)
         load_x(3, 0)
         load_x(3, 1)
@@ -366,6 +366,7 @@ def tile_list_cube_parser_layer_kernel(tc, x, tab_words, tab_scales, offs, b, g,
         cast_x(0, (1,), nc.scalar)
         quantize_x_head(0, 0)
         quantize_x_head(0, 1)
+        deal_bypass_scales()
         gather_table(1, (0,))
         cast_x(1, (0,), nc.scalar)
         hidden(0, "x_raw10")
@@ -374,16 +375,15 @@ def tile_list_cube_parser_layer_kernel(tc, x, tab_words, tab_scales, offs, b, g,
         quantize_x_head(1, 1)
         gather_table(1, (1,))
         hidden(1, "factors_b")
-        deal_bypass_scales()
-        gather_down(0)
         cast_x(2, (0, 1), nc.vector)
         quantize_x(2, (0, 1))
-        cube(0, "x_bf20")
+        cube(0, "x_raw21")
+        gather_down(0)
         cast_x(3, (0,), nc.scalar)
         hidden(2, "factors_c")
         gather_down(1)
         quantize_h(0)
-        cube(1, "wd_raw1")
+        cube(1)
         cast_x(3, (1,), nc.vector)
         quantize_h(1)
         quantize_x(3, (0,))
@@ -426,7 +426,7 @@ def tile_list_cube_parser_layer_kernel(tc, x, tab_words, tab_scales, offs, b, g,
         for t in range(PACK):
             down(2, t, 1, False)
         quantize_h(4)
-        cast_y(0, nc.vector, "wd_raw1")
+        cast_y(0, nc.vector, "h_bf1")
         for t in range(PACK):
             down(2, t, 0, t % 2 == 1)
         for t in range(PACK):

@@ -320,9 +320,12 @@ def tile_list_cube_parser_layer_kernel(tc, x, tab_words, tab_scales, offs, b, g,
             if t % 2 == 1:
                 nc.sync.dma_start(out=y_rows[:, t - 1 : t + 1, m0 : m0 + w], in_=y[:, t - 1 : t + 1, :])
 
-        def cast_y(ci, engine, tag):
-            bf = held(tag, [P, y_columns(ci)[1], PACK], BF16)
-            weave(engine, bf[:], y_f32[ci][:])
+        def cast_y(ci, engines, tag):
+            w = y_columns(ci)[1]
+            share = w // len(engines)
+            bf = held(tag, [P, w, PACK], BF16)
+            for o, engine in enumerate(engines):
+                weave(engine, bf[:, share * o : share * (o + 1)], y_f32[ci][:, :, share * o : share * (o + 1)])
             y_bf[ci] = bf
 
         def quantize_y(ci):
@@ -380,11 +383,11 @@ def tile_list_cube_parser_layer_kernel(tc, x, tab_words, tab_scales, offs, b, g,
         cube(0, "x_raw21")
         gather_down(0)
         cast_x(3, (0,), nc.scalar)
+        cast_x(3, (1,), nc.scalar)
         hidden(2, "factors_c")
         gather_down(1)
         quantize_h(0)
         cube(1)
-        cast_x(3, (1,), nc.vector)
         quantize_h(1)
         quantize_x(3, (0,))
         quantize_x(3, (1,))
@@ -426,14 +429,14 @@ def tile_list_cube_parser_layer_kernel(tc, x, tab_words, tab_scales, offs, b, g,
         for t in range(PACK):
             down(2, t, 1, False)
         quantize_h(4)
-        cast_y(0, nc.vector, "h_bf1")
+        cast_y(0, [nc.vector], "h_bf1")
         for t in range(PACK):
             down(2, t, 0, t % 2 == 1)
         for t in range(PACK):
             empty(2, t, "x_raw20")
         quantize_y(0)
-        cast_y(1, nc.vector, "x_bf00")
+        cast_y(1, [nc.vector], "x_bf00")
         quantize_y(1)
-        cast_y(2, nc.vector, "x_bf01")
+        cast_y(2, [nc.vector, nc.scalar], "x_bf01")
         quantize_y(2)
         store_scales()

@@ -21,7 +21,6 @@ P = 128
 PACK = 4
 PASS = P * PACK
 GAP = 32
-RING = 4
 QUARTER = 256
 UNITS = ((0, (0,)), (1, (0, 1)), (0, (1, 2)), (1, (2, 3)), (0, (3,)))
 Y_CHUNKS = ((0, 1), (2,), (3,))
@@ -40,14 +39,12 @@ def tile_list_cube_parser_layer_kernel(tc, x, tab_words, tab_scales, offs, b, g,
     with ExitStack() as ctx:
         keep = ctx.enter_context(tc.tile_pool(name="keep", bufs=1))
         psum = ctx.enter_context(tc.psum_pool(name="psum", bufs=1))
-        taken = []
 
         def bank(number):
             return psum.tile([P, 512], F32, name="bank%d" % number)
 
-        def next_bank():
-            taken.append(len(taken) % RING)
-            return bank(taken[-1])
+        def banks(*numbers):
+            return [bank(number) for number in numbers]
 
         def held(name, shape, dtype):
             return keep.tile(shape, dtype, name=name, align_bytes=64)
@@ -76,11 +73,12 @@ def tile_list_cube_parser_layer_kernel(tc, x, tab_words, tab_scales, offs, b, g,
         c_sb = held("c_sb", [P, PACK], F32)
         x_raw, wd_raw, tab_w = {}, {}, {}
 
-        def load_x(q, a):
-            m0 = QUARTER * q
-            raw = held("x_raw%d%d" % (q, a), [P, PACK, QUARTER], F32)
-            nc.sync.dma_start(out=raw[:], in_=x[PASS * a : PASS * (a + 1), m0 : m0 + QUARTER].rearrange("(p i) m -> p i m", i=PACK))
-            x_raw[q, a] = raw
+        def load_x(quarters, a):
+            m0, w = QUARTER * quarters[0], QUARTER * len(quarters)
+            raw = held("x_raw%d%d" % (quarters[0], a), [P, PACK, w], F32)
+            nc.sync.dma_start(out=raw[:], in_=x[PASS * a : PASS * (a + 1), m0 : m0 + w].rearrange("(p i) m -> p i m", i=PACK))
+            for o, q in enumerate(quarters):
+                x_raw[q, a] = raw[:, :, QUARTER * o : QUARTER * (o + 1)]
 
         def load_down(t):
             raw = held("wd_raw%d" % t, [P, T], F32)
@@ -95,9 +93,9 @@ def tile_list_cube_parser_layer_kernel(tc, x, tab_words, tab_scales, offs, b, g,
         def load_gains():
             nc.sync.dma_start(out=b_sb[:], in_=b.rearrange("(g p t) -> p g t", g=2, t=PACK))
             nc.sync.dma_start(out=g_sb[:], in_=g.rearrange("(g p t) -> p g t", g=2, t=PACK))
-            for jg in range(2):
-                for t in range(PACK):
-                    nc.scalar.activation(out=gb_sb[:, jg, t : t + 1], in_=b_sb[:, jg, t : t + 1], func=ACT.Copy, scale=g_sb[:, jg, t : t + 1])
+
+        def gains():
+            nc.vector.tensor_tensor(out=gb_sb[:], in0=b_sb[:], in1=g_sb[:], op=ALU.mult)
 
         def load_bypass_scales():
             for q in range(4):
@@ -137,74 +135,50 @@ def tile_list_cube_parser_layer_kernel(tc, x, tab_words, tab_scales, offs, b, g,
             else:
                 nc.scalar.activation(out=woven(out), in_=planes(in_), func=ACT.Copy)
 
-        def quantize(name, bf, tags=None):
-            count, width = bf.shape[1], bf.shape[2]
-            words = held(tags[0] if tags else name + "_w", [P, count, width], U32)
-            scales = held(tags[1] if tags and len(tags) > 1 else name + "_s", [P, count, width], U8)
-            nc.vector.quantize_mx(
-                out=words[:].rearrange("p o m -> p (o m)").bitcast(FP8X4),
-                scales=scales[:].rearrange("p o m -> p (o m)"),
-                in_=bf[:].rearrange("p o m t -> p (o m t)"),
-            )
-            return [(words[:, o, :], scales[:, o, :]) for o in range(count)]
-
-        def runs(store, quarters, key):
-            found = []
-            for o, q in enumerate(quarters):
-                words, scales, row, col = store[q, key]
-                if found and found[-1][0] is words and found[-1][2] == row and found[-1][3] + found[-1][4] == col:
-                    found[-1][4] = found[-1][4] + QUARTER
-                else:
-                    found.append([words, scales, row, col, QUARTER, QUARTER * o])
-            return [(w[:, r, c0 : c0 + n], s[:, r, c0 : c0 + n], n, at) for w, s, r, c0, n, at in found]
-
-        x_bf, x_q = {}, {}
-        x_head_w = [held("x_head_w%d" % a, [P, 1, 2 * QUARTER], U32) for a in range(2)]
-        x_head_s = [held("x_head_s%d" % a, [P, 1, 2 * QUARTER], U8) for a in range(2)]
-
-        def cast_x(q, passes, engine):
-            bf = held("x_bf%d%d" % (q, passes[0]), [P, len(passes), QUARTER, PACK], BF16)
-            for o, a in enumerate(passes):
-                weave(engine, bf[:, o], x_raw[q, a][:])
-            x_bf[q, passes] = bf
+        def columns(quarters):
+            return slice(QUARTER * quarters[0], QUARTER * (quarters[-1] + 1))
 
         def quantize_into(words, scales, bf):
-            nc.vector.quantize_mx(out=words.bitcast(FP8X4), scales=scales, in_=bf[:].rearrange("p o m t -> p (o m t)"))
+            nc.vector.quantize_mx(out=words.bitcast(FP8X4), scales=scales, in_=bf.rearrange("p m t -> p (m t)"))
 
-        def quantize_x_head(q, a):
-            cols = slice(QUARTER * q, QUARTER * (q + 1))
-            quantize_into(x_head_w[a][:, 0, cols], x_head_s[a][:, 0, cols], x_bf[q, (a,)])
-            x_q[q, a] = x_head_w[a], x_head_s[a], 0, QUARTER * q
+        x_bf = {}
+        x_w = [held("x_w%d" % a, [P, M], U32) for a in range(2)]
+        x_s = [held("x_s%d" % a, [P, M], U8) for a in range(2)]
 
-        def quantize_x(q, passes):
-            words = held("x_w%d%d" % (q, passes[0]), [P, len(passes), QUARTER], U32)
-            scales = held("x_s%d%d" % (q, passes[0]), [P, len(passes), QUARTER], U8)
-            quantize_into(words[:].rearrange("p o m -> p (o m)"), scales[:].rearrange("p o m -> p (o m)"), x_bf[q, passes])
-            for o, a in enumerate(passes):
-                x_q[q, a] = words, scales, o, 0
+        def cast_x(q, a, engine, tag=None):
+            x_bf[q, a] = held(tag or "x_bf%d%d" % (q, a), [P, QUARTER, PACK], BF16)
+            weave(engine, x_bf[q, a][:], x_raw[q, a])
 
-        factors, h_bf, h_q = {}, {}, {}
+        def quantize_x(q, a):
+            cols = columns((q,))
+            quantize_into(x_w[a][:, cols], x_s[a][:, cols], x_bf[q, a][:])
 
-        def hidden(u, tag, places=None, part=range(PACK)):
+        h_w = [held("h_w%d" % jg, [P, M], U32) for jg in range(2)]
+        h_s = [held("h_s%d" % jg, [P, M], U8) for jg in range(2)]
+        factors, h_bf = {}, {}
+
+        def hidden(u, tag, places, part=range(PACK), together=1, apart=False):
             jg, quarters = UNITS[u]
             w = QUARTER * len(quarters)
+            runs = [(q,) for q in quarters] if apart else [quarters]
+            passes = [(run, a) for run in runs for a in range(2)]
             if u not in factors:
                 both = held(tag, [P, 2, PACK, w], F32)
                 factors[u] = both[:, 0], both[:, 1]
             sq, lin = factors[u]
-            passes = [(a, run) for a in range(2) for run in reversed(runs(x_q, quarters, a))]
-            together = 2 if places else 1
+            pre = dict(zip(part, places))
             for first in part[::together]:
                 slices = range(first, first + together)
-                pre = {t: places[t] if places else next_bank() for t in slices}
                 for t in slices:
-                    for o, (a, (words, scales, n, at)) in enumerate(passes):
+                    for o, (run, a) in enumerate(passes):
+                        cols = columns(run)
+                        at = cols.start - QUARTER * quarters[0]
                         nc.tensor.matmul_mx(
-                            out=pre[t][:, at : at + n],
+                            out=pre[t][:, at : at + QUARTER * len(run)],
                             lhsT=v_w[a, jg][:, P * t : P * (t + 1)].bitcast(FP8X4),
                             lhsT_scale=v_s[4 * a : P, PASS * jg + P * t : PASS * jg + P * (t + 1)],
-                            rhs=words.bitcast(FP8X4),
-                            rhs_scale=scales,
+                            rhs=x_w[a][:, cols].bitcast(FP8X4),
+                            rhs_scale=x_s[a][:, cols],
                             start=(o == 0),
                             stop=(o == len(passes) - 1),
                         )
@@ -217,41 +191,41 @@ def tile_list_cube_parser_layer_kernel(tc, x, tab_words, tab_scales, offs, b, g,
 
         def cube(u, tag=None):
             sq, lin = factors[u]
-            bf = held(tag or "h_bf%d" % u, [P, 1, QUARTER * len(UNITS[u][1]), PACK], BF16)
-            nc.vector.tensor_tensor(out=woven(bf[:, 0]), in0=planes(sq), in1=planes(lin), op=ALU.mult)
+            bf = held(tag or "h_bf%d" % u, [P, QUARTER * len(UNITS[u][1]), PACK], BF16)
+            nc.vector.tensor_tensor(out=woven(bf[:]), in0=planes(sq), in1=planes(lin), op=ALU.mult)
             h_bf[u] = bf
 
         def quantize_h(u):
             jg, quarters = UNITS[u]
-            w = QUARTER * len(quarters)
-            words = held("h_w%d" % u, [P, 1, w], U32)
-            scales = held("h_s%d" % u, [P, 1, w], U8)
-            quantize_into(words[:, 0, :], scales[:, 0, :], h_bf[u])
-            for o, q in enumerate(quarters):
-                h_q[q, jg] = words, scales, 0, QUARTER * o
+            cols = columns(quarters)
+            quantize_into(h_w[jg][:, cols], h_s[jg][:, cols], h_bf[u][:])
 
-        wd_picked, wd_bf, wd_q = {}, {}, {}
+        wd_picked = {}
 
         def gather_down(t, tag=None):
             picked = held(tag or "picked%d" % t, [P, 2, PASS + GAP], BF16)
             nc.vector.tensor_copy(out=picked[:, :, :PASS], in_=wd_raw[t][:].indirect(offsets[:]))
             wd_picked[t] = picked
 
-        def turn_down(t, slices):
-            if slices not in wd_bf:
-                wd_bf[slices] = held("wd_bf%d" % slices[0], [P, 2 * len(slices), P, PACK], BF16)
+        wd_bf = held("wd_bf", [P, PACK, 2, P, PACK], BF16)
+        wd_w = held("wd_w", [P, PACK, 2, P], U32)
+        wd_s = held("wd_s", [P, PACK, 2, P], U8)
+
+        def turn_down(t, number):
             pairs = wd_picked[t][:].bitcast(F32)
-            turned = next_bank()[:].rearrange("p (g u n) -> p g u n", g=2, u=2)
+            turned = bank(number)[:].rearrange("p (g u n) -> p g u n", g=2, u=2)
             for jg in range(2):
                 for u in range(2):
                     nc.tensor.transpose(turned[:, jg, u, :], pairs[:, jg, u : 2 * P : 2], ident[:])
-            o = 2 * slices.index(t)
-            nc.scalar.copy(out=wd_bf[slices][:, o : o + 2].bitcast(F32), in_=turned.rearrange("p g u n -> p g n u"))
+            nc.scalar.copy(out=wd_bf[:, t].bitcast(F32), in_=turned.rearrange("p g u n -> p g n u"))
 
-        def quantize_down(slices, tags=None):
-            made = quantize("wd%d" % slices[0], wd_bf[slices], tags)
-            for o, t in enumerate(slices):
-                wd_q[t] = made[2 * o : 2 * o + 2]
+        def quantize_down(first=0, count=PACK):
+            part = slice(first, first + count)
+            quantize_into(
+                wd_w[:, part].rearrange("p t g n -> p (t g n)"),
+                wd_s[:, part].rearrange("p t g n -> p (t g n)"),
+                wd_bf[:, part].rearrange("p t g n i -> p (t g n) i"),
+            )
 
         w4_w_dealt = held("w4_w_dealt", [P, 2, 2 * N], U8)
         w4_s_dealt = held("w4_s_dealt", [P, 2, N], U8)
@@ -280,33 +254,32 @@ def tile_list_cube_parser_layer_kernel(tc, x, tab_words, tab_scales, offs, b, g,
 
         def bypass(ci, t, acc, first=True):
             sums[ci, t] = acc
+            m0, w = y_columns(ci)
+            step = 512 if w == 512 else 128
             for a in range(2):
-                for words, scales, n, at in runs(x_q, Y_CHUNKS[ci], a):
-                    step = 512 if n == 512 else 128
-                    for n0 in range(0, n, step):
-                        nc.tensor.matmul_mx(
-                            out=acc[:, at + n0 : at + n0 + step],
-                            lhsT=w4_w_dealt[:, a, 2 * P * t : 2 * P * (t + 1)].bitcast(FP4X4),
-                            lhsT_scale=w4_s_dealt[:, a, P * t : P * (t + 1)],
-                            rhs=words[:, n0 : n0 + step].bitcast(FP8X4),
-                            rhs_scale=scales[:, n0 : n0 + step],
-                            start=first,
-                            stop=False,
-                        )
-                        first = False
+                for n0 in range(0, w, step):
+                    nc.tensor.matmul_mx(
+                        out=acc[:, n0 : n0 + step],
+                        lhsT=w4_w_dealt[:, a, 2 * P * t : 2 * P * (t + 1)].bitcast(FP4X4),
+                        lhsT_scale=w4_s_dealt[:, a, P * t : P * (t + 1)],
+                        rhs=x_w[a][:, m0 + n0 : m0 + n0 + step].bitcast(FP8X4),
+                        rhs_scale=x_s[a][:, m0 + n0 : m0 + n0 + step],
+                        start=first,
+                        stop=False,
+                    )
+                    first = False
 
         def down(ci, t, jg, last):
-            found = runs(h_q, Y_CHUNKS[ci], jg)
-            for o, (words, scales, n, at) in enumerate(found):
-                nc.tensor.matmul_mx(
-                    out=sums[ci, t][:, at : at + n],
-                    lhsT=wd_q[t][jg][0].bitcast(FP8X4),
-                    lhsT_scale=wd_q[t][jg][1],
-                    rhs=words.bitcast(FP8X4),
-                    rhs_scale=scales,
-                    start=False,
-                    stop=(last and o == len(found) - 1),
-                )
+            m0, w = y_columns(ci)
+            nc.tensor.matmul_mx(
+                out=sums[ci, t][:, :w],
+                lhsT=wd_w[:, t, jg, :].bitcast(FP8X4),
+                lhsT_scale=wd_s[:, t, jg, :],
+                rhs=h_w[jg][:, m0 : m0 + w].bitcast(FP8X4),
+                rhs_scale=h_s[jg][:, m0 : m0 + w],
+                start=False,
+                stop=last,
+            )
 
         def y_columns(ci):
             return QUARTER * Y_CHUNKS[ci][0], QUARTER * len(Y_CHUNKS[ci])
@@ -345,19 +318,19 @@ def tile_list_cube_parser_layer_kernel(tc, x, tab_words, tab_scales, offs, b, g,
                 )
 
         load_table(0)
-        load_x(0, 0)
-        load_x(0, 1)
+        load_x((0,), 0)
+        load_x((0,), 1)
         load_bypass_scales()
         load_table(1)
         load_gains()
-        load_x(1, 0)
-        load_x(1, 1)
-        load_x(2, 0)
-        load_x(2, 1)
+        load_x((1,), 0)
+        load_x((1,), 1)
+        load_x((2,), 0)
+        load_x((2,), 1)
         load_down(0)
         load_down(1)
-        load_x(3, 0)
-        load_x(3, 1)
+        load_x((3,), 0)
+        load_x((3,), 1)
         load_down(2)
         load_down(3)
         load_bias()
@@ -365,53 +338,56 @@ def tile_list_cube_parser_layer_kernel(tc, x, tab_words, tab_scales, offs, b, g,
         deal_bypass_words()
         gather_scales()
         gather_table(0, (0, 1))
-        cast_x(0, (0,), nc.scalar)
-        cast_x(0, (1,), nc.scalar)
-        quantize_x_head(0, 0)
-        quantize_x_head(0, 1)
+        cast_x(0, 0, nc.scalar)
+        cast_x(0, 1, nc.scalar)
+        quantize_x(0, 0)
         deal_bypass_scales()
+        quantize_x(0, 1)
         gather_table(1, (0,))
-        cast_x(1, (0,), nc.scalar)
-        hidden(0, "x_raw10")
-        cast_x(1, (1,), nc.vector)
-        quantize_x_head(1, 0)
-        quantize_x_head(1, 1)
+        gains()
+        hidden(0, "factors_a", banks(0, 1, 2, 3))
         gather_table(1, (1,))
-        hidden(1, "factors_b")
-        cast_x(2, (0, 1), nc.vector)
-        quantize_x(2, (0, 1))
-        cube(0, "x_raw21")
-        gather_down(0)
-        cast_x(3, (0,), nc.scalar)
-        cast_x(3, (1,), nc.scalar)
-        hidden(2, "factors_c")
-        gather_down(1)
+        cast_x(1, 0, nc.vector)
+        quantize_x(1, 0)
+        cast_x(1, 1, nc.vector)
+        quantize_x(1, 1)
+        cast_x(2, 0, nc.scalar)
+        hidden(1, "factors_b", banks(4, 5, 6, 7))
+        cube(0, "x_bf11")
         quantize_h(0)
+        cast_x(2, 1, nc.vector)
+        quantize_x(2, 0)
+        quantize_x(2, 1)
+        gather_down(0)
+        hidden(2, "factors_c", banks(0, 1), range(0, 2))
+        cast_x(3, 0, nc.scalar)
+        cast_x(3, 1, nc.scalar)
+        hidden(2, "factors_c", banks(2, 3), range(2, 4))
+        for t in range(PACK):
+            bypass(0, t, bank(4 + t))
         cube(1)
+        gather_down(1)
+        quantize_x(3, 0)
+        quantize_x(3, 1)
         quantize_h(1)
-        quantize_x(3, (0,))
-        quantize_x(3, (1,))
+        hidden(3, "factors_d", banks(0, 1), range(0, 2), apart=True)
         gather_down(2)
         gather_down(3)
-        turn_down(0, (0, 1))
-        turn_down(1, (0, 1))
-        hidden(3, "factors_d", part=range(0, 3))
-        turn_down(2, (2,))
-        hidden(3, "factors_d", part=range(3, 4))
-        turn_down(3, (3,))
-        for t in range(PACK):
-            bypass(0, t, bank(RING + t))
+        turn_down(0, 2)
+        turn_down(1, 3)
+        turn_down(2, 0)
+        hidden(3, "factors_d", banks(1), range(2, 3))
+        turn_down(3, 2)
+        hidden(3, "factors_d", banks(3), range(3, 4))
         cube(2, "wd_raw3")
-        quantize_down((0, 1))
-        quantize_down((2,))
-        quantize_down((3,))
-        hidden(4, "x_raw10", halves((0, 1)))
+        quantize_down(0, 2)
+        quantize_h(2)
+        quantize_down(2, 2)
+        hidden(4, "factors_a", halves((0, 1)), together=2)
         for t in range(PACK):
             down(0, t, 1, False)
-        quantize_h(2)
-        cube(3)
-        for t in range(PACK):
             down(0, t, 0, True)
+        cube(3)
         for t, place in enumerate(halves((2, 3))):
             bypass(1, t, place, t % 2 == 0)
         for t in range(PACK):
@@ -424,7 +400,7 @@ def tile_list_cube_parser_layer_kernel(tc, x, tab_words, tab_scales, offs, b, g,
             down(1, t, 1, t % 2 == 1)
         for t in range(PACK):
             empty(1, t, "x_raw11")
-        for t, place in enumerate(halves((0, 1))):
+        for t, place in enumerate(halves((4, 5))):
             bypass(2, t, place, t % 2 == 0)
         for t in range(PACK):
             down(2, t, 1, False)
@@ -434,8 +410,8 @@ def tile_list_cube_parser_layer_kernel(tc, x, tab_words, tab_scales, offs, b, g,
             down(2, t, 0, t % 2 == 1)
         for t in range(PACK):
             empty(2, t, "x_raw20")
-        quantize_y(0)
         cast_y(1, [nc.vector], "x_bf00")
+        quantize_y(0)
         quantize_y(1)
         cast_y(2, [nc.vector, nc.scalar], "x_bf01")
         quantize_y(2)

@@ -24,6 +24,7 @@ GAP = 32
 QUARTER = 256
 UNITS = ((0, (0,)), (1, (0, 1)), (0, (1, 2)), (1, (2, 3)), (0, (3,)))
 Y_CHUNKS = ((0, 1), (2,), (3,))
+AT = {"wd_raw3": 0, "h_bf2": 0, "wd_w": 4096}
 
 
 def woven(tile_ap):
@@ -38,6 +39,7 @@ def tile_list_cube_parser_layer_kernel(tc, x, tab_words, tab_scales, offs, b, g,
     nc = tc.nc
     with ExitStack() as ctx:
         keep = ctx.enter_context(tc.tile_pool(name="keep", bufs=1))
+        reused = ctx.enter_context(tc.tile_pool(name="reused", bufs=1))
         psum = ctx.enter_context(tc.psum_pool(name="psum", bufs=1))
 
         def bank(number):
@@ -47,6 +49,8 @@ def tile_list_cube_parser_layer_kernel(tc, x, tab_words, tab_scales, offs, b, g,
             return [bank(number) for number in numbers]
 
         def held(name, shape, dtype):
+            if name in AT:
+                return reused.tile(shape, dtype, name=name, align_bytes=64, offset=AT[name])
             return keep.tile(shape, dtype, name=name, align_bytes=64)
 
         offsets = keep.tile([P, S // 16], U16, name="offsets")
@@ -145,9 +149,12 @@ def tile_list_cube_parser_layer_kernel(tc, x, tab_words, tab_scales, offs, b, g,
         x_w = [held("x_w%d" % a, [P, M], U32) for a in range(2)]
         x_s = [held("x_s%d" % a, [P, M], U8) for a in range(2)]
 
-        def cast_x(q, a, engine, tag=None):
-            x_bf[q, a] = held(tag or "x_bf%d%d" % (q, a), [P, QUARTER, PACK], BF16)
-            weave(engine, x_bf[q, a][:], x_raw[q, a])
+        def cast_x(q, a, *engines):
+            x_bf[q, a] = held("x_bf%d%d" % (q, a), [P, QUARTER, PACK], BF16)
+            share = QUARTER // len(engines)
+            for o, engine in enumerate(engines):
+                part = slice(share * o, share * (o + 1))
+                weave(engine, x_bf[q, a][:, part], x_raw[q, a][:, :, part])
 
         def quantize_x(q, a):
             cols = columns((q,))
@@ -328,9 +335,9 @@ def tile_list_cube_parser_layer_kernel(tc, x, tab_words, tab_scales, offs, b, g,
         load_x((2,), 0)
         load_x((2,), 1)
         load_down(0)
-        load_down(1)
         load_x((3,), 0)
         load_x((3,), 1)
+        load_down(1)
         load_down(2)
         load_down(3)
         load_bias()
@@ -351,35 +358,33 @@ def tile_list_cube_parser_layer_kernel(tc, x, tab_words, tab_scales, offs, b, g,
         quantize_x(1, 0)
         cast_x(1, 1, nc.vector)
         quantize_x(1, 1)
-        cast_x(2, 0, nc.scalar)
-        hidden(1, "factors_b", banks(4, 5, 6, 7))
+        cast_x(2, 0, nc.scalar, nc.vector)
+        hidden(1, "factors_b", banks(4, 5, 6, 7), apart=True)
         cube(0, "x_bf11")
         quantize_h(0)
         cast_x(2, 1, nc.vector)
         quantize_x(2, 0)
         quantize_x(2, 1)
         gather_down(0)
-        hidden(2, "factors_c", banks(0, 1), range(0, 2))
         cast_x(3, 0, nc.scalar)
-        cast_x(3, 1, nc.scalar)
-        hidden(2, "factors_c", banks(2, 3), range(2, 4))
+        cast_x(3, 1, nc.scalar, nc.vector)
+        hidden(2, "factors_c", banks(0, 1, 2, 3))
         for t in range(PACK):
             bypass(0, t, bank(4 + t))
         cube(1)
-        gather_down(1)
+        quantize_h(1)
         quantize_x(3, 0)
         quantize_x(3, 1)
-        quantize_h(1)
+        gather_down(1)
         hidden(3, "factors_d", banks(0, 1), range(0, 2), apart=True)
         gather_down(2)
         gather_down(3)
         turn_down(0, 2)
         turn_down(1, 3)
-        turn_down(2, 0)
-        hidden(3, "factors_d", banks(1), range(2, 3))
-        turn_down(3, 2)
-        hidden(3, "factors_d", banks(3), range(3, 4))
-        cube(2, "wd_raw3")
+        hidden(3, "factors_d", banks(0, 1), range(2, 4))
+        turn_down(2, 2)
+        turn_down(3, 3)
+        cube(2)
         quantize_down(0, 2)
         quantize_h(2)
         quantize_down(2, 2)
@@ -387,7 +392,7 @@ def tile_list_cube_parser_layer_kernel(tc, x, tab_words, tab_scales, offs, b, g,
         for t in range(PACK):
             down(0, t, 1, False)
             down(0, t, 0, True)
-        cube(3)
+        cube(3, "wd_bf")
         for t, place in enumerate(halves((2, 3))):
             bypass(1, t, place, t % 2 == 0)
         for t in range(PACK):
@@ -395,7 +400,7 @@ def tile_list_cube_parser_layer_kernel(tc, x, tab_words, tab_scales, offs, b, g,
         for t in range(PACK):
             empty(0, t, "factors_c")
         quantize_h(3)
-        cube(4)
+        cube(4, "wd_bf")
         for t in range(PACK):
             down(1, t, 1, t % 2 == 1)
         for t in range(PACK):
@@ -405,12 +410,12 @@ def tile_list_cube_parser_layer_kernel(tc, x, tab_words, tab_scales, offs, b, g,
         for t in range(PACK):
             down(2, t, 1, False)
         quantize_h(4)
-        cast_y(0, [nc.vector], "h_bf1")
+        cast_y(0, [nc.vector], "wd_bf")
+        cast_y(1, [nc.vector], "x_bf00")
         for t in range(PACK):
             down(2, t, 0, t % 2 == 1)
         for t in range(PACK):
             empty(2, t, "x_raw20")
-        cast_y(1, [nc.vector], "x_bf00")
         quantize_y(0)
         quantize_y(1)
         cast_y(2, [nc.vector, nc.scalar], "x_bf01")

@@ -24,7 +24,7 @@ GAP = 32
 QUARTER = 256
 UNITS = ((0, (0,)), (1, (0, 1)), (0, (1, 2)), (1, (2, 3)), (0, (3,)))
 Y_CHUNKS = ((0, 1), (2,), (3,))
-AT = {"wd_raw3": 0, "h_bf2": 0, "wd_w": 4096}
+AT = {"wd_raw3": 4096, "h_bf11": 2304, "h_bf21": 4352, "h_bf22": 6400, "h_s1": 8448, "h_bf32": 9472, "wd_w": 12032}
 
 
 def woven(tile_ap):
@@ -196,16 +196,33 @@ def tile_list_cube_parser_layer_kernel(tc, x, tab_words, tab_scales, offs, b, g,
                         bias=gb_sb[:, jg, t : t + 1], scale=g_sb[:, jg, t : t + 1],
                     )
 
-        def cube(u, tag=None):
+        def cube(u, quarters=None, tag=None):
+            quarters = quarters or UNITS[u][1]
             sq, lin = factors[u]
-            bf = held(tag or "h_bf%d" % u, [P, QUARTER * len(UNITS[u][1]), PACK], BF16)
-            nc.vector.tensor_tensor(out=woven(bf[:]), in0=planes(sq), in1=planes(lin), op=ALU.mult)
-            h_bf[u] = bf
+            cols = columns([q - UNITS[u][1][0] for q in quarters])
+            bf = held(tag or "h_bf%d%d" % (u, quarters[0]), [P, QUARTER * len(quarters), PACK], BF16)
+            nc.vector.tensor_tensor(out=woven(bf[:]), in0=planes(sq[:, :, cols]), in1=planes(lin[:, :, cols]), op=ALU.mult)
+            h_bf[u, quarters] = bf
 
-        def quantize_h(u):
-            jg, quarters = UNITS[u]
+        h_planes = {}
+
+        def product(u, quarters, tag):
+            sq, lin = factors[u]
+            cols = columns([q - UNITS[u][1][0] for q in quarters])
+            flat = held(tag, [P, PACK, QUARTER * len(quarters)], BF16)
+            nc.gpsimd.tensor_tensor(out=flat[:], in0=sq[:, :, cols], in1=lin[:, :, cols], op=ALU.mult)
+            for o, q in enumerate(quarters):
+                h_planes[u, q] = flat[:, :, QUARTER * o : QUARTER * (o + 1)]
+
+        def weave_h(u, q, engine):
+            h_bf[u, (q,)] = held("h_bf%d%d" % (u, q), [P, QUARTER, PACK], BF16)
+            weave(engine, h_bf[u, (q,)][:], h_planes[u, q])
+
+        def quantize_h(u, quarters=None):
+            quarters = quarters or UNITS[u][1]
+            jg = UNITS[u][0]
             cols = columns(quarters)
-            quantize_into(h_w[jg][:, cols], h_s[jg][:, cols], h_bf[u][:])
+            quantize_into(h_w[jg][:, cols], h_s[jg][:, cols], h_bf[u, quarters][:])
 
         wd_picked = {}
 
@@ -334,9 +351,9 @@ def tile_list_cube_parser_layer_kernel(tc, x, tab_words, tab_scales, offs, b, g,
         load_x((1,), 1)
         load_x((2,), 0)
         load_x((2,), 1)
-        load_down(0)
         load_x((3,), 0)
         load_x((3,), 1)
+        load_down(0)
         load_down(1)
         load_down(2)
         load_down(3)
@@ -360,47 +377,53 @@ def tile_list_cube_parser_layer_kernel(tc, x, tab_words, tab_scales, offs, b, g,
         quantize_x(1, 1)
         cast_x(2, 0, nc.scalar, nc.vector)
         hidden(1, "factors_b", banks(4, 5, 6, 7), apart=True)
-        cube(0, "x_bf11")
-        quantize_h(0)
+        cube(0, tag="x_bf11")
         cast_x(2, 1, nc.vector)
         quantize_x(2, 0)
         quantize_x(2, 1)
-        gather_down(0)
-        cast_x(3, 0, nc.scalar)
-        cast_x(3, 1, nc.scalar, nc.vector)
+        cast_x(3, 0, nc.vector)
+        quantize_h(0)
+        cast_x(3, 1, nc.vector)
+        quantize_x(3, 0)
+        quantize_x(3, 1)
         hidden(2, "factors_c", banks(0, 1, 2, 3))
         for t in range(PACK):
             bypass(0, t, bank(4 + t))
-        cube(1)
-        quantize_h(1)
-        quantize_x(3, 0)
-        quantize_x(3, 1)
-        gather_down(1)
-        hidden(3, "factors_d", banks(0, 1), range(0, 2), apart=True)
-        gather_down(2)
-        gather_down(3)
+        product(1, (0, 1), "x_bf31")
+        product(2, (1,), "x_bf30")
+        for t in range(PACK):
+            gather_down(t)
+        hidden(3, "factors_d", banks(0, 1), range(0, 2))
+        weave_h(1, 0, nc.scalar)
         turn_down(0, 2)
         turn_down(1, 3)
         hidden(3, "factors_d", banks(0, 1), range(2, 4))
         turn_down(2, 2)
         turn_down(3, 3)
-        cube(2)
+        weave_h(1, 1, nc.vector)
+        weave_h(2, 1, nc.vector)
+        quantize_h(1, (0,))
+        quantize_h(1, (1,))
         quantize_down(0, 2)
-        quantize_h(2)
+        quantize_h(2, (1,))
+        cube(2, (2,))
         quantize_down(2, 2)
         hidden(4, "factors_a", halves((0, 1)), together=2)
         for t in range(PACK):
             down(0, t, 1, False)
             down(0, t, 0, True)
-        cube(3, "wd_bf")
+        cube(3, (2,))
+        quantize_h(2, (2,))
+        cube(3, (3,), "wd_bf")
         for t, place in enumerate(halves((2, 3))):
             bypass(1, t, place, t % 2 == 0)
         for t in range(PACK):
             down(1, t, 0, False)
         for t in range(PACK):
             empty(0, t, "factors_c")
-        quantize_h(3)
-        cube(4, "wd_bf")
+        quantize_h(3, (2,))
+        cube(4)
+        quantize_h(3, (3,))
         for t in range(PACK):
             down(1, t, 1, t % 2 == 1)
         for t in range(PACK):
@@ -410,14 +433,14 @@ def tile_list_cube_parser_layer_kernel(tc, x, tab_words, tab_scales, offs, b, g,
         for t in range(PACK):
             down(2, t, 1, False)
         quantize_h(4)
-        cast_y(0, [nc.vector], "wd_bf")
+        cast_y(0, [nc.vector], "x_bf31")
         cast_y(1, [nc.vector], "x_bf00")
         for t in range(PACK):
             down(2, t, 0, t % 2 == 1)
         for t in range(PACK):
             empty(2, t, "x_raw20")
         quantize_y(0)
-        quantize_y(1)
         cast_y(2, [nc.vector, nc.scalar], "x_bf01")
+        quantize_y(1)
         quantize_y(2)
         store_scales()

@@ -59,17 +59,21 @@ def tile_list_cube_parser_layer_kernel(tc, x, tab_words, tab_scales, offs, b, g,
         b_sb = held("b_sb", [P, 2, PACK], F32)
         g_sb = held("g_sb", [P, 2, PACK], F32)
         w4_w = held("w4_w", [P, 2, 2 * N], U8)
-        nc.sync.dma_start(out=w4_w[:].bitcast(I32), in_=w4_words.rearrange("a p e -> p a e").bitcast(I32))
 
         tab_s = held("tab_s", [P, T], U8)
         nc.gpsimd.memset(tab_s[:].bitcast(I32), 0)
         for q in range(4):
-            nc.sync.dma_start(
+            nc.gpsimd.dma_start(
                 out=tab_s[32 * q : 32 * q + 8, :].bitcast(I32),
                 in_=tab_scales[:, 4 * q : 4 * q + 4, :].bitcast(I32),
             )
         w4_s = held("w4_s", [P, 2, N], U8)
         nc.gpsimd.memset(w4_s[:].rearrange("p a n -> p (a n)").bitcast(I32), 0)
+        for q in range(4):
+            nc.gpsimd.dma_start(
+                out=w4_s[32 * q : 32 * q + 4, :, :].bitcast(I32),
+                in_=w4_scales[:, 4 * q : 4 * q + 4, :].rearrange("a r n -> r a n").bitcast(I32),
+            )
         ident = held("ident", [P, P], F32)
         make_identity(nc, ident[:])
 
@@ -100,13 +104,6 @@ def tile_list_cube_parser_layer_kernel(tc, x, tab_words, tab_scales, offs, b, g,
 
         def gains():
             nc.vector.tensor_tensor(out=gb_sb[:], in0=b_sb[:], in1=g_sb[:], op=ALU.mult)
-
-        def load_bypass_scales():
-            for q in range(4):
-                nc.sync.dma_start(
-                    out=w4_s[32 * q : 32 * q + 4, :, :].bitcast(I32),
-                    in_=w4_scales[:, 4 * q : 4 * q + 4, :].rearrange("a r n -> r a n").bitcast(I32),
-                )
 
         def load_bias():
             nc.sync.dma_start(out=c_sb[:], in_=c.rearrange("(p t) -> p t", t=PACK))
@@ -344,11 +341,11 @@ def tile_list_cube_parser_layer_kernel(tc, x, tab_words, tab_scales, offs, b, g,
         load_table(0)
         load_x((0,), 0)
         load_x((0,), 1)
-        load_bypass_scales()
         load_table(1)
         load_gains()
         load_x((1,), 0)
         load_x((1,), 1)
+        nc.sync.dma_start(out=w4_w[:].bitcast(I32), in_=w4_words.rearrange("a p e -> p a e").bitcast(I32))
         load_x((2,), 0)
         load_x((2,), 1)
         load_x((3,), 0)
@@ -359,9 +356,8 @@ def tile_list_cube_parser_layer_kernel(tc, x, tab_words, tab_scales, offs, b, g,
         load_down(3)
         load_bias()
 
-        deal_bypass_words()
-        gather_scales()
         gather_table(0, (0, 1))
+        gather_scales()
         cast_x(0, 0, nc.scalar)
         cast_x(0, 1, nc.scalar)
         quantize_x(0, 0)
@@ -375,6 +371,7 @@ def tile_list_cube_parser_layer_kernel(tc, x, tab_words, tab_scales, offs, b, g,
         quantize_x(1, 0)
         cast_x(1, 1, nc.vector)
         quantize_x(1, 1)
+        deal_bypass_words()
         cast_x(2, 0, nc.scalar, nc.vector)
         hidden(1, "factors_b", banks(4, 5, 6, 7), apart=True)
         cube(0, tag="x_bf11")

@@ -22,9 +22,10 @@ PACK = 4
 PASS = P * PACK
 GAP = 32
 QUARTER = 256
-UNITS = ((0, (0,)), (1, (0, 1)), (0, (1, 2)), (1, (2, 3)), (0, (3,)))
+KIB = 1024
+WIDTH = {F32: 4, U32: 4, BF16: 2, U8: 1}
+UNITS = ((0, (0,)), (1, (0,)), (0, (1,)), (1, (1, 2)), (0, (2, 3)), (1, (3,)))
 Y_CHUNKS = ((0, 1), (2,), (3,))
-AT = {"wd_raw3": 4096, "h_bf11": 2304, "h_bf21": 4352, "h_bf22": 6400, "h_s1": 8448, "h_bf32": 9472, "wd_w": 12032}
 
 
 def woven(tile_ap):
@@ -35,11 +36,15 @@ def planes(tile_ap):
     return tile_ap.rearrange("p t (c i) -> p c t i", i=PACK)
 
 
+def columns(quarters):
+    return slice(QUARTER * quarters[0], QUARTER * (quarters[-1] + 1))
+
+
 def tile_list_cube_parser_layer_kernel(tc, x, tab_words, tab_scales, offs, b, g, wdT, w4_words, w4_scales, c, out_0, out_1, out_2):
     nc = tc.nc
     with ExitStack() as ctx:
-        keep = ctx.enter_context(tc.tile_pool(name="keep", bufs=1))
-        reused = ctx.enter_context(tc.tile_pool(name="reused", bufs=1))
+        lists = ctx.enter_context(tc.tile_pool(name="lists", bufs=1))
+        sbuf = ctx.enter_context(tc.tile_pool(name="sbuf", bufs=1))
         psum = ctx.enter_context(tc.psum_pool(name="psum", bufs=1))
 
         def bank(number):
@@ -48,45 +53,60 @@ def tile_list_cube_parser_layer_kernel(tc, x, tab_words, tab_scales, offs, b, g,
         def banks(*numbers):
             return [bank(number) for number in numbers]
 
-        def held(name, shape, dtype):
-            if name in AT:
-                return reused.tile(shape, dtype, name=name, align_bytes=64, offset=AT[name])
-            return keep.tile(shape, dtype, name=name, align_bytes=64)
+        def halves(*numbers):
+            return [whole[:, QUARTER * o : QUARTER * (o + 1)] for whole in map(bank, numbers) for o in range(2)]
 
-        offsets = keep.tile([P, S // 16], U16, name="offsets")
+        placed = {"top": 0}
+
+        def held(name, shape, dtype, over=None):
+            size = WIDTH[dtype]
+            for extent in shape[1:]:
+                size = size * extent
+            if over is None:
+                placed[name] = placed["top"]
+                placed["top"] = placed["top"] + -(-size // 64) * 64
+            else:
+                placed[name] = placed[over[0]] + over[1]
+            return sbuf.tile(shape, dtype, name=name, align_bytes=64, offset=placed[name])
+
+        offsets = lists.tile([P, S // 16], U16, name="offsets")
         nc.sync.dma_start(offsets[:], offs)
 
         b_sb = held("b_sb", [P, 2, PACK], F32)
         g_sb = held("g_sb", [P, 2, PACK], F32)
-        w4_w = held("w4_w", [P, 2, 2 * N], U8)
-
-        tab_s = held("tab_s", [P, T], U8)
-        nc.gpsimd.memset(tab_s[:].bitcast(I32), 0)
-        for q in range(4):
-            nc.gpsimd.dma_start(
-                out=tab_s[32 * q : 32 * q + 8, :].bitcast(I32),
-                in_=tab_scales[:, 4 * q : 4 * q + 4, :].bitcast(I32),
-            )
-        w4_s = held("w4_s", [P, 2, N], U8)
-        nc.gpsimd.memset(w4_s[:].rearrange("p a n -> p (a n)").bitcast(I32), 0)
-        for q in range(4):
-            nc.gpsimd.dma_start(
-                out=w4_s[32 * q : 32 * q + 4, :, :].bitcast(I32),
-                in_=w4_scales[:, 4 * q : 4 * q + 4, :].rearrange("a r n -> r a n").bitcast(I32),
-            )
-        ident = held("ident", [P, P], F32)
-        make_identity(nc, ident[:])
-
         gb_sb = held("gb_sb", [P, 2, PACK], F32)
         c_sb = held("c_sb", [P, PACK], F32)
+        tab_s = held("tab_s", [P, T], U8)
+        w4_s = held("w4_s", [P, 2, N], U8)
+        w4_w = held("w4_w", [P, 2, 2 * N], U8)
+        ident = held("ident", [P, P], F32)
         x_raw, wd_raw, tab_w = {}, {}, {}
 
+        def load_table_scales(queue):
+            nc.gpsimd.memset(tab_s[:].bitcast(I32), 0)
+            for q in range(4):
+                queue.dma_start(
+                    out=tab_s[32 * q : 32 * q + 8, :].bitcast(I32),
+                    in_=tab_scales[:, 4 * q : 4 * q + 4, :].bitcast(I32),
+                )
+
+        def load_bypass_scales(queue):
+            nc.gpsimd.memset(w4_s[:].rearrange("p a n -> p (a n)").bitcast(I32), 0)
+            for r in range(4):
+                queue.dma_start(
+                    out=w4_s[r:P:32, :, :].bitcast(I32),
+                    in_=w4_scales[:, r:16:4, :].rearrange("a q n -> q a n").bitcast(I32),
+                )
+
+        def load_bypass_words():
+            nc.sync.dma_start(out=w4_w[:].bitcast(I32), in_=w4_words.rearrange("a p e -> p a e").bitcast(I32))
+
         def load_x(quarters, a):
-            m0, w = QUARTER * quarters[0], QUARTER * len(quarters)
-            raw = held("x_raw%d%d" % (quarters[0], a), [P, PACK, w], F32)
-            nc.sync.dma_start(out=raw[:], in_=x[PASS * a : PASS * (a + 1), m0 : m0 + w].rearrange("(p i) m -> p i m", i=PACK))
+            cols = columns(quarters)
+            raw = held("x_raw%d%d" % (quarters[0], a), [P, PACK, QUARTER * len(quarters)], F32)
+            nc.sync.dma_start(out=raw[:], in_=x[PASS * a : PASS * (a + 1), cols].rearrange("(p i) m -> p i m", i=PACK))
             for o, q in enumerate(quarters):
-                x_raw[q, a] = raw[:, :, QUARTER * o : QUARTER * (o + 1)]
+                x_raw[q, a] = raw[:, :, columns((o,))]
 
         def load_down(t):
             raw = held("wd_raw%d" % t, [P, T], F32)
@@ -102,250 +122,237 @@ def tile_list_cube_parser_layer_kernel(tc, x, tab_words, tab_scales, offs, b, g,
             nc.sync.dma_start(out=b_sb[:], in_=b.rearrange("(g p t) -> p g t", g=2, t=PACK))
             nc.sync.dma_start(out=g_sb[:], in_=g.rearrange("(g p t) -> p g t", g=2, t=PACK))
 
-        def gains():
-            nc.vector.tensor_tensor(out=gb_sb[:], in0=b_sb[:], in1=g_sb[:], op=ALU.mult)
-
         def load_bias():
             nc.sync.dma_start(out=c_sb[:], in_=c.rearrange("(p t) -> p t", t=PACK))
+
+        def gains():
+            nc.vector.tensor_tensor(out=gb_sb[:], in0=b_sb[:], in1=g_sb[:], op=ALU.mult)
 
         v_s = held("v_s", [P, S], U8)
 
         def gather_scales():
-            listed = held("v_s_listed", [P, S], U8)
-            nc.vector.tensor_copy(out=listed[:], in_=tab_s[:].indirect(offsets[:]))
             nc.vector.tensor_copy(
-                out=v_s[:].rearrange("p (g t q) -> p g t q", g=2, t=PACK),
-                in_=listed[:].rearrange("p (g q t) -> p g t q", g=2, t=PACK),
+                out=v_s[:].rearrange("p (g t q) -> p g q t", g=2, t=PACK), in_=tab_s[:].indirect(offsets[:])
             )
 
         v_w = {}
 
-        def gather_table(a, groups, tag=None):
-            first, count = groups[0], len(groups)
-            words = held(tag or "v_w%d%d" % (a, first), [P, count, PASS], U32)
+        def gather_table(a, jg, over=None):
+            words = held("v_w%d%d" % (a, jg), [P, PASS], U32, over)
             nc.vector.tensor_copy(
-                out=words[:].rearrange("p g (t q) -> p g q t", t=PACK),
-                in_=tab_w[a][:].indirect(offsets[:, 32 * first : 32 * (first + count)]),
+                out=words[:].rearrange("p (t q) -> p q t", t=PACK),
+                in_=tab_w[a][:].indirect(offsets[:, 32 * jg : 32 * (jg + 1)]),
             )
-            for jg in groups:
-                v_w[a, jg] = words[:, jg - first, :]
+            v_w[a, jg] = words
 
         def weave(engine, out, in_):
             if engine is nc.vector:
                 nc.vector.tensor_copy(out=woven(out), in_=planes(in_))
-            else:
+            elif engine is nc.scalar:
                 nc.scalar.activation(out=woven(out), in_=planes(in_), func=ACT.Copy)
+            else:
+                nc.gpsimd.tensor_scalar(
+                    out=out, in0=in_.rearrange("p t m -> p m t"), scalar1=1.0, scalar2=0.0, op0=ALU.mult, op1=ALU.add
+                )
 
-        def columns(quarters):
-            return slice(QUARTER * quarters[0], QUARTER * (quarters[-1] + 1))
+        def weave_shared(engines, out, in_):
+            share = out.shape[1] // len(engines)
+            for o, engine in enumerate(engines):
+                part = slice(share * o, share * (o + 1))
+                weave(engine, out[:, part], in_[:, :, part])
 
         def quantize_into(words, scales, bf):
             nc.vector.quantize_mx(out=words.bitcast(FP8X4), scales=scales, in_=bf.rearrange("p m t -> p (m t)"))
 
-        x_bf = {}
-        x_w = [held("x_w%d" % a, [P, M], U32) for a in range(2)]
-        x_s = [held("x_s%d" % a, [P, M], U8) for a in range(2)]
+        x_bf, x_w, x_s = {}, {}, {}
 
-        def cast_x(q, a, *engines):
-            x_bf[q, a] = held("x_bf%d%d" % (q, a), [P, QUARTER, PACK], BF16)
-            share = QUARTER // len(engines)
-            for o, engine in enumerate(engines):
-                part = slice(share * o, share * (o + 1))
-                weave(engine, x_bf[q, a][:, part], x_raw[q, a][:, :, part])
+        def cast_x(q, a, engines, over=None):
+            x_bf[q, a] = held("x_bf%d%d" % (q, a), [P, QUARTER, PACK], BF16, over)
+            weave_shared(engines, x_bf[q, a][:], x_raw[q, a])
 
-        def quantize_x(q, a):
-            cols = columns((q,))
-            quantize_into(x_w[a][:, cols], x_s[a][:, cols], x_bf[q, a][:])
+        def quantize_x(q, a, over=None):
+            x_w[q, a] = held("x_w%d%d" % (q, a), [P, QUARTER], U32, over)
+            x_s[q, a] = held("x_s%d%d" % (q, a), [P, QUARTER], U8)
+            quantize_into(x_w[q, a][:], x_s[q, a][:], x_bf[q, a][:])
 
-        h_w = [held("h_w%d" % jg, [P, M], U32) for jg in range(2)]
-        h_s = [held("h_s%d" % jg, [P, M], U8) for jg in range(2)]
-        factors, h_bf = {}, {}
+        factors, pre, h_bf, h_planes, h_w, h_s = {}, {}, {}, {}, {}, {}
 
-        def hidden(u, tag, places, part=range(PACK), together=1, apart=False):
+        def first_product(u, slices, number, late=False):
             jg, quarters = UNITS[u]
             w = QUARTER * len(quarters)
-            runs = [(q,) for q in quarters] if apart else [quarters]
-            passes = [(run, a) for run in runs for a in range(2)]
+            whole = bank(number)
+            passes = [(o, t, q, a) for o, t in enumerate(slices) for q in quarters[::-1] for a in ((1, 0) if late else (0, 1))]
+            for o, t, q, a in passes:
+                pre[u, t] = whole[:, w * o : w * (o + 1)]
+                nc.tensor.matmul_mx(
+                    out=pre[u, t][:, columns((q - quarters[0],))],
+                    lhsT=v_w[a, jg][:, P * t : P * (t + 1)].bitcast(FP8X4),
+                    lhsT_scale=v_s[4 * a : P, PASS * jg + P * t : PASS * jg + P * (t + 1)],
+                    rhs=x_w[q, a][:].bitcast(FP8X4),
+                    rhs_scale=x_s[q, a][:],
+                    start=(a == late),
+                    stop=(a != late),
+                )
+
+        def read_factors(u, slices, over=None):
+            jg, quarters = UNITS[u]
             if u not in factors:
-                both = held(tag, [P, 2, PACK, w], F32)
+                both = held("factors%d" % u, [P, 2, PACK, QUARTER * len(quarters)], F32, over)
                 factors[u] = both[:, 0], both[:, 1]
             sq, lin = factors[u]
-            pre = dict(zip(part, places))
-            for first in part[::together]:
-                slices = range(first, first + together)
-                for t in slices:
-                    for o, (run, a) in enumerate(passes):
-                        cols = columns(run)
-                        at = cols.start - QUARTER * quarters[0]
-                        nc.tensor.matmul_mx(
-                            out=pre[t][:, at : at + QUARTER * len(run)],
-                            lhsT=v_w[a, jg][:, P * t : P * (t + 1)].bitcast(FP8X4),
-                            lhsT_scale=v_s[4 * a : P, PASS * jg + P * t : PASS * jg + P * (t + 1)],
-                            rhs=x_w[a][:, cols].bitcast(FP8X4),
-                            rhs_scale=x_s[a][:, cols],
-                            start=(o == 0),
-                            stop=(o == len(passes) - 1),
-                        )
-                for t in slices:
-                    nc.scalar.activation(out=sq[:, t, :], in_=pre[t][:, :w], func=ACT.Square, bias=b_sb[:, jg, t : t + 1])
-                    nc.scalar.activation(
-                        out=lin[:, t, :], in_=pre[t][:, :w], func=ACT.Identity,
-                        bias=gb_sb[:, jg, t : t + 1], scale=g_sb[:, jg, t : t + 1],
-                    )
+            for t in slices:
+                nc.scalar.activation(out=sq[:, t, :], in_=pre[u, t], func=ACT.Square, bias=b_sb[:, jg, t : t + 1])
+                nc.scalar.activation(
+                    out=lin[:, t, :], in_=pre[u, t], func=ACT.Identity,
+                    bias=gb_sb[:, jg, t : t + 1], scale=g_sb[:, jg, t : t + 1],
+                )
 
-        def cube(u, quarters=None, tag=None):
-            quarters = quarters or UNITS[u][1]
+        def hidden(u, numbers, over=None, part=range(PACK), late=False):
+            together = len(part) // len(numbers)
+            for o, number in enumerate(numbers):
+                slices = part[together * o : together * (o + 1)]
+                first_product(u, slices, number, late)
+                read_factors(u, slices, over)
+
+        def cube(u, q, over=None):
             sq, lin = factors[u]
-            cols = columns([q - UNITS[u][1][0] for q in quarters])
-            bf = held(tag or "h_bf%d%d" % (u, quarters[0]), [P, QUARTER * len(quarters), PACK], BF16)
+            cols = columns((q - UNITS[u][1][0],))
+            bf = held("h_bf%d%d" % (u, q), [P, QUARTER, PACK], BF16, over)
             nc.vector.tensor_tensor(out=woven(bf[:]), in0=planes(sq[:, :, cols]), in1=planes(lin[:, :, cols]), op=ALU.mult)
-            h_bf[u, quarters] = bf
+            h_bf[u, q] = bf
 
-        h_planes = {}
-
-        def product(u, quarters, tag):
+        def product(u, q, over=None):
             sq, lin = factors[u]
-            cols = columns([q - UNITS[u][1][0] for q in quarters])
-            flat = held(tag, [P, PACK, QUARTER * len(quarters)], BF16)
+            cols = columns((q - UNITS[u][1][0],))
+            flat = held("h_planes%d%d" % (u, q), [P, PACK, QUARTER], BF16, over)
             nc.gpsimd.tensor_tensor(out=flat[:], in0=sq[:, :, cols], in1=lin[:, :, cols], op=ALU.mult)
-            for o, q in enumerate(quarters):
-                h_planes[u, q] = flat[:, :, QUARTER * o : QUARTER * (o + 1)]
+            h_planes[u, q] = flat
 
-        def weave_h(u, q, engine):
-            h_bf[u, (q,)] = held("h_bf%d%d" % (u, q), [P, QUARTER, PACK], BF16)
-            weave(engine, h_bf[u, (q,)][:], h_planes[u, q])
+        def weave_h(u, q, engines, over=None):
+            h_bf[u, q] = held("h_bf%d%d" % (u, q), [P, QUARTER, PACK], BF16, over)
+            weave_shared(engines, h_bf[u, q][:], h_planes[u, q][:])
 
-        def quantize_h(u, quarters=None):
-            quarters = quarters or UNITS[u][1]
+        def quantize_h(u, q, over=None):
             jg = UNITS[u][0]
-            cols = columns(quarters)
-            quantize_into(h_w[jg][:, cols], h_s[jg][:, cols], h_bf[u, quarters][:])
+            h_w[q, jg] = held("h_w%d%d" % (q, jg), [P, QUARTER], U32, over)
+            h_s[q, jg] = held("h_s%d%d" % (q, jg), [P, QUARTER], U8)
+            quantize_into(h_w[q, jg][:], h_s[q, jg][:], h_bf[u, q][:])
 
         wd_picked = {}
 
-        def gather_down(t, tag=None):
-            picked = held(tag or "picked%d" % t, [P, 2, PASS + GAP], BF16)
+        def gather_down(t, over=None):
+            picked = held("picked%d" % t, [P, 2, PASS + GAP], BF16, over)
             nc.vector.tensor_copy(out=picked[:, :, :PASS], in_=wd_raw[t][:].indirect(offsets[:]))
             wd_picked[t] = picked
 
-        wd_bf = held("wd_bf", [P, PACK, 2, P, PACK], BF16)
-        wd_w = held("wd_w", [P, PACK, 2, P], U32)
-        wd_s = held("wd_s", [P, PACK, 2, P], U8)
+        wd_bf, wd_w, wd_s = {}, {}, {}
+
+        turned = {}
 
         def turn_down(t, number):
             pairs = wd_picked[t][:].bitcast(F32)
-            turned = bank(number)[:].rearrange("p (g u n) -> p g u n", g=2, u=2)
+            turned[t] = bank(number)[:].rearrange("p (g u n) -> p g u n", g=2, u=2)
             for jg in range(2):
                 for u in range(2):
-                    nc.tensor.transpose(turned[:, jg, u, :], pairs[:, jg, u : 2 * P : 2], ident[:])
-            nc.scalar.copy(out=wd_bf[:, t].bitcast(F32), in_=turned.rearrange("p g u n -> p g n u"))
+                    nc.tensor.transpose(turned[t][:, jg, u, :], pairs[:, jg, u : 2 * P : 2], ident[:])
 
-        def quantize_down(first=0, count=PACK):
-            part = slice(first, first + count)
-            quantize_into(
-                wd_w[:, part].rearrange("p t g n -> p (t g n)"),
-                wd_s[:, part].rearrange("p t g n -> p (t g n)"),
-                wd_bf[:, part].rearrange("p t g n i -> p (t g n) i"),
-            )
+        def lift_down(t, over=None):
+            wd_bf[t] = held("wd_bf%d" % t, [P, 2, P, PACK], BF16, over)
+            nc.scalar.copy(out=wd_bf[t][:].bitcast(F32), in_=turned[t].rearrange("p g u n -> p g n u"))
 
-        w4_w_dealt = held("w4_w_dealt", [P, 2, 2 * N], U8)
-        w4_s_dealt = held("w4_s_dealt", [P, 2, N], U8)
+        def quantize_down(t, over=None):
+            wd_w[t] = held("wd_w%d" % t, [P, 2 * P], U32, over)
+            wd_s[t] = held("wd_s%d" % t, [P, 2 * P], U8)
+            quantize_into(wd_w[t][:], wd_s[t][:], wd_bf[t][:].rearrange("p g n i -> p (g n) i"))
 
-        def deal_bypass_words():
+        w4 = {}
+
+        def deal_bypass_words(over=None):
+            w4["words"] = held("w4_w_dealt", [P, 2, 2 * N], U8, over)
             nc.vector.tensor_copy(
-                out=w4_w_dealt[:].bitcast(U16).rearrange("p a (t q) -> p a t q", t=PACK),
+                out=w4["words"][:].bitcast(U16).rearrange("p a (t q) -> p a t q", t=PACK),
                 in_=w4_w[:].bitcast(U16).rearrange("p a (q t) -> p a t q", t=PACK),
             )
 
-        def deal_bypass_scales():
+        def deal_bypass_scales(over=None):
+            w4["scales"] = held("w4_s_dealt", [P, 2, N], U8, over)
             nc.vector.tensor_copy(
-                out=w4_s_dealt[:].rearrange("p a (t q) -> p a t q", t=PACK),
+                out=w4["scales"][:].rearrange("p a (t q) -> p a t q", t=PACK),
                 in_=w4_s[:].rearrange("p a (q t) -> p a t q", t=PACK),
             )
 
         y_s = held("y_s", [P, M], U8)
         y_rows = out_0.rearrange("(p t) m -> p t m", t=PACK)
         y_words = out_1[0].rearrange("p m t -> p (m t)")
-        y_f32, y_bf = {}, {}
+        y_f32, y_bf, sums = {}, {}, {}
 
-        sums = {}
+        def open_sums(ci, slices, number):
+            w = QUARTER * len(Y_CHUNKS[ci])
+            whole = bank(number)
+            for o, t in enumerate(slices):
+                sums[ci, t] = whole[:, w * o : w * (o + 1)]
+                for q in Y_CHUNKS[ci]:
+                    for a in range(2):
+                        nc.tensor.matmul_mx(
+                            out=sums[ci, t][:, columns((q - Y_CHUNKS[ci][0],))],
+                            lhsT=w4["words"][:, a, 2 * P * t : 2 * P * (t + 1)].bitcast(FP4X4),
+                            lhsT_scale=w4["scales"][:, a, P * t : P * (t + 1)],
+                            rhs=x_w[q, a][:].bitcast(FP8X4),
+                            rhs_scale=x_s[q, a][:],
+                            start=(o, q, a) == (0, Y_CHUNKS[ci][0], 0),
+                            stop=False,
+                        )
 
-        def halves(numbers):
-            return [whole[:, QUARTER * o : QUARTER * (o + 1)] for whole in map(bank, numbers) for o in range(2)]
-
-        def bypass(ci, t, acc, first=True):
-            sums[ci, t] = acc
-            m0, w = y_columns(ci)
-            step = 512 if w == 512 else 128
-            for a in range(2):
-                for n0 in range(0, w, step):
-                    nc.tensor.matmul_mx(
-                        out=acc[:, n0 : n0 + step],
-                        lhsT=w4_w_dealt[:, a, 2 * P * t : 2 * P * (t + 1)].bitcast(FP4X4),
-                        lhsT_scale=w4_s_dealt[:, a, P * t : P * (t + 1)],
-                        rhs=x_w[a][:, m0 + n0 : m0 + n0 + step].bitcast(FP8X4),
-                        rhs_scale=x_s[a][:, m0 + n0 : m0 + n0 + step],
-                        start=first,
-                        stop=False,
-                    )
-                    first = False
-
-        def down(ci, t, jg, last):
-            m0, w = y_columns(ci)
-            nc.tensor.matmul_mx(
-                out=sums[ci, t][:, :w],
-                lhsT=wd_w[:, t, jg, :].bitcast(FP8X4),
-                lhsT_scale=wd_s[:, t, jg, :],
-                rhs=h_w[jg][:, m0 : m0 + w].bitcast(FP8X4),
-                rhs_scale=h_s[jg][:, m0 : m0 + w],
-                start=False,
-                stop=last,
-            )
-
-        def y_columns(ci):
-            return QUARTER * Y_CHUNKS[ci][0], QUARTER * len(Y_CHUNKS[ci])
-
-        def empty(ci, t, tag):
-            m0, w = y_columns(ci)
-            if ci not in y_f32:
-                y_f32[ci] = held(tag, [P, PACK, w], F32)
-            y = y_f32[ci]
-            nc.scalar.activation(out=y[:, t, :], in_=sums[ci, t][:, :w], func=ACT.Identity, bias=c_sb[:, t : t + 1])
-            if t % 2 == 1:
-                nc.sync.dma_start(out=y_rows[:, t - 1 : t + 1, m0 : m0 + w], in_=y[:, t - 1 : t + 1, :])
-
-        def cast_y(ci, engines, tag):
-            w = y_columns(ci)[1]
-            share = w // len(engines)
-            bf = held(tag, [P, w, PACK], BF16)
-            for o, engine in enumerate(engines):
-                weave(engine, bf[:, share * o : share * (o + 1)], y_f32[ci][:, :, share * o : share * (o + 1)])
-            y_bf[ci] = bf
-
-        def quantize_y(ci):
-            m0, w = y_columns(ci)
-            words = held("y_w%d" % ci, [P, w], U32)
-            nc.vector.quantize_mx(
-                out=words[:].bitcast(FP8X4), scales=y_s[:, m0 : m0 + w], in_=y_bf[ci][:].rearrange("p m t -> p (m t)")
-            )
-            nc.sync.dma_start(out=y_words[:, 4 * m0 : 4 * (m0 + w)].bitcast(I32), in_=words[:].bitcast(I32))
-
-        def store_scales():
-            for q in range(4):
-                queue = nc.scalar if q < 2 else nc.sync
-                queue.dma_start(
-                    out=out_2[0, 4 * q : 4 * q + 4, :].bitcast(I32),
-                    in_=y_s[32 * q : 32 * q + 4, :].bitcast(I32),
+        def down(ci, t, jg, stop=False):
+            for q in Y_CHUNKS[ci]:
+                nc.tensor.matmul_mx(
+                    out=sums[ci, t][:, columns((q - Y_CHUNKS[ci][0],))],
+                    lhsT=wd_w[t][:, P * jg : P * (jg + 1)].bitcast(FP8X4),
+                    lhsT_scale=wd_s[t][:, P * jg : P * (jg + 1)],
+                    rhs=h_w[q, jg][:].bitcast(FP8X4),
+                    rhs_scale=h_s[q, jg][:],
+                    start=False,
+                    stop=stop and q == Y_CHUNKS[ci][-1],
                 )
 
+        def empty(ci, t, over=None):
+            if ci not in y_f32:
+                y_f32[ci] = held("y_f32_%d" % ci, [P, PACK, QUARTER * len(Y_CHUNKS[ci])], F32, over)
+            nc.scalar.activation(out=y_f32[ci][:, t, :], in_=sums[ci, t], func=ACT.Identity, bias=c_sb[:, t : t + 1])
+
+        def store_y(ci, first, count):
+            part = slice(first, first + count)
+            nc.sync.dma_start(out=y_rows[:, part, columns(Y_CHUNKS[ci])], in_=y_f32[ci][:, part, :])
+
+        def cast_y(ci, engines, over=None):
+            y_bf[ci] = held("y_bf%d" % ci, [P, QUARTER * len(Y_CHUNKS[ci]), PACK], BF16, over)
+            weave_shared(engines, y_bf[ci][:], y_f32[ci][:])
+
+        def quantize_y(ci, over=None):
+            cols = columns(Y_CHUNKS[ci])
+            words = held("y_w%d" % ci, [P, QUARTER * len(Y_CHUNKS[ci])], U32, over)
+            quantize_into(words[:], y_s[:, cols], y_bf[ci][:])
+            nc.sync.dma_start(out=y_words[:, 4 * cols.start : 4 * cols.stop].bitcast(I32), in_=words[:].bitcast(I32))
+
+        def store_scales():
+            for r in range(4):
+                queue = nc.scalar if r < 2 else nc.sync
+                queue.dma_start(out=out_2[0, r:16:4, :].bitcast(I32), in_=y_s[r:P:32, :].bitcast(I32))
+
+        vector, scalar, gpsimd = nc.vector, nc.scalar, nc.gpsimd
+
+        load_bias()
+        load_table_scales(nc.sync)
+        make_identity(nc, ident[:])
         load_table(0)
+        load_table(1)
         load_x((0,), 0)
         load_x((0,), 1)
-        load_table(1)
         load_gains()
+        load_bypass_words()
+        load_bypass_scales(nc.sync)
         load_x((1,), 0)
         load_x((1,), 1)
-        nc.sync.dma_start(out=w4_w[:].bitcast(I32), in_=w4_words.rearrange("a p e -> p a e").bitcast(I32))
         load_x((2,), 0)
         load_x((2,), 1)
         load_x((3,), 0)
@@ -354,90 +361,110 @@ def tile_list_cube_parser_layer_kernel(tc, x, tab_words, tab_scales, offs, b, g,
         load_down(1)
         load_down(2)
         load_down(3)
-        load_bias()
 
-        gather_table(0, (0, 1))
         gather_scales()
-        cast_x(0, 0, nc.scalar)
-        cast_x(0, 1, nc.scalar)
+        gather_table(0, 0)
+        gather_table(0, 1)
+        gather_table(1, 0)
+        gather_table(1, 1)
+        cast_x(0, 0, [scalar])
+        cast_x(0, 1, [vector, scalar])
         quantize_x(0, 0)
-        deal_bypass_scales()
         quantize_x(0, 1)
-        gather_table(1, (0,))
         gains()
-        hidden(0, "factors_a", banks(0, 1, 2, 3))
-        gather_table(1, (1,))
-        cast_x(1, 0, nc.vector)
+        hidden(0, (0, 1), None, range(2))
+        hidden(0, (2, 3), None, range(2, 4), late=True)
+        deal_bypass_words(("x_bf01", 0))
+        deal_bypass_scales(("w4_w", 0))
+        hidden(1, (4, 5), late=True)
+        cast_x(1, 0, [vector])
         quantize_x(1, 0)
-        cast_x(1, 1, nc.vector)
+        cast_x(1, 1, [vector])
         quantize_x(1, 1)
-        deal_bypass_words()
-        cast_x(2, 0, nc.scalar, nc.vector)
-        hidden(1, "factors_b", banks(4, 5, 6, 7), apart=True)
-        cube(0, tag="x_bf11")
-        cast_x(2, 1, nc.vector)
+        hidden(2, (6, 7), late=True)
+        cube(0, 0, ("x_raw11", 0))
+        cast_x(2, 0, [vector], ("x_raw11", 2 * KIB))
+        cast_x(2, 1, [vector], ("factors0", 0))
         quantize_x(2, 0)
         quantize_x(2, 1)
-        cast_x(3, 0, nc.vector)
-        quantize_h(0)
-        cast_x(3, 1, nc.vector)
+        for t in range(2):
+            open_sums(0, (t,), 2 + t)
+        hidden(3, (0, 1), ("tab_w0", 0), range(2), late=True)
+        for t in range(2, PACK):
+            open_sums(0, (t,), 2 + t)
+        hidden(3, (7, 0), None, range(2, 4), late=True)
+        open_sums(1, (0, 1), 6)
+        cast_x(3, 0, [vector], ("x_raw21", 0))
+        cube(1, 0, ("x_raw21", 2 * KIB))
+        cast_x(3, 1, [vector], ("x_raw30", 0))
         quantize_x(3, 0)
         quantize_x(3, 1)
-        hidden(2, "factors_c", banks(0, 1, 2, 3))
+        quantize_h(0, 0, ("x_raw31", 0))
+        quantize_h(1, 0, ("x_raw31", KIB))
+        hidden(4, (1, 7), None, range(2), late=True)
+        gather_down(0, ("x_bf31", 0))
+        product(2, 1, ("h_bf00", 0))
+        gather_down(1)
+        weave_h(2, 1, [gpsimd])
+        gather_down(2)
+        product(3, 1)
+        gather_down(3)
+        product(3, 2)
+        turn_down(0, 0)
+        lift_down(0)
+        hidden(4, (1,), None, range(2, 3))
+        turn_down(1, 7)
+        lift_down(1)
+        hidden(4, (0,), None, range(3, 4))
+        first_product(5, (0, 1), 1)
+        turn_down(2, 7)
+        lift_down(2)
+        read_factors(5, (0, 1), ("factors1", 0))
+        hidden(5, (0,), None, range(2, 4))
+        turn_down(3, 1)
+        lift_down(3)
+        quantize_h(2, 1, ("wd_raw3", 0))
+        weave_h(3, 1, [vector], ("wd_raw3", KIB))
+        quantize_down(2, ("wd_raw3", 3 * KIB))
+        weave_h(3, 2, [vector], ("wd_raw3", 4 * KIB))
+        quantize_h(3, 1)
+        quantize_down(0, ("wd_bf2", 0))
+        quantize_down(1, ("wd_bf2", KIB))
+        for t in (2, 0, 1):
+            down(0, t, 0)
+            down(0, t, 1, stop=True)
+        open_sums(1, (2, 3), 7)
+        cube(4, 2, ("wd_bf0", 0))
+        quantize_down(3)
+        down(0, 3, 0)
+        down(0, 3, 1, stop=True)
+        quantize_h(3, 2)
+        quantize_h(4, 2)
         for t in range(PACK):
-            bypass(0, t, bank(4 + t))
-        product(1, (0, 1), "x_bf31")
-        product(2, (1,), "x_bf30")
+            down(1, t, 1)
+            down(1, t, 0, stop=t % 2 == 1)
+        open_sums(2, (0, 1), 0)
+        open_sums(2, (2, 3), 1)
+        for t in (2, 0, 1, 3):
+            empty(0, t, ("x_raw00", 0))
+            if t % 2 == 1:
+                store_y(0, t - 1, 2)
+        cube(4, 3, ("wd_bf3", 0))
+        cube(5, 3, ("h_bf42", 0))
+        quantize_h(4, 3)
+        quantize_h(5, 3)
         for t in range(PACK):
-            gather_down(t)
-        hidden(3, "factors_d", banks(0, 1), range(0, 2))
-        weave_h(1, 0, nc.scalar)
-        turn_down(0, 2)
-        turn_down(1, 3)
-        hidden(3, "factors_d", banks(0, 1), range(2, 4))
-        turn_down(2, 2)
-        turn_down(3, 3)
-        weave_h(1, 1, nc.vector)
-        weave_h(2, 1, nc.vector)
-        quantize_h(1, (0,))
-        quantize_h(1, (1,))
-        quantize_down(0, 2)
-        quantize_h(2, (1,))
-        cube(2, (2,))
-        quantize_down(2, 2)
-        hidden(4, "factors_a", halves((0, 1)), together=2)
-        for t in range(PACK):
-            down(0, t, 1, False)
-            down(0, t, 0, True)
-        cube(3, (2,))
-        quantize_h(2, (2,))
-        cube(3, (3,), "wd_bf")
-        for t, place in enumerate(halves((2, 3))):
-            bypass(1, t, place, t % 2 == 0)
-        for t in range(PACK):
-            down(1, t, 0, False)
-        for t in range(PACK):
-            empty(0, t, "factors_c")
-        quantize_h(3, (2,))
-        cube(4)
-        quantize_h(3, (3,))
-        for t in range(PACK):
-            down(1, t, 1, t % 2 == 1)
-        for t in range(PACK):
-            empty(1, t, "x_raw11")
-        for t, place in enumerate(halves((4, 5))):
-            bypass(2, t, place, t % 2 == 0)
-        for t in range(PACK):
-            down(2, t, 1, False)
-        quantize_h(4)
-        cast_y(0, [nc.vector], "x_bf31")
-        cast_y(1, [nc.vector], "x_bf00")
-        for t in range(PACK):
-            down(2, t, 0, t % 2 == 1)
-        for t in range(PACK):
-            empty(2, t, "x_raw20")
+            down(2, t, 0)
+            down(2, t, 1, stop=t % 2 == 1)
+        for ci, room in ((1, "x_raw10"), (2, "x_raw20")):
+            for t in range(PACK):
+                empty(ci, t, (room, 0))
+                if t % 2 == 1:
+                    store_y(ci, t - 1, 2)
+        cast_y(0, [vector], ("factors5", 0))
+        cast_y(1, [vector], ("factors5", 4 * KIB))
         quantize_y(0)
-        cast_y(2, [nc.vector, nc.scalar], "x_bf01")
         quantize_y(1)
+        cast_y(2, [vector, scalar])
         quantize_y(2)
         store_scales()

@@ -175,6 +175,22 @@ def tile_list_cube_parser_layer_kernel(tc, x, tab_words, tab_scales, offs, b, g,
             x_s[q, a] = held("x_s%d%d" % (q, a), [P, QUARTER], U8)
             quantize_into(x_w[q, a][:], x_s[q, a][:], x_bf[q, a][:])
 
+        def cast_pair(q, a, over=None):
+            if a == 0:
+                x_bf[q] = held("x_bf%d" % q, [P, 2, QUARTER, PACK], BF16, over)
+            weave(nc.vector, x_bf[q][:, a], x_raw[q, a])
+
+        def quantize_pair(q, over=None):
+            words = held("x_w%d" % q, [P, 2, QUARTER], U32, over)
+            scales = held("x_s%d" % q, [P, 2, QUARTER], U8)
+            quantize_into(
+                words[:].rearrange("p a m -> p (a m)"),
+                scales[:].rearrange("p a m -> p (a m)"),
+                x_bf[q][:].rearrange("p a m t -> p (a m) t"),
+            )
+            for a in range(2):
+                x_w[q, a], x_s[q, a] = words[:, a], scales[:, a]
+
         factors, pre, h_bf, h_planes, h_w, h_s = {}, {}, {}, {}, {}, {}
 
         def first_product(u, slices, number, late=False):
@@ -194,18 +210,35 @@ def tile_list_cube_parser_layer_kernel(tc, x, tab_words, tab_scales, offs, b, g,
                     stop=(a != late),
                 )
 
-        def read_factors(u, slices, over=None):
-            jg, quarters = UNITS[u]
+        def factor_tiles(u, over=None):
             if u not in factors:
-                both = held("factors%d" % u, [P, 2, PACK, QUARTER * len(quarters)], F32, over)
+                both = held("factors%d" % u, [P, 2, PACK, QUARTER * len(UNITS[u][1])], F32, over)
                 factors[u] = both[:, 0], both[:, 1]
-            sq, lin = factors[u]
-            for t in slices:
-                nc.scalar.activation(out=sq[:, t, :], in_=pre[u, t], func=ACT.Square, bias=b_sb[:, jg, t : t + 1])
+            return factors[u]
+
+        def read_square(u, t, over=None):
+            jg = UNITS[u][0]
+            nc.scalar.activation(
+                out=factor_tiles(u, over)[0][:, t, :], in_=pre[u, t], func=ACT.Square, bias=b_sb[:, jg, t : t + 1]
+            )
+
+        def read_gained(u, t, engine):
+            jg = UNITS[u][0]
+            lin = factor_tiles(u)[1][:, t, :]
+            if engine is nc.scalar:
                 nc.scalar.activation(
-                    out=lin[:, t, :], in_=pre[u, t], func=ACT.Identity,
-                    bias=gb_sb[:, jg, t : t + 1], scale=g_sb[:, jg, t : t + 1],
+                    out=lin, in_=pre[u, t], func=ACT.Identity, bias=gb_sb[:, jg, t : t + 1], scale=g_sb[:, jg, t : t + 1]
                 )
+            else:
+                nc.vector.tensor_scalar(
+                    out=lin, in0=pre[u, t], scalar1=b_sb[:, jg, t : t + 1], scalar2=g_sb[:, jg, t : t + 1],
+                    op0=ALU.add, op1=ALU.mult,
+                )
+
+        def read_factors(u, slices, over=None):
+            for t in slices:
+                read_square(u, t, over)
+                read_gained(u, t, nc.scalar)
 
         def hidden(u, numbers, over=None, part=range(PACK), late=False):
             together = len(part) // len(numbers)
@@ -269,14 +302,15 @@ def tile_list_cube_parser_layer_kernel(tc, x, tab_words, tab_scales, offs, b, g,
 
         def deal_bypass_words(over=None):
             w4["words"] = held("w4_w_dealt", [P, 2, 2 * N], U8, over)
-            nc.vector.tensor_copy(
-                out=w4["words"][:].bitcast(U16).rearrange("p a (t q) -> p a t q", t=PACK),
-                in_=w4_w[:].bitcast(U16).rearrange("p a (q t) -> p a t q", t=PACK),
-            )
+            for a in range(2):
+                nc.gpsimd.tensor_copy(
+                    out=w4["words"][:, a].rearrange("p (t q e) -> p t q e", t=PACK, e=2),
+                    in_=w4_w[:, a].rearrange("p (q t e) -> p t q e", t=PACK, e=2),
+                )
 
         def deal_bypass_scales(over=None):
             w4["scales"] = held("w4_s_dealt", [P, 2, N], U8, over)
-            nc.vector.tensor_copy(
+            nc.gpsimd.tensor_copy(
                 out=w4["scales"][:].rearrange("p a (t q) -> p a t q", t=PACK),
                 in_=w4_s[:].rearrange("p a (q t) -> p a t q", t=PACK),
             )
@@ -341,16 +375,14 @@ def tile_list_cube_parser_layer_kernel(tc, x, tab_words, tab_scales, offs, b, g,
 
         vector, scalar, gpsimd = nc.vector, nc.scalar, nc.gpsimd
 
-        load_bias()
+        load_bypass_words()
         load_table_scales(nc.sync)
-        make_identity(nc, ident[:])
         load_table(0)
+        load_bypass_scales(nc.sync)
         load_table(1)
         load_x((0,), 0)
         load_x((0,), 1)
         load_gains()
-        load_bypass_words()
-        load_bypass_scales(nc.sync)
         load_x((1,), 0)
         load_x((1,), 1)
         load_x((2,), 0)
@@ -361,6 +393,10 @@ def tile_list_cube_parser_layer_kernel(tc, x, tab_words, tab_scales, offs, b, g,
         load_down(1)
         load_down(2)
         load_down(3)
+        load_bias()
+        deal_bypass_words()
+        deal_bypass_scales()
+        make_identity(nc, ident[:])
 
         gather_scales()
         gather_table(0, 0)
@@ -374,8 +410,6 @@ def tile_list_cube_parser_layer_kernel(tc, x, tab_words, tab_scales, offs, b, g,
         gains()
         hidden(0, (0, 1), None, range(2))
         hidden(0, (2, 3), None, range(2, 4), late=True)
-        deal_bypass_words(("x_bf01", 0))
-        deal_bypass_scales(("w4_w", 0))
         hidden(1, (4, 5), late=True)
         cast_x(1, 0, [vector])
         quantize_x(1, 0)

@@ -257,13 +257,13 @@ def tile_list_cube_parser_layer_kernel(tc, x, tab_words, tab_scales, offs, b, g,
         def product(u, q, over=None):
             sq, lin = factors[u]
             cols = columns((q - UNITS[u][1][0],))
-            flat = held("h_planes%d%d" % (u, q), [P, PACK, QUARTER], BF16, over)
-            nc.gpsimd.tensor_tensor(out=flat[:], in0=sq[:, :, cols], in1=lin[:, :, cols], op=ALU.mult)
-            h_planes[u, q] = flat
-
-        def weave_h(u, q, engines, over=None):
             h_bf[u, q] = held("h_bf%d%d" % (u, q), [P, QUARTER, PACK], BF16, over)
-            weave_shared(engines, h_bf[u, q][:], h_planes[u, q][:])
+            nc.gpsimd.tensor_tensor(
+                out=h_bf[u, q][:],
+                in0=sq[:, :, cols].rearrange("p t m -> p m t"),
+                in1=lin[:, :, cols].rearrange("p t m -> p m t"),
+                op=ALU.mult,
+            )
 
         def quantize_h(u, q, over=None):
             jg = UNITS[u][0]
@@ -439,7 +439,6 @@ def tile_list_cube_parser_layer_kernel(tc, x, tab_words, tab_scales, offs, b, g,
         gather_down(0, ("x_bf31", 0))
         product(2, 1, ("h_bf00", 0))
         gather_down(1)
-        weave_h(2, 1, [gpsimd])
         gather_down(2)
         product(3, 1)
         gather_down(3)
@@ -458,10 +457,9 @@ def tile_list_cube_parser_layer_kernel(tc, x, tab_words, tab_scales, offs, b, g,
         turn_down(3, 1)
         lift_down(3)
         quantize_h(2, 1, ("wd_raw3", 0))
-        weave_h(3, 1, [vector], ("wd_raw3", KIB))
+        quantize_h(3, 1, ("wd_raw3", KIB))
         quantize_down(2, ("wd_raw3", 3 * KIB))
-        weave_h(3, 2, [vector], ("wd_raw3", 4 * KIB))
-        quantize_h(3, 1)
+        quantize_h(3, 2, ("wd_raw3", 2 * KIB))
         quantize_down(0, ("wd_bf2", 0))
         quantize_down(1, ("wd_bf2", KIB))
         for t in (2, 0, 1):
@@ -472,7 +470,6 @@ def tile_list_cube_parser_layer_kernel(tc, x, tab_words, tab_scales, offs, b, g,
         quantize_down(3)
         down(0, 3, 0)
         down(0, 3, 1, stop=True)
-        quantize_h(3, 2)
         quantize_h(4, 2)
         for t in range(PACK):
             down(1, t, 1)

@@ -258,12 +258,13 @@ def tile_list_cube_parser_layer_kernel(tc, x, tab_words, tab_scales, offs, b, g,
             sq, lin = factors[u]
             cols = columns((q - UNITS[u][1][0],))
             h_bf[u, q] = held("h_bf%d%d" % (u, q), [P, QUARTER, PACK], BF16, over)
-            nc.gpsimd.tensor_tensor(
-                out=h_bf[u, q][:],
-                in0=sq[:, :, cols].rearrange("p t m -> p m t"),
-                in1=lin[:, :, cols].rearrange("p t m -> p m t"),
-                op=ALU.mult,
-            )
+            for pair in (slice(0, 2), slice(2, 4)):
+                nc.gpsimd.tensor_tensor(
+                    out=h_bf[u, q][:, :, pair],
+                    in0=sq[:, pair, cols].rearrange("p t m -> p m t"),
+                    in1=lin[:, pair, cols].rearrange("p t m -> p m t"),
+                    op=ALU.mult,
+                )
 
         def quantize_h(u, q, over=None):
             jg = UNITS[u][0]

from contextlib import ExitStack

import concourse.mybir as mybir
from concourse.masks import make_identity

K, T, S, M, N = 1024, 2048, 1024, 1024, 512
FLOPS = 2 * M * (K * S + S * N + K * N)

F32 = mybir.dt.float32
BF16 = mybir.dt.bfloat16
I32 = mybir.dt.int32
U32 = mybir.dt.uint32
U16 = mybir.dt.uint16
U8 = mybir.dt.uint8
FP8X4 = mybir.dt.float8_e4m3fn_x4
FP4X4 = mybir.dt.float4_e2m1fn_x4
ACT = mybir.ActivationFunctionType
ALU = mybir.AluOpType

P = 128
PACK = 4
PASS = P * PACK
GAP = 32
QUARTER = 256
KIB = 1024
WIDTH = {F32: 4, U32: 4, BF16: 2, U8: 1}
UNITS = ((0, (0,)), (1, (0,)), (0, (1,)), (1, (1, 2)), (0, (2, 3)), (1, (3,)))
Y_CHUNKS = ((0, 1), (2,), (3,))


def woven(tile_ap):
    return tile_ap.rearrange("p (c i) t -> p c t i", i=PACK)


def planes(tile_ap):
    return tile_ap.rearrange("p t (c i) -> p c t i", i=PACK)


def columns(quarters):
    return slice(QUARTER * quarters[0], QUARTER * (quarters[-1] + 1))


def tile_list_cube_parser_layer_kernel(tc, x, tab_words, tab_scales, offs, b, g, wdT, w4_words, w4_scales, c, out_0, out_1, out_2):
    nc = tc.nc
    with ExitStack() as ctx:
        lists = ctx.enter_context(tc.tile_pool(name="lists", bufs=1))
        sbuf = ctx.enter_context(tc.tile_pool(name="sbuf", bufs=1))
        psum = ctx.enter_context(tc.psum_pool(name="psum", bufs=1))

        def bank(number):
            return psum.tile([P, 512], F32, name="bank%d" % number)

        def banks(*numbers):
            return [bank(number) for number in numbers]

        def halves(*numbers):
            return [whole[:, QUARTER * o : QUARTER * (o + 1)] for whole in map(bank, numbers) for o in range(2)]

        placed = {"top": 0}

        def held(name, shape, dtype, over=None):
            size = WIDTH[dtype]
            for extent in shape[1:]:
                size = size * extent
            if over is None:
                placed[name] = placed["top"]
                placed["top"] = placed["top"] + -(-size // 64) * 64
            else:
                placed[name] = placed[over[0]] + over[1]
            return sbuf.tile(shape, dtype, name=name, align_bytes=64, offset=placed[name])

        offsets = lists.tile([P, S // 16], U16, name="offsets")
        nc.sync.dma_start(offsets[:], offs)

        b_sb = held("b_sb", [P, 2, PACK], F32)
        g_sb = held("g_sb", [P, 2, PACK], F32)
        gb_sb = held("gb_sb", [P, 2, PACK], F32)
        c_sb = held("c_sb", [P, PACK], F32)
        tab_s = held("tab_s", [P, T], U8)
        w4_s = held("w4_s", [P, 2, N], U8)
        w4_w = held("w4_w", [P, 2, 2 * N], U8)
        ident = held("ident", [P, P], F32)
        x_raw, wd_raw, tab_w = {}, {}, {}

        def load_table_scales(queue):
            nc.gpsimd.memset(tab_s[:].bitcast(I32), 0)
            for q in range(4):
                queue.dma_start(
                    out=tab_s[32 * q : 32 * q + 8, :].bitcast(I32),
                    in_=tab_scales[:, 4 * q : 4 * q + 4, :].bitcast(I32),
                )

        def load_bypass_scales(queue):
            nc.gpsimd.memset(w4_s[:].rearrange("p a n -> p (a n)").bitcast(I32), 0)
            for r in range(4):
                queue.dma_start(
                    out=w4_s[r:P:32, :, :].bitcast(I32),
                    in_=w4_scales[:, r:16:4, :].rearrange("a q n -> q a n").bitcast(I32),
                )

        def load_bypass_words():
            nc.sync.dma_start(out=w4_w[:].bitcast(I32), in_=w4_words.rearrange("a p e -> p a e").bitcast(I32))

        def load_x(quarters, a):
            cols = columns(quarters)
            raw = held("x_raw%d%d" % (quarters[0], a), [P, PACK, QUARTER * len(quarters)], F32)
            nc.sync.dma_start(out=raw[:], in_=x[PASS * a : PASS * (a + 1), cols].rearrange("(p i) m -> p i m", i=PACK))
            for o, q in enumerate(quarters):
                x_raw[q, a] = raw[:, :, columns((o,))]

        def load_down(t):
            raw = held("wd_raw%d" % t, [P, T], F32)
            nc.sync.dma_start(out=raw[:], in_=wdT.rearrange("(p t) e -> p t e", t=PACK)[:, t, :])
            wd_raw[t] = raw

        def load_table(a):
            words = held("tab_w%d" % a, [P, T], U32)
            nc.sync.dma_start(out=words[:].bitcast(I32), in_=tab_words[a].rearrange("p e i -> p (e i)").bitcast(I32))
            tab_w[a] = words

        def load_gains():
            nc.sync.dma_start(out=b_sb[:], in_=b.rearrange("(g p t) -> p g t", g=2, t=PACK))
            nc.sync.dma_start(out=g_sb[:], in_=g.rearrange("(g p t) -> p g t", g=2, t=PACK))

        def load_bias():
            nc.sync.dma_start(out=c_sb[:], in_=c.rearrange("(p t) -> p t", t=PACK))

        def gains():
            nc.vector.tensor_tensor(out=gb_sb[:], in0=b_sb[:], in1=g_sb[:], op=ALU.mult)

        v_s = held("v_s", [P, S], U8)

        def gather_scales():
            nc.vector.tensor_copy(
                out=v_s[:].rearrange("p (g t q) -> p g q t", g=2, t=PACK), in_=tab_s[:].indirect(offsets[:])
            )

        v_w = {}

        def gather_table(a, jg, over=None):
            words = held("v_w%d%d" % (a, jg), [P, PASS], U32, over)
            nc.vector.tensor_copy(
                out=words[:].rearrange("p (t q) -> p q t", t=PACK),
                in_=tab_w[a][:].indirect(offsets[:, 32 * jg : 32 * (jg + 1)]),
            )
            v_w[a, jg] = words

        def weave(engine, out, in_):
            if engine is nc.vector:
                nc.vector.tensor_copy(out=woven(out), in_=planes(in_))
            elif engine is nc.scalar:
                nc.scalar.activation(out=woven(out), in_=planes(in_), func=ACT.Copy)
            else:
                nc.gpsimd.tensor_scalar(
                    out=out, in0=in_.rearrange("p t m -> p m t"), scalar1=1.0, scalar2=0.0, op0=ALU.mult, op1=ALU.add
                )

        def weave_shared(engines, out, in_):
            share = out.shape[1] // len(engines)
            for o, engine in enumerate(engines):
                part = slice(share * o, share * (o + 1))
                weave(engine, out[:, part], in_[:, :, part])

        def quantize_into(words, scales, bf):
            nc.vector.quantize_mx(out=words.bitcast(FP8X4), scales=scales, in_=bf.rearrange("p m t -> p (m t)"))

        x_bf, x_w, x_s = {}, {}, {}

        def cast_x(q, a, engines, over=None):
            x_bf[q, a] = held("x_bf%d%d" % (q, a), [P, QUARTER, PACK], BF16, over)
            weave_shared(engines, x_bf[q, a][:], x_raw[q, a])

        def quantize_x(q, a, over=None):
            x_w[q, a] = held("x_w%d%d" % (q, a), [P, QUARTER], U32, over)
            x_s[q, a] = held("x_s%d%d" % (q, a), [P, QUARTER], U8)
            quantize_into(x_w[q, a][:], x_s[q, a][:], x_bf[q, a][:])

        def cast_pair(q, a, over=None):
            if a == 0:
                x_bf[q] = held("x_bf%d" % q, [P, 2, QUARTER, PACK], BF16, over)
            weave(nc.vector, x_bf[q][:, a], x_raw[q, a])

        def quantize_pair(q, over=None):
            words = held("x_w%d" % q, [P, 2, QUARTER], U32, over)
            scales = held("x_s%d" % q, [P, 2, QUARTER], U8)
            quantize_into(
                words[:].rearrange("p a m -> p (a m)"),
                scales[:].rearrange("p a m -> p (a m)"),
                x_bf[q][:].rearrange("p a m t -> p (a m) t"),
            )
            for a in range(2):
                x_w[q, a], x_s[q, a] = words[:, a], scales[:, a]

        factors, pre, h_bf, h_planes, h_w, h_s = {}, {}, {}, {}, {}, {}

        def first_product(u, slices, number, late=False):
            jg, quarters = UNITS[u]
            w = QUARTER * len(quarters)
            whole = bank(number)
            passes = [(o, t, q, a) for o, t in enumerate(slices) for q in quarters[::-1] for a in ((1, 0) if late else (0, 1))]
            for o, t, q, a in passes:
                pre[u, t] = whole[:, w * o : w * (o + 1)]
                nc.tensor.matmul_mx(
                    out=pre[u, t][:, columns((q - quarters[0],))],
                    lhsT=v_w[a, jg][:, P * t : P * (t + 1)].bitcast(FP8X4),
                    lhsT_scale=v_s[4 * a : P, PASS * jg + P * t : PASS * jg + P * (t + 1)],
                    rhs=x_w[q, a][:].bitcast(FP8X4),
                    rhs_scale=x_s[q, a][:],
                    start=(a == late),
                    stop=(a != late),
                )

        def factor_tiles(u, over=None):
            if u not in factors:
                both = held("factors%d" % u, [P, 2, PACK, QUARTER * len(UNITS[u][1])], F32, over)
                factors[u] = both[:, 0], both[:, 1]
            return factors[u]

        def read_square(u, t, over=None):
            jg = UNITS[u][0]
            nc.scalar.activation(
                out=factor_tiles(u, over)[0][:, t, :], in_=pre[u, t], func=ACT.Square, bias=b_sb[:, jg, t : t + 1]
            )

        def read_gained(u, t, engine):
            jg = UNITS[u][0]
            lin = factor_tiles(u)[1][:, t, :]
            if engine is nc.scalar:
                nc.scalar.activation(
                    out=lin, in_=pre[u, t], func=ACT.Identity, bias=gb_sb[:, jg, t : t + 1], scale=g_sb[:, jg, t : t + 1]
                )
            else:
                nc.vector.tensor_scalar(
                    out=lin, in0=pre[u, t], scalar1=b_sb[:, jg, t : t + 1], scalar2=g_sb[:, jg, t : t + 1],
                    op0=ALU.add, op1=ALU.mult,
                )

        def read_factors(u, slices, over=None):
            for t in slices:
                read_square(u, t, over)
                read_gained(u, t, nc.scalar)

        def hidden(u, numbers, over=None, part=range(PACK), late=False):
            together = len(part) // len(numbers)
            for o, number in enumerate(numbers):
                slices = part[together * o : together * (o + 1)]
                first_product(u, slices, number, late)
                read_factors(u, slices, over)

        def cube(u, q, over=None):
            sq, lin = factors[u]
            cols = columns((q - UNITS[u][1][0],))
            bf = held("h_bf%d%d" % (u, q), [P, QUARTER, PACK], BF16, over)
            nc.vector.tensor_tensor(out=woven(bf[:]), in0=planes(sq[:, :, cols]), in1=planes(lin[:, :, cols]), op=ALU.mult)
            h_bf[u, q] = bf

        def product(u, q, over=None):
            sq, lin = factors[u]
            cols = columns((q - UNITS[u][1][0],))
            h_bf[u, q] = held("h_bf%d%d" % (u, q), [P, QUARTER, PACK], BF16, over)
            for pair in (slice(0, 2), slice(2, 4)):
                nc.gpsimd.tensor_tensor(
                    out=h_bf[u, q][:, :, pair],
                    in0=sq[:, pair, cols].rearrange("p t m -> p m t"),
                    in1=lin[:, pair, cols].rearrange("p t m -> p m t"),
                    op=ALU.mult,
                )

        def quantize_h(u, q, over=None):
            jg = UNITS[u][0]
            h_w[q, jg] = held("h_w%d%d" % (q, jg), [P, QUARTER], U32, over)
            h_s[q, jg] = held("h_s%d%d" % (q, jg), [P, QUARTER], U8)
            quantize_into(h_w[q, jg][:], h_s[q, jg][:], h_bf[u, q][:])

        wd_picked = {}

        def gather_down(t, over=None):
            picked = held("picked%d" % t, [P, 2, PASS + GAP], BF16, over)
            nc.vector.tensor_copy(out=picked[:, :, :PASS], in_=wd_raw[t][:].indirect(offsets[:]))
            wd_picked[t] = picked

        wd_bf, wd_w, wd_s = {}, {}, {}

        turned = {}

        def turn_down(t, number):
            pairs = wd_picked[t][:].bitcast(F32)
            turned[t] = bank(number)[:].rearrange("p (g u n) -> p g u n", g=2, u=2)
            for jg in range(2):
                for u in range(2):
                    nc.tensor.transpose(turned[t][:, jg, u, :], pairs[:, jg, u : 2 * P : 2], ident[:])

        def lift_down(t, over=None):
            wd_bf[t] = held("wd_bf%d" % t, [P, 2, P, PACK], BF16, over)
            nc.scalar.copy(out=wd_bf[t][:].bitcast(F32), in_=turned[t].rearrange("p g u n -> p g n u"))

        def quantize_down(t, over=None):
            wd_w[t] = held("wd_w%d" % t, [P, 2 * P], U32, over)
            wd_s[t] = held("wd_s%d" % t, [P, 2 * P], U8)
            quantize_into(wd_w[t][:], wd_s[t][:], wd_bf[t][:].rearrange("p g n i -> p (g n) i"))

        w4 = {}

        def deal_bypass_words(over=None):
            w4["words"] = held("w4_w_dealt", [P, 2, 2 * N], U8, over)
            for a in range(2):
                nc.gpsimd.tensor_copy(
                    out=w4["words"][:, a].rearrange("p (t q e) -> p t q e", t=PACK, e=2),
                    in_=w4_w[:, a].rearrange("p (q t e) -> p t q e", t=PACK, e=2),
                )

        def deal_bypass_scales(over=None):
            w4["scales"] = held("w4_s_dealt", [P, 2, N], U8, over)
            nc.gpsimd.tensor_copy(
                out=w4["scales"][:].rearrange("p a (t q) -> p a t q", t=PACK),
                in_=w4_s[:].rearrange("p a (q t) -> p a t q", t=PACK),
            )

        y_s = held("y_s", [P, M], U8)
        y_rows = out_0.rearrange("(p t) m -> p t m", t=PACK)
        y_words = out_1[0].rearrange("p m t -> p (m t)")
        y_f32, y_bf, sums = {}, {}, {}

        def open_sums(ci, slices, number):
            w = QUARTER * len(Y_CHUNKS[ci])
            whole = bank(number)
            for o, t in enumerate(slices):
                sums[ci, t] = whole[:, w * o : w * (o + 1)]
                for q in Y_CHUNKS[ci]:
                    for a in range(2):
                        nc.tensor.matmul_mx(
                            out=sums[ci, t][:, columns((q - Y_CHUNKS[ci][0],))],
                            lhsT=w4["words"][:, a, 2 * P * t : 2 * P * (t + 1)].bitcast(FP4X4),
                            lhsT_scale=w4["scales"][:, a, P * t : P * (t + 1)],
                            rhs=x_w[q, a][:].bitcast(FP8X4),
                            rhs_scale=x_s[q, a][:],
                            start=(o, q, a) == (0, Y_CHUNKS[ci][0], 0),
                            stop=False,
                        )

        def down(ci, t, jg, stop=False):
            for q in Y_CHUNKS[ci]:
                nc.tensor.matmul_mx(
                    out=sums[ci, t][:, columns((q - Y_CHUNKS[ci][0],))],
                    lhsT=wd_w[t][:, P * jg : P * (jg + 1)].bitcast(FP8X4),
                    lhsT_scale=wd_s[t][:, P * jg : P * (jg + 1)],
                    rhs=h_w[q, jg][:].bitcast(FP8X4),
                    rhs_scale=h_s[q, jg][:],
                    start=False,
                    stop=stop and q == Y_CHUNKS[ci][-1],
                )

        def empty(ci, t, over=None):
            if ci not in y_f32:
                y_f32[ci] = held("y_f32_%d" % ci, [P, PACK, QUARTER * len(Y_CHUNKS[ci])], F32, over)
            nc.scalar.activation(out=y_f32[ci][:, t, :], in_=sums[ci, t], func=ACT.Identity, bias=c_sb[:, t : t + 1])

        def store_y(ci, first, count):
            part = slice(first, first + count)
            nc.sync.dma_start(out=y_rows[:, part, columns(Y_CHUNKS[ci])], in_=y_f32[ci][:, part, :])

        def cast_y(ci, engines, over=None):
            y_bf[ci] = held("y_bf%d" % ci, [P, QUARTER * len(Y_CHUNKS[ci]), PACK], BF16, over)
            weave_shared(engines, y_bf[ci][:], y_f32[ci][:])

        def quantize_y(ci, over=None):
            cols = columns(Y_CHUNKS[ci])
            words = held("y_w%d" % ci, [P, QUARTER * len(Y_CHUNKS[ci])], U32, over)
            quantize_into(words[:], y_s[:, cols], y_bf[ci][:])
            nc.sync.dma_start(out=y_words[:, 4 * cols.start : 4 * cols.stop].bitcast(I32), in_=words[:].bitcast(I32))

        def store_scales():
            for r in range(4):
                queue = nc.scalar if r < 2 else nc.sync
                queue.dma_start(out=out_2[0, r:16:4, :].bitcast(I32), in_=y_s[r:P:32, :].bitcast(I32))

        vector, scalar, gpsimd = nc.vector, nc.scalar, nc.gpsimd

        load_bypass_words()
        load_table_scales(nc.sync)
        load_table(0)
        load_bypass_scales(nc.sync)
        load_table(1)
        load_x((0,), 0)
        load_x((0,), 1)
        load_gains()
        load_x((1,), 0)
        load_x((1,), 1)
        load_x((2,), 0)
        load_x((2,), 1)
        load_x((3,), 0)
        load_x((3,), 1)
        load_down(0)
        load_down(1)
        load_down(2)
        load_down(3)
        load_bias()
        deal_bypass_words()
        deal_bypass_scales()
        make_identity(nc, ident[:])

        gather_scales()
        gather_table(0, 0)
        gather_table(0, 1)
        gather_table(1, 0)
        gather_table(1, 1)
        cast_x(0, 0, [scalar])
        cast_x(0, 1, [vector, scalar])
        quantize_x(0, 0)
        quantize_x(0, 1)
        gains()
        hidden(0, (0, 1), None, range(2))
        hidden(0, (2, 3), None, range(2, 4), late=True)
        hidden(1, (4, 5), late=True)
        cast_x(1, 0, [vector])
        quantize_x(1, 0)
        cast_x(1, 1, [vector])
        quantize_x(1, 1)
        hidden(2, (6, 7), late=True)
        cube(0, 0, ("x_raw11", 0))
        cast_x(2, 0, [vector], ("x_raw11", 2 * KIB))
        cast_x(2, 1, [vector], ("factors0", 0))
        quantize_x(2, 0)
        quantize_x(2, 1)
        for t in range(2):
            open_sums(0, (t,), 2 + t)
        hidden(3, (0, 1), ("tab_w0", 0), range(2), late=True)
        for t in range(2, PACK):
            open_sums(0, (t,), 2 + t)
        hidden(3, (7, 0), None, range(2, 4), late=True)
        open_sums(1, (0, 1), 6)
        cast_x(3, 0, [vector], ("x_raw21", 0))
        cube(1, 0, ("x_raw21", 2 * KIB))
        cast_x(3, 1, [vector], ("x_raw30", 0))
        quantize_x(3, 0)
        quantize_x(3, 1)
        quantize_h(0, 0, ("x_raw31", 0))
        quantize_h(1, 0, ("x_raw31", KIB))
        hidden(4, (1, 7), None, range(2), late=True)
        gather_down(0, ("x_bf31", 0))
        product(2, 1, ("h_bf00", 0))
        gather_down(1)
        gather_down(2)
        product(3, 1)
        gather_down(3)
        product(3, 2)
        turn_down(0, 0)
        lift_down(0)
        hidden(4, (1,), None, range(2, 3))
        turn_down(1, 7)
        lift_down(1)
        hidden(4, (0,), None, range(3, 4))
        first_product(5, (0, 1), 1)
        turn_down(2, 7)
        lift_down(2)
        read_factors(5, (0, 1), ("factors1", 0))
        hidden(5, (0,), None, range(2, 4))
        turn_down(3, 1)
        lift_down(3)
        quantize_h(2, 1, ("wd_raw3", 0))
        quantize_h(3, 1, ("wd_raw3", KIB))
        quantize_down(2, ("wd_raw3", 3 * KIB))
        quantize_h(3, 2, ("wd_raw3", 2 * KIB))
        quantize_down(0, ("wd_bf2", 0))
        quantize_down(1, ("wd_bf2", KIB))
        for t in (2, 0, 1):
            down(0, t, 0)
            down(0, t, 1, stop=True)
        open_sums(1, (2, 3), 7)
        cube(4, 2, ("wd_bf0", 0))
        quantize_down(3)
        down(0, 3, 0)
        down(0, 3, 1, stop=True)
        quantize_h(4, 2)
        for t in range(PACK):
            down(1, t, 1)
            down(1, t, 0, stop=t % 2 == 1)
        open_sums(2, (0, 1), 0)
        open_sums(2, (2, 3), 1)
        for t in (2, 0, 1, 3):
            empty(0, t, ("x_raw00", 0))
            if t % 2 == 1:
                store_y(0, t - 1, 2)
        cube(4, 3, ("wd_bf3", 0))
        cube(5, 3, ("h_bf42", 0))
        quantize_h(4, 3)
        quantize_h(5, 3)
        for t in range(PACK):
            down(2, t, 0)
            down(2, t, 1, stop=t % 2 == 1)
        for ci, room in ((1, "x_raw10"), (2, "x_raw20")):
            for t in range(PACK):
                empty(ci, t, (room, 0))
                if t % 2 == 1:
                    store_y(ci, t - 1, 2)
        cast_y(0, [vector], ("factors5", 0))
        cast_y(1, [vector], ("factors5", 4 * KIB))
        quantize_y(0)
        quantize_y(1)
        cast_y(2, [vector, scalar])
        quantize_y(2)
        store_scales()
